import numpy as np, ml_dtypes
CORES = [66,74,82,90,194,202,210,218]
N = 8
import mx_ref
BF = ml_dtypes.bfloat16
def cols(t, e):
    v = np.concatenate([t.reshape(128, -1, 4), np.zeros((128, 1, 4), BF)], axis=1)
    return np.ascontiguousarray(v[:, e]).reshape(128, -1)
def pick(q, e):
    c = np.concatenate([q[0].reshape(128, -1, 4), np.zeros((128, 1, 4), np.uint8)], axis=1); s = np.concatenate([q[1], np.ones((16, 1), np.uint8)], axis=1)
    return (np.ascontiguousarray(c[:, e].reshape(128, -1)), np.ascontiguousarray(s[:, e]))
def join(*qs):
    return (np.concatenate([q[0] for q in qs], axis=1), np.concatenate([q[1] for q in qs], axis=1))
def put(q, e, v):
    c, s = q[0].reshape(128, -1, 4).copy(), q[1].copy(); c[:, e] = v[0].reshape(128, -1, 4); s[:, e] = v[1]
    return (c.reshape(128, -1), s)
def pk(c, s):
    return (np.ascontiguousarray(c), mx_ref.live(s))
def emit(q):
    return q[0], q[1]
def decode(q):
    o = []
    for b in range(4):
        e = np.zeros((128, 128, 4), np.float32); e[np.arange(128), np.arange(128), b] = 1
        o.append(mx_ref.matmul(mx_ref.quantize(e.reshape(128, 512).astype(BF)), q))
    return np.stack(o, axis=2).reshape(128, -1)
def f(rng, *shape):
    return mx_ref.flush((rng.standard_normal(shape, dtype=np.float32) * np.exp2(rng.integers(-2, 3, shape[:-1] + (1,)))).astype(BF))
def wide(rng, *shape, cols=0):
    v = rng.standard_normal(shape, dtype=np.float32) * np.exp2(rng.integers(-12, 13, shape)).astype(np.float32)
    if cols: v *= np.repeat(np.exp2(rng.integers(-cols, cols + 1, shape[:-2] + (1, shape[-1] // 4))) * (rng.random(shape[:-2] + (1, shape[-1] // 4)) > 0.0625), 4, axis=-1).astype(np.float32)
    return mx_ref.flush(v.astype(BF))
T, L, PL, R = 192, 32, 5, 3
def sized(v, k):
    v = v.astype(np.float32) * np.float32(k)
    v[np.abs(v) < np.float32(2.0 ** -6)] = 0
    return v.astype(BF)
def column(w, k, v):
    w[:, :, 4 * k:4 * k + 4] = np.asarray(v, np.float32).astype(BF)
def plain(rng):
    return {"x": sized(f(rng, N, 128, 4 * T), 16), "w": np.repeat(f(rng, 1, 128, 512), N, axis=0), "z": f(rng, N, 128, 512)}
def setup_inputs(rng):
    return plain(rng)
def setup_inputs_steps(rng):
    d = plain(rng)
    d["w"][:, 96:] = 0
    for t in range(R):
        v = np.zeros((128, 4))
        v[0, 0], v[64, 0] = 1.0, 2.0 ** -21
        column(d["w"], 8 * t + 6, v)
        for i in range(PL): d["w"][:, 64, 4 * (8 * t + i)] = 0
    x = d["x"].reshape(N, 128, T, 4).astype(np.float32)
    x[:, :96] = np.tile(x[:, :96, :T // 4], (1, 1, 4, 1))
    x[:, 64, :, 0] = np.repeat([5.0, 6.0, 7.0, 7.0], T // 4)
    x[:, 0, :, 0] = np.where(np.arange(N) % 2 == 0, 4.0, -4.0)[:, None]
    d["x"] = x.reshape(N, 128, 4 * T).astype(BF)
    return d
def setup_inputs_far(rng):
    d = plain(rng)
    g = 1 - 2 * rng.integers(0, 2, (N, T))
    g[::2] = 1
    v = (1.5 + 0.5 * rng.random((N, 128, 4 * T), dtype=np.float32)) * np.float32(2.0 ** 27)
    d["x"] = (v * np.repeat(g, 4, axis=1)[:, None, :].astype(np.float32)).astype(BF)
    for t in range(R):
        for i in range(PL):
            column(d["w"], 8 * t + i, np.repeat([-1.0, 1.0], 256)[rng.permutation(512)].reshape(128, 4))
        column(d["w"], 8 * t + 6, -(2.0 ** 30) * rng.choice([0.875, 1.0], (128, 4)))
    return d
def setup_inputs_cancel(rng):
    d = plain(rng)
    d["w"][:, 64:] = 0
    d["x"][:, :64, :4] = d["x"][0, :64, :4].astype(np.float32).astype(BF)
    v = rng.integers(4, 8, (64, 4)) * 2.0 ** 22 * rng.choice([-1.0, 1.0], (64, 4))
    k = [1.0, 2.0 ** -26, -1.0, 2.0 ** -26]
    for r in range(N):
        d["x"][r, 64:] = np.tile(v * k[r % 4], (1, T)).astype(np.float32).astype(BF)
    return d
def setup_inputs_bare(rng):
    d = plain(rng)
    a, b = [int(i) for i in rng.permutation(N)[:2]]
    d["x"][:, 127, ::4] = 0
    one = d["x"][a, :, :4].astype(np.float32)
    k = np.repeat(np.exp2(rng.integers(0, 4, T)), 4).astype(np.float32)
    d["x"][a] = (np.tile(one, (1, T)) * k).astype(BF)
    e = np.where(rng.permutation(T) % 4 > 0, -1, np.arange(T))
    d["x"][b] = cols(d["x"][b], e)
    d["x"][b, 127, 4 * np.flatnonzero(e >= 0)] = 65536.0
    for i in range(PL): d["w"][:, 127, 4 * i] = 1.0
    d["w"][:, 127, 4 * 6] = -1.0
    for i in range(PL): column(d["w"], 8 + i, 0)
    column(d["w"], 8 * (R - 1) + 6, 0)
    return d
def setup_inputs_spread(rng):
    return {**plain(rng), "x": sized(wide(rng, N, 128, 4 * T, cols=6), 64)}
def check_inputs(d):
    b = []
    for k, low, high in (("x", 2.0 ** -6, 2.0 ** 28), ("w", 2.0 ** -30, 2.0 ** 30), ("z", 2.0 ** -30, 2.0 ** 30)):
        v = np.abs(d[k].astype(np.float32))
        if not (np.isfinite(v).all() and ((v == 0) | (v >= low) & (v <= high)).all()): b.append("a value of " + k)
    w = d["w"].astype(np.float32)
    if (w != w[:1]).any(): b.append("w differs from rank to rank")
    return b
def reference(x, w, z):
    y, lv = np.zeros((N, 128, T), np.float32), np.zeros((N, R, T), np.float32)
    oc, osc = np.zeros((N, 128, 4 * T), np.uint8), np.zeros((N, 16, T), np.uint8)
    state = [mx_ref.quantize(np.ascontiguousarray(x[r])) for r in range(N)]
    wq = [mx_ref.quantize(np.ascontiguousarray(w[r])) for r in range(N)]
    for t in range(R):
        leaf, have = np.zeros((N, T), int), []
        total = np.zeros((128, L, 4), np.float32)
        for r in range(N):
            p = mx_ref.matmul(wq[r], state[r])[8 * t:8 * t + 7] + np.float32(0)
            have.append(decode(state[r]).reshape(128, T, 4))
            for i in range(PL): leaf[r] += (p[i] < 0) * (1 << i)
            for l in range(L):
                m = np.flatnonzero(leaf[r] == l)
                if m.size: total[:, l] = total[:, l] + have[r][:, m[np.argmax(p[6, m])]]
        v = mx_ref.quantize(np.ascontiguousarray((total * np.float32(0.125)).reshape(128, 4 * L).astype(BF)))
        v = decode(v).reshape(128, L, 4)
        for r in range(N):
            new = have[r] - v[:, leaf[r]] * np.float32(0.5)
            state[r] = mx_ref.quantize(np.ascontiguousarray(new.reshape(128, 4 * T).astype(BF)))
            lv[r, t] = leaf[r]
    for r in range(N):
        y[r] = mx_ref.matmul(mx_ref.quantize(np.ascontiguousarray(z[r])), state[r])
        oc[r], osc[r] = emit(state[r])
    return {"y": y, "oc": oc, "osc": osc, "lv": lv}

@@ -1,0 +1,362 @@
+from concourse.bass import DstId, RemoteDMATransfer
+from concourse.mybir import dt, AluOpType, ActivationFunctionType
+
+NC, L, R, PL = 192, 32, 3, 5
+W = NC + 2
+P, FLOOR, NONE, DEEP = 2.0 ** 76, -2.0 ** 74, -2.0 ** 72, -2.0 ** 80
+X4, BF, F32, U8, I32, U16 = "float8_e4m3fn_x4", "bfloat16", "float32", "uint8", "int32", "uint16"
+
+SCRATCH = {
+    "wb": ("sbuf", [128, 576], BF), "zt": ("sbuf", [128, 512], BF),
+    "qwb": ("sbuf", [128, 144], X4), "swb": ("sbuf", [128, 144], U8),
+    "qz": ("sbuf", [128, 128], X4), "sz": ("sbuf", [128, 128], U8),
+    "gone": ("sbuf", [128, 520], BF), "g1": ("sbuf", [128, 520], BF), "g8": ("sbuf", [128, 520], BF),
+    "gm": ("sbuf", [128, 520], BF),
+    "qe": ("sbuf", [128, 12 * 128], X4), "se": ("sbuf", [128, 12 * 128], U8),
+    "u": ("sbuf", [128, 128], BF), "ut": ("sbuf", [128, 128], BF), "gk": ("sbuf", [128, 512], BF),
+    "qc": ("sbuf", [128, 3 * 128], X4), "sc": ("sbuf", [128, 3 * 128], U8),
+    "bq": ("sbuf", [128, 4 * W], BF), "qb": ("sbuf", [128, W], X4), "sb": ("sbuf", [128, W], U8),
+    "m8": ("sbuf", [128, 256], BF), "m16": ("sbuf", [128, NC], BF),
+    "idg": ("sbuf", [128, NC], I32), "idh": ("sbuf", [128, NC], I32), "dg": ("sbuf", [128, NC], BF),
+    "neg": ("sbuf", [128, W], BF),
+    "ip": ("sbuf", [128, 8], I32), "jb": ("sbuf", [128, 16], I32), "ja": ("sbuf", [128, 8], I32),
+    "ik": ("sbuf", [128, 8], I32), "jc": ("sbuf", [128, 8], I32), "jd": ("sbuf", [128, 8], I32),
+    "je": ("sbuf", [128, 8], I32), "jf": ("sbuf", [128, 8], I32), "om": ("sbuf", [128, 8], U16),
+    "rm0": ("sbuf", [128, W], F32), "rm1": ("sbuf", [128, W], F32),
+    "sg0": ("sbuf", [128, NC], BF), "sg1": ("sbuf", [128, NC], BF), "ix": ("sbuf", [128, 4], F32),
+    "lt": ("sbuf", [128, NC], BF), "ld": ("sbuf", [128, NC], BF), "ls": ("sbuf", [128, NC], F32),
+    "lvs": ("sbuf", [128, R * NC], F32),
+    "va": ("sbuf", [128, 1024], BF), "vs": ("sbuf", [128, 1024], BF), "ysb": ("sbuf", [128, NC], F32),
+    "pv": ("psum", [128, 2048], F32), "px": ("psum", [128, 2048], F32),
+}
+for _t in range(R + 1):
+    SCRATCH["h%d" % _t] = ("sbuf", [128, 4 * W], BF)
+    SCRATCH["qx%d" % _t] = ("sbuf", [128, W], X4)
+    SCRATCH["sx%d" % _t] = ("sbuf", [128, W], U8)
+for _t in range(R):
+    for _n, _w in (("ws", 128), ("la", 128), ("lb", 128), ("qa", 128), ("qm", 128), ("qv", 256), ("vv", NC)):
+        SCRATCH["%s%d" % (_n, _t)] = ("sbuf", [128, _w], X4)
+        SCRATCH["%ss%d" % (_n, _t)] = ("sbuf", [128, _w], U8)
+    SCRATCH["wl%d" % _t] = ("sbuf", [128, 8], U16)
+    SCRATCH["of%d" % _t] = ("sbuf", [128, 2], U16)
+    SCRATCH["ov%d" % _t] = ("sbuf", [128, 12], U16)
+
+SEMAPHORES = ["cv", "cs", "ct", "cg", "dx", "dw", "dz", "dlv", "dout", "sent"]
+SEMAPHORES += ["%s%d" % (_n, _t) for _n in ("planec", "planes", "matec", "mates") for _t in range(R)]
+
+COUNTER = {"v": "cv", "s": "cs", "t": "ct", "g": "cg"}
+
+
+def _scheduler(g, T):
+    queue = {"v": g.vector, "s": g.scalar, "t": g.tensor, "g": g, "y": g.sync}
+    count = {"cv": 0, "cs": 0, "ct": 0, "cg": 0}
+    clock = {q: {} for q in queue}
+    known = {}
+    writer, readers = {}, {}
+
+    def wait(q, token):
+        name, value = token
+        if clock[q].get(name, 0) >= value:
+            return
+        queue[q].wait_ge(T.sem[name], value)
+        for n, v in list(known.get(token, {}).items()) + [token]:
+            clock[q][n] = max(clock[q].get(n, 0), v)
+
+    def need(q, reads, writes):
+        tokens = {}
+        own = COUNTER.get(q)
+        for k in list(reads) + list(writes):
+            if k in writer:
+                n, v = writer[k]
+                tokens[n] = max(tokens.get(n, 0), v)
+        for k in writes:
+            for n, v in readers.get(k, []):
+                if n != own:
+                    tokens[n] = max(tokens.get(n, 0), v)
+        for n in sorted(tokens):
+            wait(q, (n, tokens[n]))
+
+    def note(q, token, reads, writes):
+        known[token] = dict(clock[q])
+        for k in reads:
+            readers.setdefault(k, []).append(token)
+        for k in writes:
+            writer[k] = token
+            readers[k] = []
+
+    def run(q, reads, writes, call):
+        need(q, reads, writes)
+        name = COUNTER[q]
+        call(queue[q]).then_inc(T.sem[name], 1)
+        count[name] += 1
+        note(q, (name, count[name]), reads, writes)
+
+    def dma(q, sem, value, reads, writes, out, in_):
+        need(q, reads, writes)
+        queue[q].dma_start(out, in_).then_inc(T.sem[sem], 16)
+        note(q, (sem, value), reads, writes)
+
+    def arrive(token, writes):
+        for k in writes:
+            writer[k] = token
+            readers[k] = []
+
+    def finish(q):
+        for name in sorted(count):
+            if count[name]:
+                wait(q, (name, count[name]))
+
+    return run, dma, need, wait, arrive, finish
+
+
+def rank_program(g, core, T, topo):
+    rank = T.rank_of(core)
+    if rank is None:
+        return
+    A, F = AluOpType, ActivationFunctionType
+    run, dma, need, wait, arrive, finish = _scheduler(g, T)
+    u8, u32 = dt.uint8, dt.uint32
+
+    cores = list(T.cores)
+    first = [c for c in cores if c == cores[0] or topo.same_plane(c, cores[0])]
+    planes = [first, [c for c in cores if c not in first]]
+    mine = 0 if core in first else 1
+    me = planes[mine].index(core)
+    mate = planes[1 - mine][me]
+    assert topo.mates(core, mate)
+    for a in range(2):
+        for i in range(4):
+            assert planes[a][i] == cores[2 * i + a]
+    peers = [c for c in planes[mine] if c != core]
+
+    def bank(b, n):
+        return T.pv[:, 512 * b:512 * b + n]
+
+    dma("s", "dw", 16, [], ["wb"], T.wb[:, 0:128], T.w[:, 0:128])
+    dma("y", "dx", 16, [], ["h0"], T.h0[:, 0:4 * NC], T.x[:])
+    dma("y", "dz", 16, [], ["zt"], T.zt[:], T.z[:])
+    run("g", [], ["ip"], lambda q: q.iota(T.ip[:], [[0, 8]], 0, 1))
+    run("g", [], ["bqc"], lambda q: q.iota(T.bq[:], [[0, 4 * W]], 1, 0, allow_small_or_imprecise_dtypes=True))
+    run("g", ["bqc"], ["bqp"], lambda q: q.iota(
+        T.bq[:, 4 * NC:4 * W], [[0, 4 * W - 4 * NC]], 2, 0, allow_small_or_imprecise_dtypes=True))
+    run("v", [], ["wbz"], lambda q: q.memset(T.wb[:, 128:576], 0.0))
+    run("v", [], ["wl0"], lambda q: q.memset(T.wl0[:], 6))
+    run("v", [], ["hp0"], lambda q: q.memset(T.h0[:, 4 * NC:4 * W], 0.0))
+    run("v", [], ["gone"], lambda q: q.memset(T.gone[:], 1.0))
+    run("g", ["gone"], ["g1"], lambda q: q.affine_select(T.g1[:], T.gone[:], [[-1, 520]], A.is_equal, 0.0, 4, 4))
+    run("g", [], ["ja"], lambda q: q.iota(T.ja[:], [[4, 8]], 0, 0))
+    run("g", [], ["ik"], lambda q: q.iota(T.ik[:], [[0, 8]], L * (4 - me), L))
+    run("g", [], ["idg"], lambda q: q.iota(T.idg[:], [[1, NC]], 128, -1))
+
+    def laid(k):
+        run("v", ["u", "u0", "u1", "u2", "u3", "u4"], ["ut"], lambda q: q.transpose(T.ut[:], T.u[:]))
+        run("v", ["ut", "gkz"], ["gk0"], lambda q: q.tensor_copy(T.gk[:, 0:512:4], T.ut[:]))
+        run("v", ["gk0", "gk1", "gkz"], ["qc%d" % k], lambda q: q.quantize_mx(
+            T.qc[:, 128 * k:128 * k + 128], T.sc[:, 128 * k:128 * k + 128], T.gk[:]))
+
+    def const(k):
+        return T.qc[:, 128 * k:128 * k + 128], T.sc[:, 128 * k:128 * k + 128]
+
+    run("v", [], ["u"], lambda q: q.memset(T.u[:], 0.0))
+    run("v", [], ["gkz"], lambda q: q.memset(T.gk[:], 0.0))
+    for i in range(PL - 1):
+        run("v", ["ip"], ["jb%d" % i], lambda q: q.tensor_scalar(
+            T.jb[0:32, 4 * i:4 * i + 4], T.ip[0:32, 0:4], 1 << i, None, A.bitwise_and))
+    for i in range(PL - 1):
+        run("v", ["jb%d" % i, "u"], ["u%d" % i], lambda q: q.tensor_scalar(
+            T.u[0:32, i:128:32], T.jb[0:32, 4 * i:4 * i + 4], 2 * P / (1 << i), P, A.mult, A.subtract))
+    run("v", ["u"], ["u4"], lambda q: q.memset(T.u[0:32, 4:128:32], -P))
+    run("v", ["gkz"], ["gk1"], lambda q: q.memset(T.gk[:, 1:512:4], -P * PL / 2 / 128))
+    laid(0)
+    run("v", ["u"], ["u4"], lambda q: q.memset(T.u[0:32, 4:128:32], P))
+    laid(1)
+    run("v", [], ["neg"], lambda q: q.memset(T.neg[:], DEEP))
+    run("v", ["neg"], ["negp"], lambda q: q.memset(T.neg[:, NC:W], NONE))
+    run("v", ["wb", "wbz"], ["qwb"], lambda q: q.quantize_mx(T.qwb[:], T.swb[:], T.wb[:]))
+
+    def strength_tile(t):
+        ws, wss, wl = T["ws%d" % t], T["wss%d" % t], T["wl%d" % t]
+        run("s", ["qwb", "wl%d" % t], ["wss%d" % t], lambda q: q.activation(
+            wss[:], T.swb[:].indirect(wl[:]), F.Copy))
+        run("v", ["qwb", "wl%d" % t], ["ws%d" % t], lambda q: q.tensor_copy(
+            ws[:].bitcast(u32), T.qwb[:].bitcast(u32).indirect(wl[:])))
+
+    strength_tile(0)
+    run("v", ["h0", "hp0"], ["qx0"], lambda q: q.quantize_mx(T.qx0[:], T.sx0[:], T.h0[:]))
+
+    def unit_tiles(s, name):
+        src = T[name]
+        for b in range(4):
+            o = 128 * (4 * s + b)
+            run("v", [name], ["e%d%d" % (s, b)], lambda q: q.quantize_mx(
+                T.qe[:, o:o + 128], T.se[:, o:o + 128], src[:, 4 - b:516 - b]))
+
+    def unit(s, b):
+        o = 128 * (4 * s + b)
+        return T.qe[:, o:o + 128], T.se[:, o:o + 128]
+
+    def first_constants():
+        unit_tiles(1, "g1")
+        run("s", ["g1"], ["g8"], lambda q: q.activation(T.g8[:], T.g1[:], F.Copy, scale=0.125))
+        run("s", ["g1"], ["gm"], lambda q: q.activation(T.gm[:], T.g1[:], F.Copy, scale=-0.5))
+        run("v", [], ["u"], lambda q: q.memset(T.u[:], 0.0))
+        for i in range(PL):
+            run("v", ["u"], ["u%d" % i], lambda q: q.memset(T.u[0:32, i:128:32], 2.0 ** i))
+        run("v", ["gkz"], ["gk1"], lambda q: q.memset(T.gk[:, 1:512:4], 0.0))
+        laid(2)
+        run("v", ["idg"], ["idh"], lambda q: q.tensor_scalar(T.idh[:], T.idg[:], 15, None, A.bitwise_and))
+        run("v", [], ["m16"], lambda q: q.memset(T.m16[:], 1.0))
+        run("v", ["idh"], ["dg"], lambda q: q.tensor_scalar(T.dg[:], T.idh[:], 0.0, None, A.is_equal))
+        run("v", ["m16"], ["m16z"], lambda q: q.memset(T.m16[:, 0:NC:16], 0.0))
+        run("v", ["ip"], ["jc"], lambda q: q.tensor_scalar(
+            T.jc[:], T.ip[:], 2, 3, A.arith_shift_right, A.bitwise_and))
+        run("v", ["ik"], ["jd"], lambda q: q.tensor_scalar(T.jd[:], T.ik[:], 3 * L, None, A.bitwise_and))
+        run("v", ["jc", "ja"], ["je"], lambda q: q.tensor_tensor(T.je[:], T.ja[:], T.jc[:], A.add))
+        run("v", [], ["m8"], lambda q: q.memset(T.m8[:], 1.0))
+        run("v", ["jd", "je"], ["jf"], lambda q: q.tensor_tensor(T.jf[:], T.je[:], T.jd[:], A.add))
+        run("v", ["m8"], ["m8z"], lambda q: q.memset(T.m8[:, 0:256:8], 0.0))
+        run("v", ["jf"], ["om"], lambda q: q.tensor_copy(T.om[:], T.jf[:]))
+
+    half = (2 ** PL - 1) / 2
+    for t in range(R):
+        qx, sx = T["qx%d" % t], T["sx%d" % t]
+        kx = "qx%d" % t
+        la, las, lb, lbs = T["la%d" % t], T["las%d" % t], T["lb%d" % t], T["lbs%d" % t]
+        run("t", ["qwb", kx], ["b0"], lambda q: q.matmul_mx(
+            bank(0, W), T.qwb[:, 8 * t:8 * t + 128], T.swb[:, 8 * t:8 * t + 128], qx[:], sx[:], True, True))
+        for c in range(2):
+            run("t", ["ws%d" % t, "wss%d" % t, kx], ["b%d" % (1 + c)], lambda q: q.matmul_mx(
+                bank(1 + c, W), T["ws%d" % t][:], T["wss%d" % t][:], qx[:], sx[:], True, False))
+        run("v", ["b0", "bqc", "bqp"], ["bq"], lambda q: q.tensor_scalar(
+            T.bq[:, 0:4 * W:4], bank(0, W), 0.0, 0.5, A.is_lt, A.subtract))
+        run("v", ["bq"], ["qb"], lambda q: q.quantize_mx(T.qb[:], T.sb[:], T.bq[:]))
+        for c in range(2):
+            e, es = const(c)
+            run("t", ["qc%d" % c, "qb"], ["b%d" % (1 + c)], lambda q: q.matmul_mx(
+                bank(1 + c, W), e, es, T.qb[:], T.sb[:], False, True))
+        for c in range(2):
+            rm, sg = T["rm%d" % c], T["sg%d" % c]
+            run("v", ["b%d" % (1 + c), "neg", "negp"], ["rm%d" % c], lambda q: q.tensor_tensor_scan(
+                rm[:], bank(1 + c, W), T.neg[:], FLOOR, A.max, A.max))
+            run("s", ["rm%d" % c], ["sg%d" % c, "ix%d" % c], lambda q: q.activation(
+                sg[:], rm[:, 0:NC], F.Sign, bias=rm[:, NC:NC + 1], scale=-1.0, accum_out=T.ix[:, c:c + 1]))
+        of = T["of%d" % t]
+        run("v", ["ix0", "ix1"], ["of%d" % t], lambda q: q.tensor_copy(of[:], T.ix[:, 0:2]))
+        run("s", [kx, "of%d" % t], ["reps%d" % t], lambda q: q.activation(
+            las[:, 0:L], sx[:].indirect(of[:]), F.Copy))
+        run("v", [kx, "of%d" % t], ["rep%d" % t], lambda q: q.tensor_copy(
+            la[:, 0:L].bitcast(u32), qx[:].bitcast(u32).indirect(of[:])))
+        ids, slot = [], []
+        for c in peers:
+            rid, pid = topo.addr(c, core)
+            ids.append(DstId(rid=rid, pnc=pid))
+            slot.append(L * ((me - planes[mine].index(c)) % 4))
+        mask = topo.mask(core, peers[0])
+        need("g", ["rep%d" % t], [])
+        g.remote_dma_fused([RemoteDMATransfer(
+            dst_ids=ids, dma_engine_mask=mask, remote_sem=T.sem["planec%d" % t], srcs=[la[:, 0:L].bitcast(u8)],
+            dsts=[la[:, o:o + L].bitcast(u8) for o in slot])], local_sem=T.sem.sent)
+        need("g", ["reps%d" % t], [])
+        g.remote_dma_fused([RemoteDMATransfer(
+            dst_ids=ids, dma_engine_mask=mask, remote_sem=T.sem["planes%d" % t], srcs=[las[:, 0:L]],
+            dsts=[las[:, o:o + L] for o in slot])], local_sem=T.sem.sent)
+        n = len(topo.engines(core, peers[0])) * len(peers)
+        arrive(("planec%d" % t, n), ["pc%d" % t])
+        arrive(("planes%d" % t, n), ["ps%d" % t])
+        rid, pid = topo.addr(mate, core)
+        mask = topo.mask(core, mate)
+        mc, ms = T.sem["matec%d" % t], T.sem["mates%d" % t]
+        g.remote_dma(lb[:, 0:L].bitcast(u8), la[:, 0:L].bitcast(u8), mc, T.sem.sent, pid, rid, mask)
+        g.remote_dma(lbs[:, 0:L], las[:, 0:L], ms, T.sem.sent, pid, rid, mask)
+        need("g", ["pc%d" % t], [])
+        g.remote_dma(lb[:, L:4 * L].bitcast(u8), la[:, L:4 * L].bitcast(u8), mc, T.sem.sent, pid, rid, mask)
+        need("g", ["ps%d" % t], [])
+        g.remote_dma(lbs[:, L:4 * L], las[:, L:4 * L], ms, T.sem.sent, pid, rid, mask)
+        n = 2 * len(topo.engines(core, mate))
+        arrive(("matec%d" % t, n), ["mc%d" % t])
+        arrive(("mates%d" % t, n), ["ms%d" % t])
+        if t == 0:
+            first_constants()
+        e, es = const(2)
+        run("t", ["qc2", "qb"], ["b3"], lambda q: q.matmul_mx(
+            bank(3, NC), e, es, T.qb[:, 0:NC], T.sb[:, 0:NC], True, True))
+        for b in range(4):
+            e, es = unit(1, b)
+            run("t", ["e1%d" % b, kx], ["px%d" % b], lambda q: q.matmul_mx(
+                T.px[:, 512 * b:512 * b + NC], e, es, qx[:, 0:NC], sx[:, 0:NC], True, False))
+        run("s", ["b3"], ["lt"], lambda q: q.activation(T.lt[:], bank(3, NC), F.Copy))
+        run("s", ["b3"], ["lvs%d" % t], lambda q: q.activation(
+            T.lvs[0:1, NC * t:NC * t + NC], T.pv[0:1, 3 * 512:3 * 512 + NC], F.Identity, bias=half))
+        dma("y", "dlv", 16 * (t + 1), ["lvs%d" % t], [], T.lv[t:t + 1, :], T.lvs[0:1, NC * t:NC * t + NC])
+        run("v", ["lt", "dg"], ["ld"], lambda q: q.tensor_tensor(T.ld[:], T.lt[:], T.dg[:], A.mult))
+        run("v", ["ld", "m16", "m16z"], ["ls"], lambda q: q.tensor_tensor_scan(
+            T.ls[:], T.m16[:], T.ld[:], 0.0, A.mult, A.add))
+        ov = T["ov%d" % t]
+        run("v", ["ls"], ["ov%d" % t], lambda q: q.tensor_scalar(
+            ov[:], T.ls[:, 15:NC:16], 8.0, 8.0 * half + 7.0, A.mult, A.add))
+        if t == 0:
+            unit_tiles(0, "g8")
+
+        def plane_values(src, srcs, out, outs, kq, kc, ks, a, engine):
+            run("v", kc + ["om"], [kq], lambda q: q.tensor_copy(
+                out[:].bitcast(u32), src[:].bitcast(u32).indirect(T.om[:])))
+            run("s", ks + ["om"], [kq + "s"], lambda q: q.activation(outs[:], srcs[:].indirect(T.om[:]), F.Copy))
+            for b in range(4):
+                e, es = unit(0, b)
+                run("t", ["e0%d" % b, kq, kq + "s"], ["b%d" % b], lambda q: q.matmul_mx(
+                    bank(b, 4 * L), e, es, out[:], outs[:], True, True))
+            for b in range(4):
+                place = T.va[:, 256 * b + a:256 * b + 256:2]
+                if engine[b] == "s":
+                    run("s", ["b%d" % b], ["va%d%d" % (b, a)], lambda q: q.activation(place, bank(b, 4 * L), F.Copy))
+                else:
+                    run("v", ["b%d" % b], ["va%d%d" % (b, a)], lambda q: q.tensor_copy(place, bank(b, 4 * L)))
+
+        plane_values(la, las, T["qa%d" % t], T["qas%d" % t], "qa%d" % t, ["rep%d" % t, "pc%d" % t],
+                     ["reps%d" % t, "ps%d" % t], mine, "ssss")
+        if t == 0:
+            unit_tiles(2, "gm")
+        if t == 1:
+            run("v", ["zt"], ["qz"], lambda q: q.quantize_mx(T.qz[:], T.sz[:], T.zt[:]))
+        if t + 1 < R:
+            run("v", [], ["wl%d" % (t + 1)], lambda q: q.memset(T["wl%d" % (t + 1)][:], 8 * (t + 1) + 6))
+            strength_tile(t + 1)
+        hn = T["h%d" % (t + 1)]
+        run("v", [], ["hp%d" % (t + 1)], lambda q: q.memset(hn[:, 4 * NC:4 * W], 0.0))
+        plane_values(lb, lbs, T["qm%d" % t], T["qms%d" % t], "qm%d" % t, ["mc%d" % t], ["ms%d" % t], 1 - mine, "vsss")
+        for b in range(4):
+            run("v", ["va%d0" % b, "va%d1" % b, "m8", "m8z"], ["vs%d" % b], lambda q: q.tensor_tensor_scan(
+                T.vs[:, b:1024:4], T.m8[:], T.va[:, 256 * b:256 * b + 256], 0.0, A.mult, A.add))
+        qv, qvs = T["qv%d" % t], T["qvs%d" % t]
+        run("v", ["vs0", "vs1", "vs2", "vs3"], ["qv%d" % t], lambda q: q.quantize_mx(qv[:], qvs[:], T.vs[:]))
+        vv, vvs = T["vv%d" % t], T["vvs%d" % t]
+        run("s", ["qv%d" % t, "ov%d" % t], ["vvs%d" % t], lambda q: q.activation(vvs[:], qvs[:].indirect(ov[:]), F.Copy))
+        run("v", ["qv%d" % t, "ov%d" % t], ["vv%d" % t], lambda q: q.tensor_copy(
+            vv[:].bitcast(u32), qv[:].bitcast(u32).indirect(ov[:])))
+        for b in range(4):
+            e, es = unit(2, b)
+            run("t", ["e2%d" % b, "vv%d" % t, "vvs%d" % t], ["px%d" % b], lambda q: q.matmul_mx(
+                T.px[:, 512 * b:512 * b + NC], e, es, vv[:], vvs[:], False, True))
+        for b in range(4):
+            out, in_ = hn[:, b:4 * NC:4], T.px[:, 512 * b:512 * b + NC]
+            if b % 2 == 0:
+                run("s", ["px%d" % b], ["h%d%d" % (t + 1, b)], lambda q: q.activation(out, in_, F.Copy))
+            else:
+                run("v", ["px%d" % b], ["h%d%d" % (t + 1, b)], lambda q: q.tensor_copy(out, in_))
+        run("v", ["h%d%d" % (t + 1, b) for b in range(4)] + ["hp%d" % (t + 1)], ["qx%d" % (t + 1)],
+            lambda q: q.quantize_mx(T["qx%d" % (t + 1)][:], T["sx%d" % (t + 1)][:], hn[:]))
+
+    qx, sx = T["qx%d" % R], T["sx%d" % R]
+    kx = "qx%d" % R
+    run("t", ["qz", kx], ["b0"], lambda q: q.matmul_mx(
+        bank(0, NC), T.qz[:], T.sz[:], qx[:, 0:NC], sx[:, 0:NC], True, True))
+    total = 16 * 6
+    dma("y", "dout", total, [kx], [], T.oc[:], qx[:, 0:NC].bitcast(u8))
+    for k in range(4):
+        dma("s", "dout", total, [kx], [], T.osc[4 * k:4 * k + 4, :], sx[32 * k:32 * k + 4, 0:NC])
+    run("v", ["b0"], ["ysb"], lambda q: q.tensor_copy(T.ysb[:], bank(0, NC)))
+    dma("y", "dout", total, ["ysb"], [], T.y[:], T.ysb[:])
+    wait("g", ("sent", R * (2 * len(topo.engines(core, peers[0])) + 4 * len(topo.engines(core, mate)))))
+    finish("g")
+    wait("g", ("dlv", 16 * R))
+    wait("g", ("dout", total))

@@ -3,38 +3,30 @@ from concourse.mybir import dt, AluOpType, ActivationFunctionType
 
 NC, L, R, PL = 192, 32, 3, 5
 W = NC + 2
-P, FLOOR, NONE, DEEP = 2.0 ** 76, -2.0 ** 74, -2.0 ** 72, -2.0 ** 80
+S = 5 * L
+P, FLOOR, NONE, DEEP, BIG = 2.0 ** 76, -2.0 ** 74, -2.0 ** 72, -2.0 ** 80, 2.0 ** 64
 X4, BF, F32, U8, I32, U16 = "float8_e4m3fn_x4", "bfloat16", "float32", "uint8", "int32", "uint16"
 
-SCRATCH = {
-    "wb": ("sbuf", [128, 576], BF), "zt": ("sbuf", [128, 512], BF),
-    "qwb": ("sbuf", [128, 144], X4), "swb": ("sbuf", [128, 144], U8),
-    "qz": ("sbuf", [128, 128], X4), "sz": ("sbuf", [128, 128], U8),
-    "gone": ("sbuf", [128, 520], BF), "g1": ("sbuf", [128, 520], BF), "g8": ("sbuf", [128, 520], BF),
-    "gm": ("sbuf", [128, 520], BF),
-    "qe": ("sbuf", [128, 12 * 128], X4), "se": ("sbuf", [128, 12 * 128], U8),
-    "u": ("sbuf", [128, 128], BF), "ut": ("sbuf", [128, 128], BF), "gk": ("sbuf", [128, 512], BF),
-    "qc": ("sbuf", [128, 3 * 128], X4), "sc": ("sbuf", [128, 3 * 128], U8),
-    "bq": ("sbuf", [128, 4 * W], BF), "qb": ("sbuf", [128, W], X4), "sb": ("sbuf", [128, W], U8),
-    "m8": ("sbuf", [128, 256], BF), "m16": ("sbuf", [128, NC], BF),
-    "idg": ("sbuf", [128, NC], I32), "idh": ("sbuf", [128, NC], I32), "dg": ("sbuf", [128, NC], BF),
-    "neg": ("sbuf", [128, W], BF),
-    "ip": ("sbuf", [128, 8], I32), "jb": ("sbuf", [128, 16], I32), "ja": ("sbuf", [128, 8], I32),
-    "ik": ("sbuf", [128, 8], I32), "jc": ("sbuf", [128, 8], I32), "jd": ("sbuf", [128, 8], I32),
-    "je": ("sbuf", [128, 8], I32), "jf": ("sbuf", [128, 8], I32), "om": ("sbuf", [128, 8], U16),
-    "rm0": ("sbuf", [128, W], F32), "rm1": ("sbuf", [128, W], F32),
-    "sg0": ("sbuf", [128, NC], BF), "sg1": ("sbuf", [128, NC], BF), "ix": ("sbuf", [128, 4], F32),
-    "lt": ("sbuf", [128, NC], BF), "ld": ("sbuf", [128, NC], BF), "ls": ("sbuf", [128, NC], F32),
-    "lvs": ("sbuf", [128, R * NC], F32),
-    "va": ("sbuf", [128, 1024], BF), "vs": ("sbuf", [128, 1024], BF), "ysb": ("sbuf", [128, NC], F32),
-    "pv": ("psum", [128, 2048], F32), "px": ("psum", [128, 2048], F32),
-}
+SCRATCH = {"pv": ("psum", [128, 2048], F32), "px": ("psum", [128, 2048], F32)}
+for _n, _w, _d in (
+        ("wb", 576, BF), ("zt", 512, BF), ("qwb", 144, X4), ("swb", 144, U8), ("qz", 128, X4), ("sz", 128, U8),
+        ("gone", 520, BF), ("g1", 520, BF), ("g8", 520, BF), ("gm", 520, BF), ("ct", 520, BF),
+        ("qe", 12 * 128, X4), ("se", 12 * 128, U8), ("u", 256, BF), ("ut", 256, BF), ("gk", 1024, BF),
+        ("qc", 3 * 128, X4), ("sc", 3 * 128, U8), ("bq", 4 * W, BF), ("qb", W, X4), ("sb", W, U8),
+        ("m16", NC, BF), ("idg", NC, I32), ("idh", NC, I32), ("dg", NC, BF), ("neg", W, BF),
+        ("jb", 32, I32), ("jm", 32, I32), ("jp", 32, BF), ("ip", 10, I32), ("ja", 10, I32), ("jc", 10, I32),
+        ("jj", 10, I32), ("jf", 10, F32), ("jl", 10, I32), ("j5", 10, I32), ("jk", 10, I32), ("j3", 10, I32),
+        ("jr", 10, I32), ("jx", 10, I32), ("jy", 10, I32), ("jz", 10, I32), ("om", 10, U16),
+        ("rm0", W, F32), ("rm1", W, F32), ("sg0", NC, BF), ("sg1", NC, BF), ("ix", 4, F32),
+        ("lt", NC, BF), ("ld", NC, BF), ("ls", NC, F32), ("lvs", R * NC, F32),
+        ("va", 4 * S, BF), ("vb", 4 * S, BF), ("vs", 4 * S, BF), ("ysb", NC, F32)):
+    SCRATCH[_n] = ("sbuf", [128, _w], _d)
 for _t in range(R + 1):
     SCRATCH["h%d" % _t] = ("sbuf", [128, 4 * W], BF)
     SCRATCH["qx%d" % _t] = ("sbuf", [128, W], X4)
     SCRATCH["sx%d" % _t] = ("sbuf", [128, W], U8)
 for _t in range(R):
-    for _n, _w in (("ws", 128), ("la", 128), ("lb", 128), ("qa", 128), ("qm", 128), ("qv", 256), ("vv", NC)):
+    for _n, _w in (("ws", 128), ("la", 256), ("lb", 256), ("qa", S), ("qm", S), ("qv", S), ("vv", NC)):
         SCRATCH["%s%d" % (_n, _t)] = ("sbuf", [128, _w], X4)
         SCRATCH["%ss%d" % (_n, _t)] = ("sbuf", [128, _w], U8)
     SCRATCH["wl%d" % _t] = ("sbuf", [128, 8], U16)
@@ -127,52 +119,51 @@ def rank_program(g, core, T, topo):
     for a in range(2):
         for i in range(4):
             assert planes[a][i] == cores[2 * i + a]
-    peers = [c for c in planes[mine] if c != core]
+    peers = [planes[mine][(me + k) % 4] for k in (1, 2, 3)]
 
     def bank(b, n):
         return T.pv[:, 512 * b:512 * b + n]
 
     dma("s", "dw", 16, [], ["wb"], T.wb[:, 0:128], T.w[:, 0:128])
     dma("y", "dx", 16, [], ["h0"], T.h0[:, 0:4 * NC], T.x[:])
-    dma("y", "dz", 16, [], ["zt"], T.zt[:], T.z[:])
-    run("g", [], ["ip"], lambda q: q.iota(T.ip[:], [[0, 8]], 0, 1))
-    run("g", [], ["bqc"], lambda q: q.iota(T.bq[:], [[0, 4 * W]], 1, 0, allow_small_or_imprecise_dtypes=True))
-    run("g", ["bqc"], ["bqp"], lambda q: q.iota(
-        T.bq[:, 4 * NC:4 * W], [[0, 4 * W - 4 * NC]], 2, 0, allow_small_or_imprecise_dtypes=True))
-    run("v", [], ["wbz"], lambda q: q.memset(T.wb[:, 128:576], 0.0))
-    run("v", [], ["wl0"], lambda q: q.memset(T.wl0[:], 6))
-    run("v", [], ["hp0"], lambda q: q.memset(T.h0[:, 4 * NC:4 * W], 0.0))
-    run("v", [], ["gone"], lambda q: q.memset(T.gone[:], 1.0))
-    run("g", ["gone"], ["g1"], lambda q: q.affine_select(T.g1[:], T.gone[:], [[-1, 520]], A.is_equal, 0.0, 4, 4))
-    run("g", [], ["ja"], lambda q: q.iota(T.ja[:], [[4, 8]], 0, 0))
-    run("g", [], ["ik"], lambda q: q.iota(T.ik[:], [[0, 8]], L * (4 - me), L))
-    run("g", [], ["idg"], lambda q: q.iota(T.idg[:], [[1, NC]], 128, -1))
-
-    def laid(k):
-        run("v", ["u", "u0", "u1", "u2", "u3", "u4"], ["ut"], lambda q: q.transpose(T.ut[:], T.u[:]))
-        run("v", ["ut", "gkz"], ["gk0"], lambda q: q.tensor_copy(T.gk[:, 0:512:4], T.ut[:]))
-        run("v", ["gk0", "gk1", "gkz"], ["qc%d" % k], lambda q: q.quantize_mx(
-            T.qc[:, 128 * k:128 * k + 128], T.sc[:, 128 * k:128 * k + 128], T.gk[:]))
+    for i in range(PL - 1):
+        run("g", [], ["jb%d" % i], lambda q: q.iota(T.jb[0:32, 8 * i:8 * i + 8], [[0, 8]], 0, 8 >> i))
 
     def const(k):
         return T.qc[:, 128 * k:128 * k + 128], T.sc[:, 128 * k:128 * k + 128]
 
-    run("v", [], ["u"], lambda q: q.memset(T.u[:], 0.0))
+    us = ["u%d" % i for i in range(PL + 1)]
     run("v", [], ["gkz"], lambda q: q.memset(T.gk[:], 0.0))
-    for i in range(PL - 1):
-        run("v", ["ip"], ["jb%d" % i], lambda q: q.tensor_scalar(
-            T.jb[0:32, 4 * i:4 * i + 4], T.ip[0:32, 0:4], 1 << i, None, A.bitwise_and))
-    for i in range(PL - 1):
-        run("v", ["jb%d" % i, "u"], ["u%d" % i], lambda q: q.tensor_scalar(
-            T.u[0:32, i:128:32], T.jb[0:32, 4 * i:4 * i + 4], 2 * P / (1 << i), P, A.mult, A.subtract))
+    run("v", [], ["u"], lambda q: q.memset(T.u[0:32, :], 0.0))
+    run("s", ["gkz"], ["gone"], lambda q: q.activation(T.gone[:], T.gk[:, 0:520], F.Identity, bias=1.0))
+    run("g", ["gone"], ["g1"], lambda q: q.affine_select(T.g1[:], T.gone[:], [[-1, 520]], A.is_equal, 0.0, 4, 4))
+    run("s", ["gone"], ["bqa"], lambda q: q.activation(T.bq[:, 0:512], T.gone[:, 0:512], F.Copy))
+    run("s", ["gone"], ["bqc"], lambda q: q.activation(T.bq[:, 512:4 * NC], T.gone[:, 0:4 * NC - 512], F.Copy))
+    run("s", ["gone"], ["bqp"], lambda q: q.activation(
+        T.bq[:, 4 * NC:4 * W], T.gone[:, 0:4 * W - 4 * NC], F.Copy, scale=2.0))
+    run("v", ["jb%d" % i for i in range(PL - 1)], ["jm"], lambda q: q.tensor_scalar(
+        T.jm[0:32, :], T.jb[0:32, :], 8, None, A.bitwise_and))
     run("v", ["u"], ["u4"], lambda q: q.memset(T.u[0:32, 4:128:32], -P))
-    run("v", ["gkz"], ["gk1"], lambda q: q.memset(T.gk[:, 1:512:4], -P * PL / 2 / 128))
-    laid(0)
-    run("v", ["u"], ["u4"], lambda q: q.memset(T.u[0:32, 4:128:32], P))
-    laid(1)
-    run("v", [], ["neg"], lambda q: q.memset(T.neg[:], DEEP))
-    run("v", ["neg"], ["negp"], lambda q: q.memset(T.neg[:, NC:W], NONE))
+    run("v", ["jm"], ["jp"], lambda q: q.tensor_scalar(
+        T.jp[0:32, :], T.jm[0:32, :], 2 * P / 8, P, A.mult, A.subtract))
+    run("v", ["u"], ["u5"], lambda q: q.memset(T.u[0:32, 132:256:32], P))
+    for i in range(PL - 1):
+        run("v", ["jp", "u"], ["u%d" % i], lambda q: q.tensor_copy(T.u[0:32, i:256:32], T.jp[0:32, 8 * i:8 * i + 8]))
+    run("v", ["gkz", "gone"], ["gk1"], lambda q: q.memset(T.gk[:, 1:1024:4], -P * PL / 2 / 128))
+    run("v", ["u"] + us, ["ut"], lambda q: q.transpose(T.ut[0:32, :], T.u[0:32, :]))
+    run("v", [], ["wbz"], lambda q: q.memset(T.wb[:, 128:576], 0.0))
+    run("v", ["ut", "gkz", "gone"], ["gk0"], lambda q: q.tensor_copy(T.gk[0:32, 0:1024:4], T.ut[0:32, :]))
+    run("v", [], ["wl0"], lambda q: q.memset(T.wl0[:], 6))
+    run("v", [], ["hp0"], lambda q: q.memset(T.h0[:, 4 * NC:4 * W], 0.0))
+    run("v", ["gk0", "gk1", "gkz"], ["qc0", "qc1"], lambda q: q.quantize_mx(T.qc[:, 0:256], T.sc[:, 0:256], T.gk[:]))
     run("v", ["wb", "wbz"], ["qwb"], lambda q: q.quantize_mx(T.qwb[:], T.swb[:], T.wb[:]))
+    run("v", ["h0", "hp0"], ["qx0"], lambda q: q.quantize_mx(T.qx0[:], T.sx0[:], T.h0[:]))
+    dma("y", "dz", 16, ["qx0"], ["zt"], T.zt[:], T.z[:])
+    run("g", [], ["ip"], lambda q: q.iota(T.ip[:], [[0, 10]], 0, 1))
+    run("g", [], ["ja"], lambda q: q.iota(T.ja[:], [[16, 10]], 0, 0))
+    run("g", [], ["idg"], lambda q: q.iota(T.idg[:], [[1, NC]], 128, -1))
+    run("s", ["gone"], ["neg"], lambda q: q.activation(T.neg[:, 0:NC], T.gone[:, 0:NC], F.Copy, scale=DEEP))
+    run("s", ["gone"], ["negp"], lambda q: q.activation(T.neg[:, NC:W], T.gone[:, 0:W - NC], F.Copy, scale=NONE))
 
     def strength_tile(t):
         ws, wss, wl = T["ws%d" % t], T["wss%d" % t], T["wl%d" % t]
@@ -181,12 +172,9 @@ def rank_program(g, core, T, topo):
         run("v", ["qwb", "wl%d" % t], ["ws%d" % t], lambda q: q.tensor_copy(
             ws[:].bitcast(u32), T.qwb[:].bitcast(u32).indirect(wl[:])))
 
-    strength_tile(0)
-    run("v", ["h0", "hp0"], ["qx0"], lambda q: q.quantize_mx(T.qx0[:], T.sx0[:], T.h0[:]))
-
-    def unit_tiles(s, name):
+    def unit_tiles(s, name, which=(0, 1, 2, 3)):
         src = T[name]
-        for b in range(4):
+        for b in which:
             o = 128 * (4 * s + b)
             run("v", [name], ["e%d%d" % (s, b)], lambda q: q.quantize_mx(
                 T.qe[:, o:o + 128], T.se[:, o:o + 128], src[:, 4 - b:516 - b]))
@@ -196,26 +184,41 @@ def rank_program(g, core, T, topo):
         return T.qe[:, o:o + 128], T.se[:, o:o + 128]
 
     def first_constants():
-        unit_tiles(1, "g1")
-        run("s", ["g1"], ["g8"], lambda q: q.activation(T.g8[:], T.g1[:], F.Copy, scale=0.125))
-        run("s", ["g1"], ["gm"], lambda q: q.activation(T.gm[:], T.g1[:], F.Copy, scale=-0.5))
-        run("v", [], ["u"], lambda q: q.memset(T.u[:], 0.0))
-        for i in range(PL):
-            run("v", ["u"], ["u%d" % i], lambda q: q.memset(T.u[0:32, i:128:32], 2.0 ** i))
+        run("v", ["ip"], ["jc"], lambda q: q.tensor_scalar(T.jc[:], T.ip[:], 15, None, A.bitwise_and))
+        run("v", [], ["u"], lambda q: q.memset(T.u[0:32, 0:128], 0.0))
+        run("v", ["jc", "ja"], ["jj"], lambda q: q.tensor_tensor(T.jj[:], T.ja[:], T.jc[:], A.add))
         run("v", ["gkz"], ["gk1"], lambda q: q.memset(T.gk[:, 1:512:4], 0.0))
-        laid(2)
+        for i in range(PL):
+            run("s", ["u", "gone"], ["u%d" % i], lambda q: q.activation(
+                T.u[0:32, i:128:32], T.gone[0:32, 0:4], F.Copy, scale=2.0 ** i))
+        run("s", ["g1"], ["g8"], lambda q: q.activation(T.g8[:], T.g1[:], F.Copy, scale=0.125))
+        run("s", ["gone"], ["m16"], lambda q: q.activation(T.m16[:], T.gone[:, 0:NC], F.Copy))
+        run("s", ["g1"], ["gm"], lambda q: q.activation(T.gm[:], T.g1[:], F.Copy, scale=-0.5))
+        run("s", ["gone", "m16"], ["m16z"], lambda q: q.activation(
+            T.m16[:, 0:NC:16], T.gone[:, 0:12], F.Copy, scale=0.0))
+        run("v", ["jj"], ["jf"], lambda q: q.tensor_scalar(T.jf[:], T.jj[:], -2.0, 0.2, A.add, A.mult))
         run("v", ["idg"], ["idh"], lambda q: q.tensor_scalar(T.idh[:], T.idg[:], 15, None, A.bitwise_and))
-        run("v", [], ["m16"], lambda q: q.memset(T.m16[:], 1.0))
+        run("v", ["jf"], ["jl"], lambda q: q.tensor_copy(T.jl[:], T.jf[:]))
         run("v", ["idh"], ["dg"], lambda q: q.tensor_scalar(T.dg[:], T.idh[:], 0.0, None, A.is_equal))
-        run("v", ["m16"], ["m16z"], lambda q: q.memset(T.m16[:, 0:NC:16], 0.0))
-        run("v", ["ip"], ["jc"], lambda q: q.tensor_scalar(
-            T.jc[:], T.ip[:], 2, 3, A.arith_shift_right, A.bitwise_and))
-        run("v", ["ik"], ["jd"], lambda q: q.tensor_scalar(T.jd[:], T.ik[:], 3 * L, None, A.bitwise_and))
-        run("v", ["jc", "ja"], ["je"], lambda q: q.tensor_tensor(T.je[:], T.ja[:], T.jc[:], A.add))
-        run("v", [], ["m8"], lambda q: q.memset(T.m8[:], 1.0))
-        run("v", ["jd", "je"], ["jf"], lambda q: q.tensor_tensor(T.jf[:], T.je[:], T.jd[:], A.add))
-        run("v", ["m8"], ["m8z"], lambda q: q.memset(T.m8[:, 0:256:8], 0.0))
-        run("v", ["jf"], ["om"], lambda q: q.tensor_copy(T.om[:], T.jf[:]))
+        run("v", ["jl"], ["j5"], lambda q: q.tensor_scalar(T.j5[:], T.jl[:], -5.0, 4.0 - me, A.mult, A.add))
+        run("v", ["u"] + us, ["ut"], lambda q: q.transpose(T.ut[0:32, 0:128], T.u[0:32, 0:128]))
+        run("v", ["j5", "jj"], ["jk"], lambda q: q.tensor_tensor(T.jk[:], T.j5[:], T.jj[:], A.add))
+        run("v", ["ut", "gkz"], ["gk0"], lambda q: q.tensor_copy(T.gk[0:32, 0:512:4], T.ut[0:32, 0:128]))
+        run("v", ["jk"], ["j3"], lambda q: q.tensor_scalar(T.j3[:], T.jk[:], 3, None, A.bitwise_and))
+        run("v", ["jk"], ["jr"], lambda q: q.tensor_scalar(T.jr[:], T.jk[:], 8.0 - me, 4.0 * L, A.is_ge, A.mult))
+        run("v", ["j3"], ["jx"], lambda q: q.tensor_scalar(T.jx[:], T.j3[:], 1.0 * L, None, A.mult))
+        run("v", ["gk0", "gk1", "gkz"], ["qc2"], lambda q: q.quantize_mx(
+            T.qc[:, 256:384], T.sc[:, 256:384], T.gk[:, 0:512]))
+        run("v", ["jx", "jl"], ["jy"], lambda q: q.tensor_tensor(T.jy[:], T.jx[:], T.jl[:], A.add))
+        restart_column(T.la0, T.las0, "ra0", mine)
+        run("v", ["jy", "jr"], ["jz"], lambda q: q.tensor_tensor(T.jz[:], T.jy[:], T.jr[:], A.max))
+        restart_column(T.lb0, T.lbs0, "rb0", 1 - mine)
+        run("v", ["jz"], ["om"], lambda q: q.tensor_copy(T.om[:], T.jz[:]))
+        unit_tiles(0, "g8")
+
+    def restart_column(codes, scales, key, a):
+        run("v", ["ct", "ctm"], [key], lambda q: q.quantize_mx(
+            codes[:, 128:256], scales[:, 128:256], T.ct[:, 4 * a:4 * a + 512]))
 
     half = (2 ** PL - 1) / 2
     for t in range(R):
@@ -224,12 +227,18 @@ def rank_program(g, core, T, topo):
         la, las, lb, lbs = T["la%d" % t], T["las%d" % t], T["lb%d" % t], T["lbs%d" % t]
         run("t", ["qwb", kx], ["b0"], lambda q: q.matmul_mx(
             bank(0, W), T.qwb[:, 8 * t:8 * t + 128], T.swb[:, 8 * t:8 * t + 128], qx[:], sx[:], True, True))
+        if t == 0:
+            strength_tile(0)
+            run("s", ["gone"], ["ctm"], lambda q: q.activation(T.ct[:], T.gone[:], F.Copy, scale=-BIG))
+            run("s", ["gone", "ctm"], ["ct"], lambda q: q.activation(T.ct[:, 0:4], T.gone[:, 0:4], F.Copy, scale=BIG))
         for c in range(2):
             run("t", ["ws%d" % t, "wss%d" % t, kx], ["b%d" % (1 + c)], lambda q: q.matmul_mx(
                 bank(1 + c, W), T["ws%d" % t][:], T["wss%d" % t][:], qx[:], sx[:], True, False))
-        run("v", ["b0", "bqc", "bqp"], ["bq"], lambda q: q.tensor_scalar(
+        run("v", ["b0", "bqa", "bqc", "bqp"], ["bq"], lambda q: q.tensor_scalar(
             T.bq[:, 0:4 * W:4], bank(0, W), 0.0, 0.5, A.is_lt, A.subtract))
         run("v", ["bq"], ["qb"], lambda q: q.quantize_mx(T.qb[:], T.sb[:], T.bq[:]))
+        if t == 0:
+            unit_tiles(1, "g1", (0, 1))
         for c in range(2):
             e, es = const(c)
             run("t", ["qc%d" % c, "qb"], ["b%d" % (1 + c)], lambda q: q.matmul_mx(
@@ -240,6 +249,8 @@ def rank_program(g, core, T, topo):
                 rm[:], bank(1 + c, W), T.neg[:], FLOOR, A.max, A.max))
             run("s", ["rm%d" % c], ["sg%d" % c, "ix%d" % c], lambda q: q.activation(
                 sg[:], rm[:, 0:NC], F.Sign, bias=rm[:, NC:NC + 1], scale=-1.0, accum_out=T.ix[:, c:c + 1]))
+        if t == 0:
+            unit_tiles(1, "g1", (2, 3))
         of = T["of%d" % t]
         run("v", ["ix0", "ix1"], ["of%d" % t], lambda q: q.tensor_copy(of[:], T.ix[:, 0:2]))
         run("s", [kx, "of%d" % t], ["reps%d" % t], lambda q: q.activation(
@@ -267,16 +278,18 @@ def rank_program(g, core, T, topo):
         mask = topo.mask(core, mate)
         mc, ms = T.sem["matec%d" % t], T.sem["mates%d" % t]
         g.remote_dma(lb[:, 0:L].bitcast(u8), la[:, 0:L].bitcast(u8), mc, T.sem.sent, pid, rid, mask)
-        g.remote_dma(lbs[:, 0:L], las[:, 0:L], ms, T.sem.sent, pid, rid, mask)
         need("g", ["pc%d" % t], [])
         g.remote_dma(lb[:, L:4 * L].bitcast(u8), la[:, L:4 * L].bitcast(u8), mc, T.sem.sent, pid, rid, mask)
         need("g", ["ps%d" % t], [])
-        g.remote_dma(lbs[:, L:4 * L], las[:, L:4 * L], ms, T.sem.sent, pid, rid, mask)
-        n = 2 * len(topo.engines(core, mate))
-        arrive(("matec%d" % t, n), ["mc%d" % t])
+        g.remote_dma(lbs[:, 0:4 * L], las[:, 0:4 * L], ms, T.sem.sent, pid, rid, mask)
+        n = len(topo.engines(core, mate))
+        arrive(("matec%d" % t, 2 * n), ["mc%d" % t])
         arrive(("mates%d" % t, n), ["ms%d" % t])
         if t == 0:
             first_constants()
+        else:
+            restart_column(la, las, "ra%d" % t, mine)
+            restart_column(lb, lbs, "rb%d" % t, 1 - mine)
         e, es = const(2)
         run("t", ["qc2", "qb"], ["b3"], lambda q: q.matmul_mx(
             bank(3, NC), e, es, T.qb[:, 0:NC], T.sb[:, 0:NC], True, True))
@@ -288,45 +301,58 @@ def rank_program(g, core, T, topo):
         run("s", ["b3"], ["lvs%d" % t], lambda q: q.activation(
             T.lvs[0:1, NC * t:NC * t + NC], T.pv[0:1, 3 * 512:3 * 512 + NC], F.Identity, bias=half))
         dma("y", "dlv", 16 * (t + 1), ["lvs%d" % t], [], T.lv[t:t + 1, :], T.lvs[0:1, NC * t:NC * t + NC])
+        ov, hn = T["ov%d" % t], T["h%d" % (t + 1)]
         run("v", ["lt", "dg"], ["ld"], lambda q: q.tensor_tensor(T.ld[:], T.lt[:], T.dg[:], A.mult))
-        run("v", ["ld", "m16", "m16z"], ["ls"], lambda q: q.tensor_tensor_scan(
-            T.ls[:], T.m16[:], T.ld[:], 0.0, A.mult, A.add))
-        ov = T["ov%d" % t]
-        run("v", ["ls"], ["ov%d" % t], lambda q: q.tensor_scalar(
-            ov[:], T.ls[:, 15:NC:16], 8.0, 8.0 * half + 7.0, A.mult, A.add))
-        if t == 0:
-            unit_tiles(0, "g8")
-
-        def plane_values(src, srcs, out, outs, kq, kc, ks, a, engine):
-            run("v", kc + ["om"], [kq], lambda q: q.tensor_copy(
-                out[:].bitcast(u32), src[:].bitcast(u32).indirect(T.om[:])))
-            run("s", ks + ["om"], [kq + "s"], lambda q: q.activation(outs[:], srcs[:].indirect(T.om[:]), F.Copy))
-            for b in range(4):
-                e, es = unit(0, b)
-                run("t", ["e0%d" % b, kq, kq + "s"], ["b%d" % b], lambda q: q.matmul_mx(
-                    bank(b, 4 * L), e, es, out[:], outs[:], True, True))
-            for b in range(4):
-                place = T.va[:, 256 * b + a:256 * b + 256:2]
-                if engine[b] == "s":
-                    run("s", ["b%d" % b], ["va%d%d" % (b, a)], lambda q: q.activation(place, bank(b, 4 * L), F.Copy))
-                else:
-                    run("v", ["b%d" % b], ["va%d%d" % (b, a)], lambda q: q.tensor_copy(place, bank(b, 4 * L)))
-
-        plane_values(la, las, T["qa%d" % t], T["qas%d" % t], "qa%d" % t, ["rep%d" % t, "pc%d" % t],
-                     ["reps%d" % t, "ps%d" % t], mine, "ssss")
-        if t == 0:
-            unit_tiles(2, "gm")
-        if t == 1:
-            run("v", ["zt"], ["qz"], lambda q: q.quantize_mx(T.qz[:], T.sz[:], T.zt[:]))
         if t + 1 < R:
             run("v", [], ["wl%d" % (t + 1)], lambda q: q.memset(T["wl%d" % (t + 1)][:], 8 * (t + 1) + 6))
-            strength_tile(t + 1)
-        hn = T["h%d" % (t + 1)]
+        run("v", ["ld", "m16", "m16z"], ["ls"], lambda q: q.tensor_tensor_scan(
+            T.ls[:], T.m16[:], T.ld[:], 0.0, A.mult, A.add))
         run("v", [], ["hp%d" % (t + 1)], lambda q: q.memset(hn[:, 4 * NC:4 * W], 0.0))
-        plane_values(lb, lbs, T["qm%d" % t], T["qms%d" % t], "qm%d" % t, ["mc%d" % t], ["ms%d" % t], 1 - mine, "vsss")
+        run("v", ["ls"], ["ov%d" % t], lambda q: q.tensor_scalar(
+            ov[:], T.ls[:, 15:NC:16], 5.0, 5.0 * half + 3.0, A.mult, A.add))
+        if t + 1 < R:
+            strength_tile(t + 1)
+        if t == 1:
+            run("v", ["zt"], ["qz"], lambda q: q.quantize_mx(T.qz[:], T.sz[:], T.zt[:]))
+
+        def plane_values(src, srcs, out, outs, kq, kc, ks, parts, copied, dst, kd):
+            keys = []
+            for a, z, engine in parts:
+                keys.append("%s_%d" % (kq, a))
+                run("v", kc + ["om"], [keys[-1]], lambda q: q.tensor_copy(
+                    out[:, 16 * a:16 * z].bitcast(u32), src[:, 0:130].bitcast(u32).indirect(T.om[:, a:z])))
+            for a, z, engine in parts:
+                keys.append("%ss_%d" % (kq, a))
+                if engine == "s":
+                    run("s", ks + ["om"], [keys[-1]], lambda q: q.activation(
+                        outs[:, 16 * a:16 * z], srcs[:, 0:130].indirect(T.om[:, a:z]), F.Copy))
+                else:
+                    run("v", ks + ["om"], [keys[-1]], lambda q: q.tensor_copy(
+                        outs[:, 16 * a:16 * z], srcs[:, 0:130].indirect(T.om[:, a:z])))
+            for b in (0, 2, 1, 3):
+                e, es = unit(0, b)
+                run("t", ["e0%d" % b] + keys, ["b%d" % b], lambda q: q.matmul_mx(
+                    bank(b, S), e, es, out[:], outs[:], True, True))
+            for b, engine in copied:
+                place = dst[:, S * b:S * b + S]
+                if engine == "s":
+                    run("s", ["b%d" % b], ["%s%d" % (kd, b)], lambda q: q.activation(place, bank(b, S), F.Copy))
+                else:
+                    run("v", ["b%d" % b], ["%s%d" % (kd, b)], lambda q: q.tensor_copy(place, bank(b, S)))
+
+        plane_values(la, las, T["qa%d" % t], T["qas%d" % t], "qa%d" % t, ["rep%d" % t, "pc%d" % t, "ra%d" % t],
+                     ["reps%d" % t, "ps%d" % t, "ra%d" % t], ((0, 10, "s"),),
+                     ((0, "v"), (2, "s"), (1, "v"), (3, "s")), T.va, "va")
+        if t == 0:
+            unit_tiles(2, "gm")
+        plane_values(lb, lbs, T["qm%d" % t], T["qms%d" % t], "qm%d" % t, ["mc%d" % t, "rb%d" % t],
+                     ["ms%d" % t, "rb%d" % t], ((0, 6, "s"), (6, 10, "v")), ((2, "s"), (3, "s")), T.vb, "vb")
         for b in range(4):
-            run("v", ["va%d0" % b, "va%d1" % b, "m8", "m8z"], ["vs%d" % b], lambda q: q.tensor_tensor_scan(
-                T.vs[:, b:1024:4], T.m8[:], T.va[:, 256 * b:256 * b + 256], 0.0, A.mult, A.add))
+            own = T.va[:, S * b:S * b + S]
+            far, key = (bank(b, S), "b%d" % b) if b < 2 else (T.vb[:, S * b:S * b + S], "vb%d" % b)
+            even, odd = (own, far) if mine == 0 else (far, own)
+            run("v", ["va%d" % b, key], ["vs%d" % b], lambda q: q.tensor_tensor_scan(
+                T.vs[:, b:4 * S:4], even, odd, 0.0, A.add, A.add))
         qv, qvs = T["qv%d" % t], T["qvs%d" % t]
         run("v", ["vs0", "vs1", "vs2", "vs3"], ["qv%d" % t], lambda q: q.quantize_mx(qv[:], qvs[:], T.vs[:]))
         vv, vvs = T["vv%d" % t], T["vvs%d" % t]
@@ -356,7 +382,7 @@ def rank_program(g, core, T, topo):
         dma("s", "dout", total, [kx], [], T.osc[4 * k:4 * k + 4, :], sx[32 * k:32 * k + 4, 0:NC])
     run("v", ["b0"], ["ysb"], lambda q: q.tensor_copy(T.ysb[:], bank(0, NC)))
     dma("y", "dout", total, ["ysb"], [], T.y[:], T.ysb[:])
-    wait("g", ("sent", R * (2 * len(topo.engines(core, peers[0])) + 4 * len(topo.engines(core, mate)))))
+    wait("g", ("sent", R * (2 * len(topo.engines(core, peers[0])) + 3 * len(topo.engines(core, mate)))))
     finish("g")
     wait("g", ("dlv", 16 * R))
     wait("g", ("dout", total))

@@ -4,29 +4,30 @@ from concourse.mybir import dt, AluOpType, ActivationFunctionType
 NC, L, R, PL = 192, 32, 3, 5
 W = NC + 2
 S = 5 * L
-P, FLOOR, NONE, DEEP, BIG = 2.0 ** 76, -2.0 ** 74, -2.0 ** 72, -2.0 ** 80, 2.0 ** 64
+P, FLOOR, PAD, BIG = 2.0 ** 76, -2.0 ** 74, -2.0 ** -5, 2.0 ** 61
 X4, BF, F32, U8, I32, U16 = "float8_e4m3fn_x4", "bfloat16", "float32", "uint8", "int32", "uint16"
+
+CALLS = (("c", ((1, 0), (0, 1), (1, 1)), (1,)), ("s", ((1, 0), (0, 1), (1, 1)), (0, 2)), ("c", ((0, 2), (0, 3)), ()))
+HELPERS = (("s", ((0, 2), (0, 3))), ("c", ((1, 2), (1, 3))), ("s", ((1, 2), (1, 3))))
 
 SCRATCH = {"pv": ("psum", [128, 2048], F32), "px": ("psum", [128, 2048], F32)}
 for _n, _w, _d in (
         ("wb", 576, BF), ("zt", 512, BF), ("qwb", 144, X4), ("swb", 144, U8), ("qz", 128, X4), ("sz", 128, U8),
-        ("gone", 520, BF), ("g1", 520, BF), ("g8", 520, BF), ("gm", 520, BF), ("ct", 520, BF),
-        ("qe", 12 * 128, X4), ("se", 12 * 128, U8), ("u", 256, BF), ("ut", 256, BF), ("gk", 1024, BF),
+        ("g0", 520, BF), ("g8", 520, BF), ("gm", 520, BF),
+        ("qe", 8 * 128, X4), ("se", 8 * 128, U8), ("u", 384, BF), ("ut", 384, BF), ("gk", 1536, BF),
         ("qc", 3 * 128, X4), ("sc", 3 * 128, U8), ("bq", 4 * W, BF), ("qb", W, X4), ("sb", W, U8),
-        ("m16", NC, BF), ("idg", NC, I32), ("idh", NC, I32), ("dg", NC, BF), ("neg", W, BF),
-        ("jb", 32, I32), ("jm", 32, I32), ("jp", 32, BF), ("ip", 10, I32), ("ja", 10, I32), ("jc", 10, I32),
-        ("jj", 10, I32), ("jf", 10, F32), ("jl", 10, I32), ("j5", 10, I32), ("jk", 10, I32), ("j3", 10, I32),
-        ("jr", 10, I32), ("jx", 10, I32), ("jy", 10, I32), ("jz", 10, I32), ("om", 10, U16),
+        ("m16", NC, BF), ("idg", NC, I32), ("idh", NC, I32), ("dg", NC, BF),
+        ("jb", 32, I32), ("jm", 32, I32), ("jp", 32, BF),
         ("rm0", W, F32), ("rm1", W, F32), ("sg0", NC, BF), ("sg1", NC, BF), ("ix", 4, F32),
         ("lt", NC, BF), ("ld", NC, BF), ("ls", NC, F32), ("lvs", R * NC, F32),
-        ("va", 4 * S, BF), ("vb", 4 * S, BF), ("vs", 4 * S, BF), ("ysb", NC, F32)):
+        ("va", 8 * S, BF), ("vs", 4 * S, BF), ("ysb", NC, F32)):
     SCRATCH[_n] = ("sbuf", [128, _w], _d)
 for _t in range(R + 1):
     SCRATCH["h%d" % _t] = ("sbuf", [128, 4 * W], BF)
     SCRATCH["qx%d" % _t] = ("sbuf", [128, W], X4)
     SCRATCH["sx%d" % _t] = ("sbuf", [128, W], U8)
 for _t in range(R):
-    for _n, _w in (("ws", 128), ("la", 256), ("lb", 256), ("qa", S), ("qm", S), ("qv", S), ("vv", NC)):
+    for _n, _w in (("ws", 128), ("la", 8 * L), ("hd", L), ("qv", S), ("vv", NC)):
         SCRATCH["%s%d" % (_n, _t)] = ("sbuf", [128, _w], X4)
         SCRATCH["%ss%d" % (_n, _t)] = ("sbuf", [128, _w], U8)
     SCRATCH["wl%d" % _t] = ("sbuf", [128, 8], U16)
@@ -34,7 +35,7 @@ for _t in range(R):
     SCRATCH["ov%d" % _t] = ("sbuf", [128, 12], U16)
 
 SEMAPHORES = ["cv", "cs", "ct", "cg", "dx", "dw", "dz", "dlv", "dout", "sent"]
-SEMAPHORES += ["%s%d" % (_n, _t) for _n in ("planec", "planes", "matec", "mates") for _t in range(R)]
+SEMAPHORES += ["%s%d" % (_n, _t) for _n in ("near", "late", "hand") for _t in range(R)]
 
 COUNTER = {"v": "cv", "s": "cs", "t": "ct", "g": "cg"}
 
@@ -101,28 +102,69 @@ def _scheduler(g, T):
     return run, dma, need, wait, arrive, finish
 
 
+def _places(T, topo, core):
+    cores = list(T.cores)
+    first = [c for c in cores if c == cores[0] or topo.same_plane(c, cores[0])]
+    planes = [first, [c for c in cores if c not in first]]
+    for a in range(2):
+        for i in range(4):
+            assert planes[a][i] == cores[2 * i + a]
+    mine = 0 if core in first else 1
+    able = [c for c in topo.cores_of(core) if c != core and all(topo.may_write(c, d) for d in cores)]
+    able.sort(key=lambda c: topo.die(c) != topo.die(core))
+    return planes, mine, planes[mine].index(core), able
+
+
+def _write(T, topo, core, t, kind, src, to, planes, mine, me):
+    ids, dsts = [], []
+    for a, k in to:
+        far = planes[(mine + a) % 2][(me + k) % 4]
+        rid, pid = topo.addr(far, core)
+        ids.append(DstId(rid=rid, pnc=pid))
+        o = L * (2 * k + mine)
+        dsts.append(T["la%d" % t][:, o:o + L].bitcast(dt.uint8) if kind == "c" else T["las%d" % t][:, o:o + L])
+    sem = T.sem[("near%d" if to[0][1] < 2 else "late%d") % t]
+    return RemoteDMATransfer(dst_ids=ids, dma_engine_mask=topo.mask(core, far), remote_sem=sem, srcs=[src], dsts=dsts)
+
+
+def _handed(T, t, kind):
+    return T["hd%d" % t][:].bitcast(dt.uint8) if kind == "c" else T["hds%d" % t][:]
+
+
+def _hand_on(g, core, T, topo):
+    ranks = [c for c in topo.cores_of(core) if T.rank_of(c) is not None]
+    if not ranks:
+        return
+    planes, mine, me, able = _places(T, topo, ranks[0])
+    if core not in able[:len(HELPERS)]:
+        return
+    kind, to = HELPERS[able.index(core)]
+    n_off = len(topo.engines(core, planes[1 - mine][me]))
+    for t in range(R):
+        g.wait_ge(T.sem["hand%d" % t], len(topo.engines(ranks[0], core)) - n_off)
+        g.remote_dma_fused([_write(T, topo, core, t, kind, _handed(T, t, kind), to, planes, mine, me)],
+                           local_sem=T.sem.sent)
+    g.wait_ge(T.sem.sent, R * n_off)
+
+
 def rank_program(g, core, T, topo):
-    rank = T.rank_of(core)
-    if rank is None:
+    if T.rank_of(core) is None:
+        _hand_on(g, core, T, topo)
         return
     A, F = AluOpType, ActivationFunctionType
     run, dma, need, wait, arrive, finish = _scheduler(g, T)
     u8, u32 = dt.uint8, dt.uint32
-
-    cores = list(T.cores)
-    first = [c for c in cores if c == cores[0] or topo.same_plane(c, cores[0])]
-    planes = [first, [c for c in cores if c not in first]]
-    mine = 0 if core in first else 1
-    me = planes[mine].index(core)
+    planes, mine, me, able = _places(T, topo, core)
     mate = planes[1 - mine][me]
-    assert topo.mates(core, mate)
-    for a in range(2):
-        for i in range(4):
-            assert planes[a][i] == cores[2 * i + a]
-    peers = [planes[mine][(me + k) % 4] for k in (1, 2, 3)]
+    on_chip = topo.mask(core, able[0]) & ~topo.mask(core, mate)
+    n_off = len(topo.engines(core, mate))
+    n_on = len(topo.engines(core, able[0])) - n_off
 
     def bank(b, n):
         return T.pv[:, 512 * b:512 * b + n]
+
+    def fill(key, out, n, value, after=(), a=0, z=128):
+        run("s", ["g0"] + list(after), [key], lambda q: q.activation(out, T.g0[a:z, 0:n], F.Copy, scale=8.0 * value))
 
     dma("s", "dw", 16, [], ["wb"], T.wb[:, 0:128], T.w[:, 0:128])
     dma("y", "dx", 16, [], ["h0"], T.h0[:, 0:4 * NC], T.x[:])
@@ -133,14 +175,15 @@ def rank_program(g, core, T, topo):
         return T.qc[:, 128 * k:128 * k + 128], T.sc[:, 128 * k:128 * k + 128]
 
     us = ["u%d" % i for i in range(PL + 1)]
-    run("v", [], ["gkz"], lambda q: q.memset(T.gk[:], 0.0))
+    run("v", [], ["g0"], lambda q: q.memset(T.g0[:], 0.125))
     run("v", [], ["u"], lambda q: q.memset(T.u[0:32, :], 0.0))
-    run("s", ["gkz"], ["gone"], lambda q: q.activation(T.gone[:], T.gk[:, 0:520], F.Identity, bias=1.0))
-    run("g", ["gone"], ["g1"], lambda q: q.affine_select(T.g1[:], T.gone[:], [[-1, 520]], A.is_equal, 0.0, 4, 4))
-    run("s", ["gone"], ["bqa"], lambda q: q.activation(T.bq[:, 0:512], T.gone[:, 0:512], F.Copy))
-    run("s", ["gone"], ["bqc"], lambda q: q.activation(T.bq[:, 512:4 * NC], T.gone[:, 0:4 * NC - 512], F.Copy))
-    run("s", ["gone"], ["bqp"], lambda q: q.activation(
-        T.bq[:, 4 * NC:4 * W], T.gone[:, 0:4 * W - 4 * NC], F.Copy, scale=2.0))
+    run("v", [], ["gka"], lambda q: q.memset(T.gk[:, 0:512], 0.0))
+    run("g", ["g0"], ["g8"], lambda q: q.affine_select(T.g8[:], T.g0[:], [[-1, 520]], A.is_equal, 0.0, 4, 4))
+    fill("gkb", T.gk[:, 512:1024], 512, 0.0)
+    fill("wbz", T.wb[:, 128:576], 448, 0.0)
+    fill("hp0", T.h0[:, 4 * NC:4 * W], 4 * W - 4 * NC, 0.0)
+    fill("bqa", T.bq[:, 0:512], 512, 0.0)
+    fill("bqc", T.bq[:, 512:4 * W], 4 * W - 512, 0.0)
     run("v", ["jb%d" % i for i in range(PL - 1)], ["jm"], lambda q: q.tensor_scalar(
         T.jm[0:32, :], T.jb[0:32, :], 8, None, A.bitwise_and))
     run("v", ["u"], ["u4"], lambda q: q.memset(T.u[0:32, 4:128:32], -P))
@@ -149,21 +192,14 @@ def rank_program(g, core, T, topo):
     run("v", ["u"], ["u5"], lambda q: q.memset(T.u[0:32, 132:256:32], P))
     for i in range(PL - 1):
         run("v", ["jp", "u"], ["u%d" % i], lambda q: q.tensor_copy(T.u[0:32, i:256:32], T.jp[0:32, 8 * i:8 * i + 8]))
-    run("v", ["gkz", "gone"], ["gk1"], lambda q: q.memset(T.gk[:, 1:1024:4], -P * PL / 2 / 128))
-    run("v", ["u"] + us, ["ut"], lambda q: q.transpose(T.ut[0:32, :], T.u[0:32, :]))
-    run("v", [], ["wbz"], lambda q: q.memset(T.wb[:, 128:576], 0.0))
-    run("v", ["ut", "gkz", "gone"], ["gk0"], lambda q: q.tensor_copy(T.gk[0:32, 0:1024:4], T.ut[0:32, :]))
     run("v", [], ["wl0"], lambda q: q.memset(T.wl0[:], 6))
-    run("v", [], ["hp0"], lambda q: q.memset(T.h0[:, 4 * NC:4 * W], 0.0))
-    run("v", ["gk0", "gk1", "gkz"], ["qc0", "qc1"], lambda q: q.quantize_mx(T.qc[:, 0:256], T.sc[:, 0:256], T.gk[:]))
+    run("v", ["u"] + us, ["ut"], lambda q: q.transpose(T.ut[0:32, 0:256], T.u[0:32, 0:256]))
+    run("v", ["gka", "gkb"], ["gk1"], lambda q: q.memset(T.gk[64:128, 0:1024:4], P * PL / 64))
+    run("v", ["ut", "gka", "gkb"], ["gk0"], lambda q: q.tensor_copy(T.gk[0:32, 0:1024:4], T.ut[0:32, 0:256]))
     run("v", ["wb", "wbz"], ["qwb"], lambda q: q.quantize_mx(T.qwb[:], T.swb[:], T.wb[:]))
-    run("v", ["h0", "hp0"], ["qx0"], lambda q: q.quantize_mx(T.qx0[:], T.sx0[:], T.h0[:]))
-    dma("y", "dz", 16, ["qx0"], ["zt"], T.zt[:], T.z[:])
-    run("g", [], ["ip"], lambda q: q.iota(T.ip[:], [[0, 10]], 0, 1))
-    run("g", [], ["ja"], lambda q: q.iota(T.ja[:], [[16, 10]], 0, 0))
-    run("g", [], ["idg"], lambda q: q.iota(T.idg[:], [[1, NC]], 128, -1))
-    run("s", ["gone"], ["neg"], lambda q: q.activation(T.neg[:, 0:NC], T.gone[:, 0:NC], F.Copy, scale=DEEP))
-    run("s", ["gone"], ["negp"], lambda q: q.activation(T.neg[:, NC:W], T.gone[:, 0:W - NC], F.Copy, scale=NONE))
+    run("v", ["gk0", "gk1", "gka", "gkb"], ["qc0", "qc1"], lambda q: q.quantize_mx(
+        T.qc[:, 0:256], T.sc[:, 0:256], T.gk[:, 0:1024]))
+    fill("bqp", T.bq[64:128, 4 * NC:4 * W:4], W - NC, PAD, ["bqc"], 64, 128)
 
     def strength_tile(t):
         ws, wss, wl = T["ws%d" % t], T["wss%d" % t], T["wl%d" % t]
@@ -171,6 +207,14 @@ def rank_program(g, core, T, topo):
             wss[:], T.swb[:].indirect(wl[:]), F.Copy))
         run("v", ["qwb", "wl%d" % t], ["ws%d" % t], lambda q: q.tensor_copy(
             ws[:].bitcast(u32), T.qwb[:].bitcast(u32).indirect(wl[:])))
+
+    strength_tile(0)
+    run("v", ["h0", "hp0"], ["qx0"], lambda q: q.quantize_mx(T.qx0[:], T.sx0[:], T.h0[:]))
+    dma("y", "dz", 16, ["qx0"], ["zt"], T.zt[:], T.z[:])
+    run("g", [], ["idg"], lambda q: q.iota(T.idg[:], [[1, NC]], 128, -1))
+    ns = ["n%d" % i for i in range(PL)]
+    for i in range(PL):
+        fill(ns[i], T.u[0:32, 256 + i:384:32], 4, 2.0 ** i, ["u"], 0, 32)
 
     def unit_tiles(s, name, which=(0, 1, 2, 3)):
         src = T[name]
@@ -184,123 +228,87 @@ def rank_program(g, core, T, topo):
         return T.qe[:, o:o + 128], T.se[:, o:o + 128]
 
     def first_constants():
-        run("v", ["ip"], ["jc"], lambda q: q.tensor_scalar(T.jc[:], T.ip[:], 15, None, A.bitwise_and))
-        run("v", [], ["u"], lambda q: q.memset(T.u[0:32, 0:128], 0.0))
-        run("v", ["jc", "ja"], ["jj"], lambda q: q.tensor_tensor(T.jj[:], T.ja[:], T.jc[:], A.add))
-        run("v", ["gkz"], ["gk1"], lambda q: q.memset(T.gk[:, 1:512:4], 0.0))
-        for i in range(PL):
-            run("s", ["u", "gone"], ["u%d" % i], lambda q: q.activation(
-                T.u[0:32, i:128:32], T.gone[0:32, 0:4], F.Copy, scale=2.0 ** i))
-        run("s", ["g1"], ["g8"], lambda q: q.activation(T.g8[:], T.g1[:], F.Copy, scale=0.125))
-        run("s", ["gone"], ["m16"], lambda q: q.activation(T.m16[:], T.gone[:, 0:NC], F.Copy))
-        run("s", ["g1"], ["gm"], lambda q: q.activation(T.gm[:], T.g1[:], F.Copy, scale=-0.5))
-        run("s", ["gone", "m16"], ["m16z"], lambda q: q.activation(
-            T.m16[:, 0:NC:16], T.gone[:, 0:12], F.Copy, scale=0.0))
-        run("v", ["jj"], ["jf"], lambda q: q.tensor_scalar(T.jf[:], T.jj[:], -2.0, 0.2, A.add, A.mult))
+        fill("gkc", T.gk[:, 1024:1536], 512, 0.0)
+        run("s", ["g8"], ["gm"], lambda q: q.activation(T.gm[:], T.g8[:], F.Copy, scale=-0.5))
+        fill("m16", T.m16[:], NC, 1.0)
+        fill("m16z", T.m16[:, 0:NC:16], NC // 16, 0.0, ["m16"])
         run("v", ["idg"], ["idh"], lambda q: q.tensor_scalar(T.idh[:], T.idg[:], 15, None, A.bitwise_and))
-        run("v", ["jf"], ["jl"], lambda q: q.tensor_copy(T.jl[:], T.jf[:]))
+        run("v", ["u"] + ns, ["un"], lambda q: q.transpose(T.ut[0:32, 256:384], T.u[0:32, 256:384]))
         run("v", ["idh"], ["dg"], lambda q: q.tensor_scalar(T.dg[:], T.idh[:], 0.0, None, A.is_equal))
-        run("v", ["jl"], ["j5"], lambda q: q.tensor_scalar(T.j5[:], T.jl[:], -5.0, 4.0 - me, A.mult, A.add))
-        run("v", ["u"] + us, ["ut"], lambda q: q.transpose(T.ut[0:32, 0:128], T.u[0:32, 0:128]))
-        run("v", ["j5", "jj"], ["jk"], lambda q: q.tensor_tensor(T.jk[:], T.j5[:], T.jj[:], A.add))
-        run("v", ["ut", "gkz"], ["gk0"], lambda q: q.tensor_copy(T.gk[0:32, 0:512:4], T.ut[0:32, 0:128]))
-        run("v", ["jk"], ["j3"], lambda q: q.tensor_scalar(T.j3[:], T.jk[:], 3, None, A.bitwise_and))
-        run("v", ["jk"], ["jr"], lambda q: q.tensor_scalar(T.jr[:], T.jk[:], 8.0 - me, 4.0 * L, A.is_ge, A.mult))
-        run("v", ["j3"], ["jx"], lambda q: q.tensor_scalar(T.jx[:], T.j3[:], 1.0 * L, None, A.mult))
-        run("v", ["gk0", "gk1", "gkz"], ["qc2"], lambda q: q.quantize_mx(
-            T.qc[:, 256:384], T.sc[:, 256:384], T.gk[:, 0:512]))
-        run("v", ["jx", "jl"], ["jy"], lambda q: q.tensor_tensor(T.jy[:], T.jx[:], T.jl[:], A.add))
-        restart_column(T.la0, T.las0, "ra0", mine)
-        run("v", ["jy", "jr"], ["jz"], lambda q: q.tensor_tensor(T.jz[:], T.jy[:], T.jr[:], A.max))
-        restart_column(T.lb0, T.lbs0, "rb0", 1 - mine)
-        run("v", ["jz"], ["om"], lambda q: q.tensor_copy(T.om[:], T.jz[:]))
-        unit_tiles(0, "g8")
-
-    def restart_column(codes, scales, key, a):
-        run("v", ["ct", "ctm"], [key], lambda q: q.quantize_mx(
-            codes[:, 128:256], scales[:, 128:256], T.ct[:, 4 * a:4 * a + 512]))
+        run("v", ["un", "gkc"], ["gk2"], lambda q: q.tensor_copy(T.gk[0:32, 1024:1536:4], T.ut[0:32, 256:384]))
+        run("v", [], ["up"], lambda q: q.memset(T.va[:, 4:8 * S:5], BIG))
+        run("v", ["gk2", "gkc"], ["qc2"], lambda q: q.quantize_mx(
+            T.qc[:, 256:384], T.sc[:, 256:384], T.gk[:, 1024:1536]))
+        for b in range(4):
+            run("v", ["up"], ["down%d" % b], lambda q: q.memset(T.va[:, 2 * S * b + S + 4:2 * S * b + 2 * S:5], -BIG))
+        unit_tiles(1, "gm")
 
     half = (2 ** PL - 1) / 2
+    sent = 0
     for t in range(R):
         qx, sx = T["qx%d" % t], T["sx%d" % t]
         kx = "qx%d" % t
-        la, las, lb, lbs = T["la%d" % t], T["las%d" % t], T["lb%d" % t], T["lbs%d" % t]
+        la, las = T["la%d" % t], T["las%d" % t]
         run("t", ["qwb", kx], ["b0"], lambda q: q.matmul_mx(
-            bank(0, W), T.qwb[:, 8 * t:8 * t + 128], T.swb[:, 8 * t:8 * t + 128], qx[:], sx[:], True, True))
-        if t == 0:
-            strength_tile(0)
-            run("s", ["gone"], ["ctm"], lambda q: q.activation(T.ct[:], T.gone[:], F.Copy, scale=-BIG))
-            run("s", ["gone", "ctm"], ["ct"], lambda q: q.activation(T.ct[:, 0:4], T.gone[:, 0:4], F.Copy, scale=BIG))
+            bank(0, NC), T.qwb[:, 8 * t:8 * t + 128], T.swb[:, 8 * t:8 * t + 128], qx[:, 0:NC], sx[:, 0:NC], True, True))
         for c in range(2):
             run("t", ["ws%d" % t, "wss%d" % t, kx], ["b%d" % (1 + c)], lambda q: q.matmul_mx(
                 bank(1 + c, W), T["ws%d" % t][:], T["wss%d" % t][:], qx[:], sx[:], True, False))
-        run("v", ["b0", "bqa", "bqc", "bqp"], ["bq"], lambda q: q.tensor_scalar(
-            T.bq[:, 0:4 * W:4], bank(0, W), 0.0, 0.5, A.is_lt, A.subtract))
-        run("v", ["bq"], ["qb"], lambda q: q.quantize_mx(T.qb[:], T.sb[:], T.bq[:]))
         if t == 0:
-            unit_tiles(1, "g1", (0, 1))
+            unit_tiles(0, "g8", (0,))
+        run("v", ["b0", "bqa", "bqc"], ["bq"], lambda q: q.tensor_scalar(
+            T.bq[:, 0:4 * NC:4], bank(0, NC), 0.0, 0.5, A.is_lt, A.subtract))
+        run("v", ["bq", "bqp"], ["qb"], lambda q: q.quantize_mx(T.qb[:], T.sb[:], T.bq[:]))
+        if t == 0:
+            unit_tiles(0, "g8", (1,))
         for c in range(2):
             e, es = const(c)
             run("t", ["qc%d" % c, "qb"], ["b%d" % (1 + c)], lambda q: q.matmul_mx(
                 bank(1 + c, W), e, es, T.qb[:], T.sb[:], False, True))
         for c in range(2):
             rm, sg = T["rm%d" % c], T["sg%d" % c]
-            run("v", ["b%d" % (1 + c), "neg", "negp"], ["rm%d" % c], lambda q: q.tensor_tensor_scan(
-                rm[:], bank(1 + c, W), T.neg[:], FLOOR, A.max, A.max))
+            run("v", ["b%d" % (1 + c), "wbz"], ["rm%d" % c], lambda q: q.tensor_tensor_scan(
+                rm[:], bank(1 + c, W), T.wb[:, 128:128 + W], FLOOR, A.max, A.add))
             run("s", ["rm%d" % c], ["sg%d" % c, "ix%d" % c], lambda q: q.activation(
                 sg[:], rm[:, 0:NC], F.Sign, bias=rm[:, NC:NC + 1], scale=-1.0, accum_out=T.ix[:, c:c + 1]))
         if t == 0:
-            unit_tiles(1, "g1", (2, 3))
+            unit_tiles(0, "g8", (2, 3))
         of = T["of%d" % t]
         run("v", ["ix0", "ix1"], ["of%d" % t], lambda q: q.tensor_copy(of[:], T.ix[:, 0:2]))
-        run("s", [kx, "of%d" % t], ["reps%d" % t], lambda q: q.activation(
-            las[:, 0:L], sx[:].indirect(of[:]), F.Copy))
+        rep, reps = la[:, L * mine:L * mine + L], las[:, L * mine:L * mine + L]
+        run("s", [kx, "of%d" % t], ["reps%d" % t], lambda q: q.activation(reps, sx[:].indirect(of[:]), F.Copy))
         run("v", [kx, "of%d" % t], ["rep%d" % t], lambda q: q.tensor_copy(
-            la[:, 0:L].bitcast(u32), qx[:].bitcast(u32).indirect(of[:])))
-        ids, slot = [], []
-        for c in peers:
-            rid, pid = topo.addr(c, core)
-            ids.append(DstId(rid=rid, pnc=pid))
-            slot.append(L * ((me - planes[mine].index(c)) % 4))
-        mask = topo.mask(core, peers[0])
-        need("g", ["rep%d" % t], [])
-        g.remote_dma_fused([RemoteDMATransfer(
-            dst_ids=ids, dma_engine_mask=mask, remote_sem=T.sem["planec%d" % t], srcs=[la[:, 0:L].bitcast(u8)],
-            dsts=[la[:, o:o + L].bitcast(u8) for o in slot])], local_sem=T.sem.sent)
-        need("g", ["reps%d" % t], [])
-        g.remote_dma_fused([RemoteDMATransfer(
-            dst_ids=ids, dma_engine_mask=mask, remote_sem=T.sem["planes%d" % t], srcs=[las[:, 0:L]],
-            dsts=[las[:, o:o + L] for o in slot])], local_sem=T.sem.sent)
-        n = len(topo.engines(core, peers[0])) * len(peers)
-        arrive(("planec%d" % t, n), ["pc%d" % t])
-        arrive(("planes%d" % t, n), ["ps%d" % t])
-        rid, pid = topo.addr(mate, core)
-        mask = topo.mask(core, mate)
-        mc, ms = T.sem["matec%d" % t], T.sem["mates%d" % t]
-        g.remote_dma(lb[:, 0:L].bitcast(u8), la[:, 0:L].bitcast(u8), mc, T.sem.sent, pid, rid, mask)
-        need("g", ["pc%d" % t], [])
-        g.remote_dma(lb[:, L:4 * L].bitcast(u8), la[:, L:4 * L].bitcast(u8), mc, T.sem.sent, pid, rid, mask)
-        need("g", ["ps%d" % t], [])
-        g.remote_dma(lbs[:, 0:4 * L], las[:, 0:4 * L], ms, T.sem.sent, pid, rid, mask)
-        n = len(topo.engines(core, mate))
-        arrive(("matec%d" % t, 2 * n), ["mc%d" % t])
-        arrive(("mates%d" % t, n), ["ms%d" % t])
+            rep.bitcast(u32), qx[:].bitcast(u32).indirect(of[:])))
+        for kind, to, helpers in CALLS:
+            need("g", [("rep%d" if kind == "c" else "reps%d") % t], [])
+            src = rep.bitcast(u8) if kind == "c" else reps
+            transfers = [_write(T, topo, core, t, kind, src, to, planes, mine, me)]
+            sent += n_off
+            if helpers:
+                ids = []
+                for h in helpers:
+                    rid, pid = topo.addr(able[h], core)
+                    ids.append(DstId(rid=rid, pnc=pid))
+                transfers.append(RemoteDMATransfer(
+                    dst_ids=ids, dma_engine_mask=on_chip, remote_sem=T.sem["hand%d" % t], srcs=[src],
+                    dsts=[_handed(T, t, kind)] * len(ids)))
+                sent += n_on
+            g.remote_dma_fused(transfers, local_sem=T.sem.sent)
+        arrive(("near%d" % t, 2 * 3 * n_off), ["near%d" % t])
+        arrive(("late%d" % t, 2 * 4 * n_off), ["late%d" % t])
+        for b in range(4):
+            e, es = unit(0, b)
+            run("t", ["e0%d" % b, kx], ["px%d" % b], lambda q: q.matmul_mx(
+                T.px[:, 512 * b:512 * b + NC], e, es, qx[:, 0:NC], sx[:, 0:NC], True, False))
         if t == 0:
             first_constants()
-        else:
-            restart_column(la, las, "ra%d" % t, mine)
-            restart_column(lb, lbs, "rb%d" % t, 1 - mine)
         e, es = const(2)
         run("t", ["qc2", "qb"], ["b3"], lambda q: q.matmul_mx(
             bank(3, NC), e, es, T.qb[:, 0:NC], T.sb[:, 0:NC], True, True))
-        for b in range(4):
-            e, es = unit(1, b)
-            run("t", ["e1%d" % b, kx], ["px%d" % b], lambda q: q.matmul_mx(
-                T.px[:, 512 * b:512 * b + NC], e, es, qx[:, 0:NC], sx[:, 0:NC], True, False))
         run("s", ["b3"], ["lt"], lambda q: q.activation(T.lt[:], bank(3, NC), F.Copy))
         run("s", ["b3"], ["lvs%d" % t], lambda q: q.activation(
             T.lvs[0:1, NC * t:NC * t + NC], T.pv[0:1, 3 * 512:3 * 512 + NC], F.Identity, bias=half))
-        dma("y", "dlv", 16 * (t + 1), ["lvs%d" % t], [], T.lv[t:t + 1, :], T.lvs[0:1, NC * t:NC * t + NC])
+        dma("y", "dlv", 16 * (t + 1), ["lvs%d" % t, "late%d" % t], [], T.lv[t:t + 1, :], T.lvs[0:1, NC * t:NC * t + NC])
         ov, hn = T["ov%d" % t], T["h%d" % (t + 1)]
         run("v", ["lt", "dg"], ["ld"], lambda q: q.tensor_tensor(T.ld[:], T.lt[:], T.dg[:], A.mult))
         if t + 1 < R:
@@ -315,44 +323,28 @@ def rank_program(g, core, T, topo):
         if t == 1:
             run("v", ["zt"], ["qz"], lambda q: q.quantize_mx(T.qz[:], T.sz[:], T.zt[:]))
 
-        def plane_values(src, srcs, out, outs, kq, kc, ks, parts, copied, dst, kd):
-            keys = []
-            for a, z, engine in parts:
-                keys.append("%s_%d" % (kq, a))
-                run("v", kc + ["om"], [keys[-1]], lambda q: q.tensor_copy(
-                    out[:, 16 * a:16 * z].bitcast(u32), src[:, 0:130].bitcast(u32).indirect(T.om[:, a:z])))
-            for a, z, engine in parts:
-                keys.append("%ss_%d" % (kq, a))
-                if engine == "s":
-                    run("s", ks + ["om"], [keys[-1]], lambda q: q.activation(
-                        outs[:, 16 * a:16 * z], srcs[:, 0:130].indirect(T.om[:, a:z]), F.Copy))
-                else:
-                    run("v", ks + ["om"], [keys[-1]], lambda q: q.tensor_copy(
-                        outs[:, 16 * a:16 * z], srcs[:, 0:130].indirect(T.om[:, a:z])))
-            for b in (0, 2, 1, 3):
+        def unpack(first, keys, order):
+            o = 2 * L * first
+            for b, engine in order:
                 e, es = unit(0, b)
                 run("t", ["e0%d" % b] + keys, ["b%d" % b], lambda q: q.matmul_mx(
-                    bank(b, S), e, es, out[:], outs[:], True, True))
-            for b, engine in copied:
-                place = dst[:, S * b:S * b + S]
-                if engine == "s":
-                    run("s", ["b%d" % b], ["%s%d" % (kd, b)], lambda q: q.activation(place, bank(b, S), F.Copy))
-                else:
-                    run("v", ["b%d" % b], ["%s%d" % (kd, b)], lambda q: q.tensor_copy(place, bank(b, S)))
+                    bank(b, 4 * L), e, es, la[:, o:o + 4 * L], las[:, o:o + 4 * L], True, True))
+            for b, engine in order:
+                for j in range(2):
+                    i, c = (me - first - j) % 4, 512 * b + 2 * L * j
+                    out, in_ = T.va[:, 2 * S * b + i:2 * S * b + 2 * S:5], T.pv[:, c:c + 2 * L]
+                    if engine == "s":
+                        run("s", ["b%d" % b], ["va%d%d" % (b, i)], lambda q: q.activation(out, in_, F.Copy))
+                    else:
+                        run("v", ["b%d" % b], ["va%d%d" % (b, i)], lambda q: q.tensor_copy(out, in_))
 
-        plane_values(la, las, T["qa%d" % t], T["qas%d" % t], "qa%d" % t, ["rep%d" % t, "pc%d" % t, "ra%d" % t],
-                     ["reps%d" % t, "ps%d" % t, "ra%d" % t], ((0, 10, "s"),),
-                     ((0, "v"), (2, "s"), (1, "v"), (3, "s")), T.va, "va")
-        if t == 0:
-            unit_tiles(2, "gm")
-        plane_values(lb, lbs, T["qm%d" % t], T["qms%d" % t], "qm%d" % t, ["mc%d" % t, "rb%d" % t],
-                     ["ms%d" % t, "rb%d" % t], ((0, 6, "s"), (6, 10, "v")), ((2, "s"), (3, "s")), T.vb, "vb")
-        for b in range(4):
-            own = T.va[:, S * b:S * b + S]
-            far, key = (bank(b, S), "b%d" % b) if b < 2 else (T.vb[:, S * b:S * b + S], "vb%d" % b)
-            even, odd = (own, far) if mine == 0 else (far, own)
-            run("v", ["va%d" % b, key], ["vs%d" % b], lambda q: q.tensor_tensor_scan(
-                T.vs[:, b:4 * S:4], even, odd, 0.0, A.add, A.add))
+        unpack(0, ["rep%d" % t, "reps%d" % t, "near%d" % t], ((0, "v"), (2, "s"), (1, "v"), (3, "s")))
+        unpack(2, ["late%d" % t], ((1, "v"), (0, "s"), (3, "v"), (2, "s")))
+        for b in (1, 0, 3, 2):
+            o = 2 * S * b
+            run("v", ["up", "down%d" % b] + ["va%d%d" % (b, i) for i in range(4)], ["vs%d" % b],
+                lambda q: q.tensor_tensor_scan(
+                    T.vs[:, b:4 * S:4], T.va[:, o:o + S], T.va[:, o + S:o + 2 * S], 0.0, A.add, A.add))
         qv, qvs = T["qv%d" % t], T["qvs%d" % t]
         run("v", ["vs0", "vs1", "vs2", "vs3"], ["qv%d" % t], lambda q: q.quantize_mx(qv[:], qvs[:], T.vs[:]))
         vv, vvs = T["vv%d" % t], T["vvs%d" % t]
@@ -360,15 +352,15 @@ def rank_program(g, core, T, topo):
         run("v", ["qv%d" % t, "ov%d" % t], ["vv%d" % t], lambda q: q.tensor_copy(
             vv[:].bitcast(u32), qv[:].bitcast(u32).indirect(ov[:])))
         for b in range(4):
-            e, es = unit(2, b)
-            run("t", ["e2%d" % b, "vv%d" % t, "vvs%d" % t], ["px%d" % b], lambda q: q.matmul_mx(
+            e, es = unit(1, b)
+            run("t", ["e1%d" % b, "vv%d" % t, "vvs%d" % t], ["px%d" % b], lambda q: q.matmul_mx(
                 T.px[:, 512 * b:512 * b + NC], e, es, vv[:], vvs[:], False, True))
         for b in range(4):
             out, in_ = hn[:, b:4 * NC:4], T.px[:, 512 * b:512 * b + NC]
             if b % 2 == 0:
-                run("s", ["px%d" % b], ["h%d%d" % (t + 1, b)], lambda q: q.activation(out, in_, F.Copy))
+                run("s", ["px%d" % b], ["h%d%d" % (t + 1, b)], lambda q: q.activation(out, in_, F.Copy, scale=8.0))
             else:
-                run("v", ["px%d" % b], ["h%d%d" % (t + 1, b)], lambda q: q.tensor_copy(out, in_))
+                run("v", ["px%d" % b], ["h%d%d" % (t + 1, b)], lambda q: q.tensor_scalar(out, in_, 8.0, None, A.mult))
         run("v", ["h%d%d" % (t + 1, b) for b in range(4)] + ["hp%d" % (t + 1)], ["qx%d" % (t + 1)],
             lambda q: q.quantize_mx(T["qx%d" % (t + 1)][:], T["sx%d" % (t + 1)][:], hn[:]))
 
@@ -382,7 +374,7 @@ def rank_program(g, core, T, topo):
         dma("s", "dout", total, [kx], [], T.osc[4 * k:4 * k + 4, :], sx[32 * k:32 * k + 4, 0:NC])
     run("v", ["b0"], ["ysb"], lambda q: q.tensor_copy(T.ysb[:], bank(0, NC)))
     dma("y", "dout", total, ["ysb"], [], T.y[:], T.ysb[:])
-    wait("g", ("sent", R * (2 * len(topo.engines(core, peers[0])) + 3 * len(topo.engines(core, mate)))))
+    wait("g", ("sent", sent))
     finish("g")
     wait("g", ("dlv", 16 * R))
     wait("g", ("dout", total))

@@ -2,23 +2,25 @@ from concourse.bass import DstId, RemoteDMATransfer
 from concourse.mybir import dt, AluOpType, ActivationFunctionType
 
 NC, L, R, PL = 192, 32, 3, 5
-W = NC + 2
+W = 256
+H = NC - 128
 S = 5 * L
-P, FLOOR, PAD, BIG = 2.0 ** 76, -2.0 ** 74, -2.0 ** -5, 2.0 ** 61
+P, FLOOR, PAD, BIG, TINY = 2.0 ** 76, -2.0 ** 74, -2.0 ** -5, 2.0 ** 61, 2.0 ** -120
 X4, BF, F32, U8, I32, U16 = "float8_e4m3fn_x4", "bfloat16", "float32", "uint8", "int32", "uint16"
 
-CALLS = (("c", ((1, 0), (0, 1), (1, 1)), (1,)), ("s", ((1, 0), (0, 1), (1, 1)), (0, 2)), ("c", ((0, 2), (0, 3)), ()))
-HELPERS = (("s", ((0, 2), (0, 3))), ("c", ((1, 2), (1, 3))), ("s", ((1, 2), (1, 3))))
+NEAR = ((1, 0), (0, 1), (1, 1))
+CALLS = (("c", (), (1, 3)), ("s", NEAR, (0, 2)), ("c", NEAR, ()), ("s", ((0, 3),), ()))
+HELPERS = (("s", ((0, 2), (1, 2))), ("c", ((1, 2), (1, 3))), ("s", ((1, 3),)), ("c", ((0, 2), (0, 3))))
 
 SCRATCH = {"pv": ("psum", [128, 2048], F32), "px": ("psum", [128, 2048], F32)}
 for _n, _w, _d in (
         ("wb", 576, BF), ("zt", 512, BF), ("qwb", 144, X4), ("swb", 144, U8), ("qz", 128, X4), ("sz", 128, U8),
         ("g0", 520, BF), ("g8", 520, BF), ("gm", 520, BF),
-        ("qe", 8 * 128, X4), ("se", 8 * 128, U8), ("u", 384, BF), ("ut", 384, BF), ("gk", 1536, BF),
-        ("qc", 3 * 128, X4), ("sc", 3 * 128, U8), ("bq", 4 * W, BF), ("qb", W, X4), ("sb", W, U8),
+        ("qe", 8 * 128, X4), ("se", 8 * 128, U8), ("u", 256, BF), ("ut", 256, BF), ("gk", 1024, BF),
+        ("qc", 256, X4), ("sc", 256, U8), ("bq", 4 * W, BF), ("qb", W, X4), ("sb", W, U8),
         ("m16", NC, BF), ("idg", NC, I32), ("idh", NC, I32), ("dg", NC, BF),
-        ("jb", 32, I32), ("jm", 32, I32), ("jp", 32, BF),
-        ("rm0", W, F32), ("rm1", W, F32), ("sg0", NC, BF), ("sg1", NC, BF), ("ix", 4, F32),
+        ("jb", 16, I32), ("jm", 16, I32), ("jp", 16, BF), ("tiny", 1, F32),
+        ("rm", NC + 2, F32), ("sg", NC, BF), ("ix", 4, F32),
         ("lt", NC, BF), ("ld", NC, BF), ("ls", NC, F32), ("lvs", R * NC, F32),
         ("va", 8 * S, BF), ("vs", 4 * S, BF), ("ysb", NC, F32)):
     SCRATCH[_n] = ("sbuf", [128, _w], _d)
@@ -34,7 +36,7 @@ for _t in range(R):
     SCRATCH["of%d" % _t] = ("sbuf", [128, 2], U16)
     SCRATCH["ov%d" % _t] = ("sbuf", [128, 12], U16)
 
-SEMAPHORES = ["cv", "cs", "ct", "cg", "dx", "dw", "dz", "dlv", "dout", "sent"]
+SEMAPHORES = ["cv", "cs", "ct", "cg", "dx0", "dx1", "dw", "dz", "dlv", "dout", "sent"]
 SEMAPHORES += ["%s%d" % (_n, _t) for _n in ("near", "late", "hand") for _t in range(R)]
 
 COUNTER = {"v": "cv", "s": "cs", "t": "ct", "g": "cg"}
@@ -112,7 +114,8 @@ def _places(T, topo, core):
     mine = 0 if core in first else 1
     able = [c for c in topo.cores_of(core) if c != core and all(topo.may_write(c, d) for d in cores)]
     able.sort(key=lambda c: topo.die(c) != topo.die(core))
-    return planes, mine, planes[mine].index(core), able
+    able += [c for c in topo.cores_of(core) if c != core and c not in able and topo.die(c) == topo.die(core)]
+    return planes, mine, planes[mine].index(core), able[:len(HELPERS)]
 
 
 def _write(T, topo, core, t, kind, src, to, planes, mine, me):
@@ -131,20 +134,28 @@ def _handed(T, t, kind):
     return T["hd%d" % t][:].bitcast(dt.uint8) if kind == "c" else T["hds%d" % t][:]
 
 
+def _hand_over(topo, core, helper, far, t, alone):
+    if alone and t > 0:
+        return topo.mask(core, helper), len(topo.engines(core, helper))
+    return (topo.mask(core, helper) & ~topo.mask(core, far),
+            len(topo.engines(core, helper)) - len(topo.engines(core, far)))
+
+
 def _hand_on(g, core, T, topo):
     ranks = [c for c in topo.cores_of(core) if T.rank_of(c) is not None]
     if not ranks:
         return
     planes, mine, me, able = _places(T, topo, ranks[0])
-    if core not in able[:len(HELPERS)]:
+    if core not in able:
         return
     kind, to = HELPERS[able.index(core)]
-    n_off = len(topo.engines(core, planes[1 - mine][me]))
+    far = planes[mine][(me + 1) % 4]
+    alone = [not call[1] for call in CALLS if able.index(core) in call[2]][0]
     for t in range(R):
-        g.wait_ge(T.sem["hand%d" % t], len(topo.engines(ranks[0], core)) - n_off)
+        g.wait_ge(T.sem["hand%d" % t], _hand_over(topo, ranks[0], core, far, t, alone)[1])
         g.remote_dma_fused([_write(T, topo, core, t, kind, _handed(T, t, kind), to, planes, mine, me)],
                            local_sem=T.sem.sent)
-    g.wait_ge(T.sem.sent, R * n_off)
+    g.wait_ge(T.sem.sent, R * len(topo.engines(core, far)))
 
 
 def rank_program(g, core, T, topo):
@@ -156,20 +167,19 @@ def rank_program(g, core, T, topo):
     u8, u32 = dt.uint8, dt.uint32
     planes, mine, me, able = _places(T, topo, core)
     mate = planes[1 - mine][me]
-    on_chip = topo.mask(core, able[0]) & ~topo.mask(core, mate)
     n_off = len(topo.engines(core, mate))
-    n_on = len(topo.engines(core, able[0])) - n_off
 
-    def bank(b, n):
-        return T.pv[:, 512 * b:512 * b + n]
+    def bank(k, a, z):
+        return (T.pv if k < 4 else T.px)[:, 512 * (k % 4) + a:512 * (k % 4) + z]
 
     def fill(key, out, n, value, after=(), a=0, z=128):
         run("s", ["g0"] + list(after), [key], lambda q: q.activation(out, T.g0[a:z, 0:n], F.Copy, scale=8.0 * value))
 
+    dma("y", "dx0", 16, [], ["h00"], T.h0[:, 0:512], T.x[:, 0:512])
     dma("s", "dw", 16, [], ["wb"], T.wb[:, 0:128], T.w[:, 0:128])
-    dma("y", "dx", 16, [], ["h0"], T.h0[:, 0:4 * NC], T.x[:])
+    dma("y", "dx1", 16, [], ["h01"], T.h0[:, 512:4 * NC], T.x[:, 512:4 * NC])
     for i in range(PL - 1):
-        run("g", [], ["jb%d" % i], lambda q: q.iota(T.jb[0:32, 8 * i:8 * i + 8], [[0, 8]], 0, 8 >> i))
+        run("g", [], ["jb%d" % i], lambda q: q.iota(T.jb[0:32, 4 * i:4 * i + 4], [[0, 4]], 0, 8 >> i))
 
     def const(k):
         return T.qc[:, 128 * k:128 * k + 128], T.sc[:, 128 * k:128 * k + 128]
@@ -179,27 +189,23 @@ def rank_program(g, core, T, topo):
     run("v", [], ["u"], lambda q: q.memset(T.u[0:32, :], 0.0))
     run("v", [], ["gka"], lambda q: q.memset(T.gk[:, 0:512], 0.0))
     run("g", ["g0"], ["g8"], lambda q: q.affine_select(T.g8[:], T.g0[:], [[-1, 520]], A.is_equal, 0.0, 4, 4))
-    fill("gkb", T.gk[:, 512:1024], 512, 0.0)
     fill("wbz", T.wb[:, 128:576], 448, 0.0)
     fill("hp0", T.h0[:, 4 * NC:4 * W], 4 * W - 4 * NC, 0.0)
     fill("bqa", T.bq[:, 0:512], 512, 0.0)
-    fill("bqc", T.bq[:, 512:4 * W], 4 * W - 512, 0.0)
+    fill("bqc", T.bq[:, 512:1024], 512, 0.0)
     run("v", ["jb%d" % i for i in range(PL - 1)], ["jm"], lambda q: q.tensor_scalar(
         T.jm[0:32, :], T.jb[0:32, :], 8, None, A.bitwise_and))
-    run("v", ["u"], ["u4"], lambda q: q.memset(T.u[0:32, 4:128:32], -P))
+    run("v", ["u"], ["u4"], lambda q: q.memset(T.u[0:32, 4:64:32], -P))
     run("v", ["jm"], ["jp"], lambda q: q.tensor_scalar(
         T.jp[0:32, :], T.jm[0:32, :], 2 * P / 8, P, A.mult, A.subtract))
-    run("v", ["u"], ["u5"], lambda q: q.memset(T.u[0:32, 132:256:32], P))
+    run("v", ["u"], ["u5"], lambda q: q.memset(T.u[0:32, 68:128:32], P))
     for i in range(PL - 1):
-        run("v", ["jp", "u"], ["u%d" % i], lambda q: q.tensor_copy(T.u[0:32, i:256:32], T.jp[0:32, 8 * i:8 * i + 8]))
+        run("v", ["jp", "u"], ["u%d" % i], lambda q: q.tensor_copy(T.u[0:32, i:128:32], T.jp[0:32, 4 * i:4 * i + 4]))
+    run("v", ["gka"], ["gk1"], lambda q: q.memset(T.gk[64:128, 0:512:4], P * PL / 64))
+    run("v", ["u"] + us, ["ut"], lambda q: q.transpose(T.ut[0:32, 0:128], T.u[0:32, 0:128]))
     run("v", [], ["wl0"], lambda q: q.memset(T.wl0[:], 6))
-    run("v", ["u"] + us, ["ut"], lambda q: q.transpose(T.ut[0:32, 0:256], T.u[0:32, 0:256]))
-    run("v", ["gka", "gkb"], ["gk1"], lambda q: q.memset(T.gk[64:128, 0:1024:4], P * PL / 64))
-    run("v", ["ut", "gka", "gkb"], ["gk0"], lambda q: q.tensor_copy(T.gk[0:32, 0:1024:4], T.ut[0:32, 0:256]))
+    run("v", ["ut", "gka"], ["gk0"], lambda q: q.tensor_copy(T.gk[0:32, 0:512:4], T.ut[0:32, 0:128]))
     run("v", ["wb", "wbz"], ["qwb"], lambda q: q.quantize_mx(T.qwb[:], T.swb[:], T.wb[:]))
-    run("v", ["gk0", "gk1", "gka", "gkb"], ["qc0", "qc1"], lambda q: q.quantize_mx(
-        T.qc[:, 0:256], T.sc[:, 0:256], T.gk[:, 0:1024]))
-    fill("bqp", T.bq[64:128, 4 * NC:4 * W:4], W - NC, PAD, ["bqc"], 64, 128)
 
     def strength_tile(t):
         ws, wss, wl = T["ws%d" % t], T["wss%d" % t], T["wl%d" % t]
@@ -208,13 +214,19 @@ def rank_program(g, core, T, topo):
         run("v", ["qwb", "wl%d" % t], ["ws%d" % t], lambda q: q.tensor_copy(
             ws[:].bitcast(u32), T.qwb[:].bitcast(u32).indirect(wl[:])))
 
+    def pack(t, h, keys):
+        run("v", keys, ["qx%d%d" % (t, h)], lambda q: q.quantize_mx(
+            T["qx%d" % t][:, 128 * h:128 * h + 128], T["sx%d" % t][:, 128 * h:128 * h + 128],
+            T["h%d" % t][:, 512 * h:512 * h + 512]))
+
     strength_tile(0)
-    run("v", ["h0", "hp0"], ["qx0"], lambda q: q.quantize_mx(T.qx0[:], T.sx0[:], T.h0[:]))
-    dma("y", "dz", 16, ["qx0"], ["zt"], T.zt[:], T.z[:])
+    pack(0, 0, ["h00"])
+    run("v", ["gk0", "gk1", "gka"], ["qc0"], lambda q: q.quantize_mx(T.qc[:, 0:128], T.sc[:, 0:128], T.gk[:, 0:512]))
+    pack(0, 1, ["h01", "hp0"])
+    fill("bqp", T.bq[64:128, 4 * NC:4 * NC + 8:4], 2, PAD, ["bqc"], 64, 128)
+    fill("tiny", T.tiny[:], 1, -TINY)
+    dma("y", "dz", 16, ["qx01"], ["zt"], T.zt[:], T.z[:])
     run("g", [], ["idg"], lambda q: q.iota(T.idg[:], [[1, NC]], 128, -1))
-    ns = ["n%d" % i for i in range(PL)]
-    for i in range(PL):
-        fill(ns[i], T.u[0:32, 256 + i:384:32], 4, 2.0 ** i, ["u"], 0, 32)
 
     def unit_tiles(s, name, which=(0, 1, 2, 3)):
         src = T[name]
@@ -228,17 +240,23 @@ def rank_program(g, core, T, topo):
         return T.qe[:, o:o + 128], T.se[:, o:o + 128]
 
     def first_constants():
-        fill("gkc", T.gk[:, 1024:1536], 512, 0.0)
+        ns = ["n%d" % i for i in range(PL + 1)]
+        for i in range(PL - 1):
+            fill(ns[i], T.u[0:32, 128 + i:256:32], 4, 2.0 ** i, ["u"], 0, 32)
+        fill(ns[4], T.u[0:32, 132:192:32], 2, 16.0, ["u"], 0, 32)
+        fill(ns[5], T.u[0:32, 196:256:32], 2, -16.0, ["u"], 0, 32)
         run("s", ["g8"], ["gm"], lambda q: q.activation(T.gm[:], T.g8[:], F.Copy, scale=-0.5))
         fill("m16", T.m16[:], NC, 1.0)
         fill("m16z", T.m16[:, 0:NC:16], NC // 16, 0.0, ["m16"])
+        unit_tiles(0, "g8", (2, 3))
+        run("v", [], ["gkc"], lambda q: q.memset(T.gk[:, 512:1024], 0.0))
         run("v", ["idg"], ["idh"], lambda q: q.tensor_scalar(T.idh[:], T.idg[:], 15, None, A.bitwise_and))
-        run("v", ["u"] + ns, ["un"], lambda q: q.transpose(T.ut[0:32, 256:384], T.u[0:32, 256:384]))
+        run("v", ["u"] + ns, ["un"], lambda q: q.transpose(T.ut[0:32, 128:256], T.u[0:32, 128:256]))
         run("v", ["idh"], ["dg"], lambda q: q.tensor_scalar(T.dg[:], T.idh[:], 0.0, None, A.is_equal))
-        run("v", ["un", "gkc"], ["gk2"], lambda q: q.tensor_copy(T.gk[0:32, 1024:1536:4], T.ut[0:32, 256:384]))
+        run("v", ["un", "gkc"], ["gk2"], lambda q: q.tensor_copy(T.gk[0:32, 512:1024:4], T.ut[0:32, 128:256]))
         run("v", [], ["up"], lambda q: q.memset(T.va[:, 4:8 * S:5], BIG))
-        run("v", ["gk2", "gkc"], ["qc2"], lambda q: q.quantize_mx(
-            T.qc[:, 256:384], T.sc[:, 256:384], T.gk[:, 1024:1536]))
+        run("v", ["gk2", "gkc"], ["qc1"], lambda q: q.quantize_mx(
+            T.qc[:, 128:256], T.sc[:, 128:256], T.gk[:, 512:1024]))
         for b in range(4):
             run("v", ["up"], ["down%d" % b], lambda q: q.memset(T.va[:, 2 * S * b + S + 4:2 * S * b + 2 * S:5], -BIG))
         unit_tiles(1, "gm")
@@ -247,100 +265,110 @@ def rank_program(g, core, T, topo):
     sent = 0
     for t in range(R):
         qx, sx = T["qx%d" % t], T["sx%d" % t]
-        kx = "qx%d" % t
+        kx = ["qx%d0" % t, "qx%d1" % t]
         la, las = T["la%d" % t], T["las%d" % t]
-        run("t", ["qwb", kx], ["b0"], lambda q: q.matmul_mx(
-            bank(0, NC), T.qwb[:, 8 * t:8 * t + 128], T.swb[:, 8 * t:8 * t + 128], qx[:, 0:NC], sx[:, 0:NC], True, True))
-        for c in range(2):
-            run("t", ["ws%d" % t, "wss%d" % t, kx], ["b%d" % (1 + c)], lambda q: q.matmul_mx(
-                bank(1 + c, W), T["ws%d" % t][:], T["wss%d" % t][:], qx[:], sx[:], True, False))
+        for h in range(2):
+            a, z = 128 * h, 128 * h + 128
+            run("t", ["qwb", kx[h]], ["b%d" % (2 * h)], lambda q: q.matmul_mx(
+                bank(2 * h, 0, 128), T.qwb[:, 8 * t:8 * t + 128], T.swb[:, 8 * t:8 * t + 128],
+                qx[:, a:z], sx[:, a:z], True, True))
+            run("t", ["ws%d" % t, "wss%d" % t, kx[h]], ["b%d" % (1 + 2 * h)], lambda q: q.matmul_mx(
+                bank(1 + 2 * h, 0, 128), T["ws%d" % t][:], T["wss%d" % t][:], qx[:, a:z], sx[:, a:z], True, False))
+        run("v", ["b0", "bqa"], ["bq0"], lambda q: q.tensor_scalar(
+            T.bq[:, 0:512:4], bank(0, 0, 128), 0.0, 0.5, A.is_lt, A.subtract))
+        run("s", ["b2", "bqc", "tiny"], ["bq1"], lambda q: q.activation(
+            T.bq[:, 512:4 * NC:4], bank(2, 0, H), F.Sign, bias=T.tiny[:], scale=-1.0))
+        for h in range(2):
+            a, z = 128 * h, 128 * h + 128
+            run("v", ["bq%d" % h] + ["bqp"] * h, ["qb%d" % h], lambda q: q.quantize_mx(
+                T.qb[:, a:z], T.sb[:, a:z], T.bq[:, 4 * a:4 * z]))
+        for h in range(2):
+            a, z = 128 * h, 128 * h + 128
+            e, es = const(0)
+            run("t", ["qc0", "qb%d" % h], ["b%d" % (1 + 2 * h)], lambda q: q.matmul_mx(
+                bank(1 + 2 * h, 0, 128), e, es, T.qb[:, a:z], T.sb[:, a:z], False, True))
+        run("v", ["b1", "wbz"], ["rm0"], lambda q: q.tensor_tensor_scan(
+            T.rm[:, 0:128], bank(1, 0, 128), T.wb[:, 128:256], FLOOR, A.max, A.add))
+        run("v", ["b3", "wbz", "rm0"], ["rm1"], lambda q: q.tensor_tensor_scan(
+            T.rm[:, 128:NC + 2], bank(3, 0, H + 2), T.wb[:, 128:128 + H + 2], T.rm[:, 127:128], A.max, A.add))
+        run("s", ["rm0", "rm1"], ["sg", "ix"], lambda q: q.activation(
+            T.sg[:], T.rm[:, 0:NC], F.Sign, bias=T.rm[:, NC:NC + 1], scale=-1.0, accum_out=T.ix[:, 0:1]))
         if t == 0:
-            unit_tiles(0, "g8", (0,))
-        run("v", ["b0", "bqa", "bqc"], ["bq"], lambda q: q.tensor_scalar(
-            T.bq[:, 0:4 * NC:4], bank(0, NC), 0.0, 0.5, A.is_lt, A.subtract))
-        run("v", ["bq", "bqp"], ["qb"], lambda q: q.quantize_mx(T.qb[:], T.sb[:], T.bq[:]))
-        if t == 0:
-            unit_tiles(0, "g8", (1,))
-        for c in range(2):
-            e, es = const(c)
-            run("t", ["qc%d" % c, "qb"], ["b%d" % (1 + c)], lambda q: q.matmul_mx(
-                bank(1 + c, W), e, es, T.qb[:], T.sb[:], False, True))
-        for c in range(2):
-            rm, sg = T["rm%d" % c], T["sg%d" % c]
-            run("v", ["b%d" % (1 + c), "wbz"], ["rm%d" % c], lambda q: q.tensor_tensor_scan(
-                rm[:], bank(1 + c, W), T.wb[:, 128:128 + W], FLOOR, A.max, A.add))
-            run("s", ["rm%d" % c], ["sg%d" % c, "ix%d" % c], lambda q: q.activation(
-                sg[:], rm[:, 0:NC], F.Sign, bias=rm[:, NC:NC + 1], scale=-1.0, accum_out=T.ix[:, c:c + 1]))
-        if t == 0:
-            unit_tiles(0, "g8", (2, 3))
+            unit_tiles(0, "g8", (0, 1))
         of = T["of%d" % t]
-        run("v", ["ix0", "ix1"], ["of%d" % t], lambda q: q.tensor_copy(of[:], T.ix[:, 0:2]))
+        ko = ["of%d%d" % (t, i) for i in range(3)]
+        run("v", ["ix"], ko[0:1], lambda q: q.tensor_copy(of[:, 0:1], T.ix[:, 0:1]))
+        run("v", ["ix"], ko[1:2], lambda q: q.tensor_copy(of[0:64, 1:2], T.ix[64:128, 0:1]))
+        run("v", ["ix"], ko[2:3], lambda q: q.tensor_copy(of[64:128, 1:2], T.ix[0:64, 0:1]))
         rep, reps = la[:, L * mine:L * mine + L], las[:, L * mine:L * mine + L]
-        run("s", [kx, "of%d" % t], ["reps%d" % t], lambda q: q.activation(reps, sx[:].indirect(of[:]), F.Copy))
-        run("v", [kx, "of%d" % t], ["rep%d" % t], lambda q: q.tensor_copy(
+        run("s", kx + ko, ["reps%d" % t], lambda q: q.activation(reps, sx[:].indirect(of[:]), F.Copy))
+        run("v", kx + ko, ["rep%d" % t], lambda q: q.tensor_copy(
             rep.bitcast(u32), qx[:].bitcast(u32).indirect(of[:])))
         for kind, to, helpers in CALLS:
             need("g", [("rep%d" if kind == "c" else "reps%d") % t], [])
             src = rep.bitcast(u8) if kind == "c" else reps
-            transfers = [_write(T, topo, core, t, kind, src, to, planes, mine, me)]
-            sent += n_off
+            transfers = []
             if helpers:
                 ids = []
                 for h in helpers:
                     rid, pid = topo.addr(able[h], core)
                     ids.append(DstId(rid=rid, pnc=pid))
+                mask, n = _hand_over(topo, core, able[helpers[0]], mate, t, not to)
                 transfers.append(RemoteDMATransfer(
-                    dst_ids=ids, dma_engine_mask=on_chip, remote_sem=T.sem["hand%d" % t], srcs=[src],
+                    dst_ids=ids, dma_engine_mask=mask, remote_sem=T.sem["hand%d" % t], srcs=[src],
                     dsts=[_handed(T, t, kind)] * len(ids)))
-                sent += n_on
+                sent += n
+            if to:
+                transfers.append(_write(T, topo, core, t, kind, src, to, planes, mine, me))
+                sent += n_off
             g.remote_dma_fused(transfers, local_sem=T.sem.sent)
         arrive(("near%d" % t, 2 * 3 * n_off), ["near%d" % t])
         arrive(("late%d" % t, 2 * 4 * n_off), ["late%d" % t])
-        for b in range(4):
-            e, es = unit(0, b)
-            run("t", ["e0%d" % b, kx], ["px%d" % b], lambda q: q.matmul_mx(
-                T.px[:, 512 * b:512 * b + NC], e, es, qx[:, 0:NC], sx[:, 0:NC], True, False))
         if t == 0:
             first_constants()
-        e, es = const(2)
-        run("t", ["qc2", "qb"], ["b3"], lambda q: q.matmul_mx(
-            bank(3, NC), e, es, T.qb[:, 0:NC], T.sb[:, 0:NC], True, True))
-        run("s", ["b3"], ["lt"], lambda q: q.activation(T.lt[:], bank(3, NC), F.Copy))
-        run("s", ["b3"], ["lvs%d" % t], lambda q: q.activation(
-            T.lvs[0:1, NC * t:NC * t + NC], T.pv[0:1, 3 * 512:3 * 512 + NC], F.Identity, bias=half))
+        e, es = const(1)
+        run("t", ["qc1", "qb0", "qb1"], ["b7"], lambda q: q.matmul_mx(
+            bank(7, 0, NC), e, es, T.qb[:, 0:NC], T.sb[:, 0:NC], True, True))
+        run("s", ["b7"], ["lt0"], lambda q: q.activation(T.lt[:, 0:128], bank(7, 0, 128), F.Copy))
+        run("s", ["b7"], ["lt1"], lambda q: q.activation(T.lt[:, 128:NC], bank(7, 128, NC), F.Copy, scale=0.5))
+        run("s", ["lt0", "lt1"], ["lvs%d" % t], lambda q: q.activation(
+            T.lvs[0:1, NC * t:NC * t + NC], T.lt[0:1, :], F.Identity, bias=half))
         dma("y", "dlv", 16 * (t + 1), ["lvs%d" % t, "late%d" % t], [], T.lv[t:t + 1, :], T.lvs[0:1, NC * t:NC * t + NC])
         ov, hn = T["ov%d" % t], T["h%d" % (t + 1)]
-        run("v", ["lt", "dg"], ["ld"], lambda q: q.tensor_tensor(T.ld[:], T.lt[:], T.dg[:], A.mult))
+        run("v", [], ["hp%d" % (t + 1)], lambda q: q.memset(hn[:, 4 * NC:4 * W], 0.0))
+        run("v", ["lt0", "lt1", "dg"], ["ld"], lambda q: q.tensor_tensor(T.ld[:], T.lt[:], T.dg[:], A.mult))
         if t + 1 < R:
             run("v", [], ["wl%d" % (t + 1)], lambda q: q.memset(T["wl%d" % (t + 1)][:], 8 * (t + 1) + 6))
         run("v", ["ld", "m16", "m16z"], ["ls"], lambda q: q.tensor_tensor_scan(
             T.ls[:], T.m16[:], T.ld[:], 0.0, A.mult, A.add))
-        run("v", [], ["hp%d" % (t + 1)], lambda q: q.memset(hn[:, 4 * NC:4 * W], 0.0))
-        run("v", ["ls"], ["ov%d" % t], lambda q: q.tensor_scalar(
-            ov[:], T.ls[:, 15:NC:16], 5.0, 5.0 * half + 3.0, A.mult, A.add))
         if t + 1 < R:
             strength_tile(t + 1)
+        run("v", ["ls"], ["ov%d" % t], lambda q: q.tensor_scalar(
+            ov[:], T.ls[:, 15:NC:16], 5.0, 5.0 * half + 3.0, A.mult, A.add))
         if t == 1:
             run("v", ["zt"], ["qz"], lambda q: q.quantize_mx(T.qz[:], T.sz[:], T.zt[:]))
 
-        def unpack(first, keys, order):
-            o = 2 * L * first
+        order = ((1, "v"), (0, "s"), (3, "v"), (2, "s"))
+        for h, keys in enumerate((["rep%d" % t, "reps%d" % t, "near%d" % t], ["late%d" % t])):
+            o = 4 * L * h
             for b, engine in order:
                 e, es = unit(0, b)
-                run("t", ["e0%d" % b] + keys, ["b%d" % b], lambda q: q.matmul_mx(
-                    bank(b, 4 * L), e, es, la[:, o:o + 4 * L], las[:, o:o + 4 * L], True, True))
+                run("t", ["e0%d" % b] + keys, ["b%d" % (b + 4 * h)], lambda q: q.matmul_mx(
+                    bank(b + 4 * h, 0, 4 * L), e, es, la[:, o:o + 4 * L], las[:, o:o + 4 * L], True, True))
             for b, engine in order:
                 for j in range(2):
-                    i, c = (me - first - j) % 4, 512 * b + 2 * L * j
-                    out, in_ = T.va[:, 2 * S * b + i:2 * S * b + 2 * S:5], T.pv[:, c:c + 2 * L]
+                    i, k = (me - 2 * h - j) % 4, b + 4 * h
+                    out, in_ = T.va[:, 2 * S * b + i:2 * S * b + 2 * S:5], bank(k, 2 * L * j, 2 * L * j + 2 * L)
                     if engine == "s":
-                        run("s", ["b%d" % b], ["va%d%d" % (b, i)], lambda q: q.activation(out, in_, F.Copy))
+                        run("s", ["b%d" % k], ["va%d%d" % (b, i)], lambda q: q.activation(out, in_, F.Copy))
                     else:
-                        run("v", ["b%d" % b], ["va%d%d" % (b, i)], lambda q: q.tensor_copy(out, in_))
-
-        unpack(0, ["rep%d" % t, "reps%d" % t, "near%d" % t], ((0, "v"), (2, "s"), (1, "v"), (3, "s")))
-        unpack(2, ["late%d" % t], ((1, "v"), (0, "s"), (3, "v"), (2, "s")))
-        for b in (1, 0, 3, 2):
+                        run("v", ["b%d" % k], ["va%d%d" % (b, i)], lambda q: q.tensor_copy(out, in_))
+        for h, a in enumerate((0, H)):
+            for b, engine in order:
+                e, es = unit(0, b)
+                run("t", ["e0%d" % b] + kx, ["b%d" % (b + 4 * h)], lambda q: q.matmul_mx(
+                    bank(b + 4 * h, 0, 128), e, es, qx[:, a:a + 128], sx[:, a:a + 128], True, False))
+        for b, engine in order:
             o = 2 * S * b
             run("v", ["up", "down%d" % b] + ["va%d%d" % (b, i) for i in range(4)], ["vs%d" % b],
                 lambda q: q.tensor_tensor_scan(
@@ -348,32 +376,47 @@ def rank_program(g, core, T, topo):
         qv, qvs = T["qv%d" % t], T["qvs%d" % t]
         run("v", ["vs0", "vs1", "vs2", "vs3"], ["qv%d" % t], lambda q: q.quantize_mx(qv[:], qvs[:], T.vs[:]))
         vv, vvs = T["vv%d" % t], T["vvs%d" % t]
-        run("s", ["qv%d" % t, "ov%d" % t], ["vvs%d" % t], lambda q: q.activation(vvs[:], qvs[:].indirect(ov[:]), F.Copy))
-        run("v", ["qv%d" % t, "ov%d" % t], ["vv%d" % t], lambda q: q.tensor_copy(
-            vv[:].bitcast(u32), qv[:].bitcast(u32).indirect(ov[:])))
-        for b in range(4):
-            e, es = unit(1, b)
-            run("t", ["e1%d" % b, "vv%d" % t, "vvs%d" % t], ["px%d" % b], lambda q: q.matmul_mx(
-                T.px[:, 512 * b:512 * b + NC], e, es, vv[:], vvs[:], False, True))
-        for b in range(4):
-            out, in_ = hn[:, b:4 * NC:4], T.px[:, 512 * b:512 * b + NC]
-            if b % 2 == 0:
-                run("s", ["px%d" % b], ["h%d%d" % (t + 1, b)], lambda q: q.activation(out, in_, F.Copy, scale=8.0))
+        for h, (a, z) in enumerate(((0, 8), (8, 12))):
+            run("s", ["qv%d" % t, "ov%d" % t], ["vvs%d%d" % (t, h)], lambda q: q.activation(
+                vvs[:, 16 * a:16 * z], qvs[:].indirect(ov[:, a:z]), F.Copy))
+            run("v", ["qv%d" % t, "ov%d" % t], ["vv%d%d" % (t, h)], lambda q: q.tensor_copy(
+                vv[:, 16 * a:16 * z].bitcast(u32), qv[:].bitcast(u32).indirect(ov[:, a:z])))
+        for h, a in enumerate((0, H)):
+            keys = ["%s%d%d" % (k, t, j) for k in ("vv", "vvs") for j in range(h + 1)]
+            for b in range(4):
+                e, es = unit(1, b)
+                run("t", ["e1%d" % b] + keys, ["b%d" % (b + 4 * h)], lambda q: q.matmul_mx(
+                    bank(b + 4 * h, 0, 128), e, es, vv[:, a:a + 128], vvs[:, a:a + 128], False, True))
+
+        def cast(h, b, engine):
+            k, key = b + 4 * h, "h%d%d%d" % (t + 1, h, b)
+            out, in_ = (hn[:, b:512:4], bank(k, 0, 128)) if h == 0 else (hn[:, 512 + b:4 * NC:4], bank(k, 128 - H, 128))
+            if engine == "s":
+                run("s", ["b%d" % k], [key], lambda q: q.activation(out, in_, F.Copy, scale=8.0))
             else:
-                run("v", ["px%d" % b], ["h%d%d" % (t + 1, b)], lambda q: q.tensor_scalar(out, in_, 8.0, None, A.mult))
-        run("v", ["h%d%d" % (t + 1, b) for b in range(4)] + ["hp%d" % (t + 1)], ["qx%d" % (t + 1)],
-            lambda q: q.quantize_mx(T["qx%d" % (t + 1)][:], T["sx%d" % (t + 1)][:], hn[:]))
+                run("v", ["b%d" % k], [key], lambda q: q.tensor_scalar(out, in_, 8.0, None, A.mult))
+
+        for b in range(4):
+            cast(0, b, "sv"[b % 2])
+        for b in range(3):
+            cast(1, b, "s")
+        pack(t + 1, 0, ["h%d0%d" % (t + 1, b) for b in range(4)])
+        cast(1, 3, "v")
+        pack(t + 1, 1, ["h%d1%d" % (t + 1, b) for b in range(4)] + ["hp%d" % (t + 1)])
 
     qx, sx = T["qx%d" % R], T["sx%d" % R]
-    kx = "qx%d" % R
-    run("t", ["qz", kx], ["b0"], lambda q: q.matmul_mx(
-        bank(0, NC), T.qz[:], T.sz[:], qx[:, 0:NC], sx[:, 0:NC], True, True))
-    total = 16 * 6
-    dma("y", "dout", total, [kx], [], T.oc[:], qx[:, 0:NC].bitcast(u8))
+    kx = ["qx%d0" % R, "qx%d1" % R]
+    for h in range(2):
+        run("t", ["qz", kx[h]], ["b%d" % h], lambda q: q.matmul_mx(
+            bank(h, 0, 128), T.qz[:], T.sz[:], qx[:, 128 * h:128 * h + 128], sx[:, 128 * h:128 * h + 128], True, True))
+    total = 16 * 7
+    dma("y", "dout", total, kx[0:1], [], T.oc[:, 0:512], qx[:, 0:128].bitcast(u8))
+    dma("y", "dout", total, kx[1:2], [], T.oc[:, 512:4 * NC], qx[:, 128:NC].bitcast(u8))
+    run("s", ["b0"], ["ysb0"], lambda q: q.activation(T.ysb[:, 0:128], bank(0, 0, 128), F.Copy))
+    run("v", ["b1"], ["ysb1"], lambda q: q.tensor_copy(T.ysb[:, 128:NC], bank(1, 0, H)))
     for k in range(4):
-        dma("s", "dout", total, [kx], [], T.osc[4 * k:4 * k + 4, :], sx[32 * k:32 * k + 4, 0:NC])
-    run("v", ["b0"], ["ysb"], lambda q: q.tensor_copy(T.ysb[:], bank(0, NC)))
-    dma("y", "dout", total, ["ysb"], [], T.y[:], T.ysb[:])
+        dma("s", "dout", total, kx, [], T.osc[4 * k:4 * k + 4, :], sx[32 * k:32 * k + 4, 0:NC])
+    dma("y", "dout", total, ["ysb0", "ysb1"], [], T.y[:], T.ysb[:])
     wait("g", ("sent", sent))
     finish("g")
     wait("g", ("dlv", 16 * R))

@@ -4,30 +4,37 @@ from concourse.mybir import dt, AluOpType, ActivationFunctionType
 NC, L, R, PL = 192, 32, 3, 5
 W = 256
 H = NC - 128
+O = 128
 S = 5 * L
 P, FLOOR, PAD, BIG, TINY = 2.0 ** 76, -2.0 ** 74, -2.0 ** -5, 2.0 ** 61, 2.0 ** -120
 X4, BF, F32, U8, I32, U16 = "float8_e4m3fn_x4", "bfloat16", "float32", "uint8", "int32", "uint16"
 
-NEAR = ((1, 0), (0, 1), (1, 1))
-CALLS = (("c", (), (1, 3)), ("s", NEAR, (0, 2)), ("c", NEAR, ()), ("s", ((0, 3),), ()))
-HELPERS = (("s", ((0, 2), (1, 2))), ("c", ((1, 2), (1, 3))), ("s", ((1, 3),)), ("c", ((0, 2), (0, 3))))
+NEAR, SAME, OTHER = ((0, 1), (1, 1), (1, 0)), ((0, 2), (0, 3)), ((1, 2), (1, 3))
+CODES, SCALES = ("c", 0, L), ("s", 0, L)
+PLAN = [(((CODES, "in", (1, 3)),), ((SCALES, "out", NEAR), (SCALES, "in", (2, 0, 4))), ((CODES, "out", NEAR),),
+         ((CODES, "out", SAME[1:]),))]
+PLAN += [(((CODES, "all", (1, 4, 3)),), ((SCALES, "out", NEAR), (SCALES, "in", (2, 0))), ((CODES, "out", NEAR),),
+          ((SCALES, "out", SAME[1:]),))] * (R - 1)
+HELPERS = [{0: (SCALES, SAME[:1]), 1: (CODES, OTHER), 2: (SCALES, OTHER), 3: (CODES, SAME[:1]), 4: (SCALES, SAME[1:])}]
+HELPERS += [{0: (SCALES, SAME[:1]), 1: (CODES, OTHER), 2: (SCALES, OTHER), 3: (CODES, SAME[1:]),
+             4: (CODES, SAME[:1])}] * (R - 1)
 
 SCRATCH = {"pv": ("psum", [128, 2048], F32), "px": ("psum", [128, 2048], F32)}
 for _n, _w, _d in (
-        ("wb", 576, BF), ("zt", 512, BF), ("qwb", 144, X4), ("swb", 144, U8), ("qz", 128, X4), ("sz", 128, U8),
-        ("g0", 520, BF), ("g8", 520, BF), ("gm", 520, BF),
+        ("wb", 648, BF), ("zt", 512, BF), ("qwb", 144, X4), ("swb", 144, U8), ("qz", 128, X4), ("sz", 128, U8),
+        ("g8", 520, BF), ("gm", 520, BF),
         ("qe", 8 * 128, X4), ("se", 8 * 128, U8), ("u", 256, BF), ("ut", 256, BF), ("gk", 1024, BF),
         ("qc", 256, X4), ("sc", 256, U8), ("bq", 4 * W, BF), ("qb", W, X4), ("sb", W, U8),
         ("m16", NC, BF), ("idg", NC, I32), ("idh", NC, I32), ("dg", NC, BF),
-        ("jb", 16, I32), ("jm", 16, I32), ("jp", 16, BF), ("tiny", 1, F32),
+        ("jb", 16, I32), ("jm", 16, I32), ("tiny", 1, F32),
         ("rm", NC + 2, F32), ("sg", NC, BF), ("ix", 4, F32),
-        ("lt", NC, BF), ("ld", NC, BF), ("ls", NC, F32), ("lvs", R * NC, F32),
+        ("ld", NC, BF), ("ls", NC, BF), ("lvs", R * NC, F32),
         ("va", 8 * S, BF), ("vs", 4 * S, BF), ("ysb", NC, F32)):
     SCRATCH[_n] = ("sbuf", [128, _w], _d)
 for _t in range(R + 1):
     SCRATCH["h%d" % _t] = ("sbuf", [128, 4 * W], BF)
-    SCRATCH["qx%d" % _t] = ("sbuf", [128, W], X4)
-    SCRATCH["sx%d" % _t] = ("sbuf", [128, W], U8)
+    SCRATCH["qx%d" % _t] = ("sbuf", [128, O + W], X4)
+    SCRATCH["sx%d" % _t] = ("sbuf", [128, O + W], U8)
 for _t in range(R):
     for _n, _w in (("ws", 128), ("la", 8 * L), ("hd", L), ("qv", S), ("vv", NC)):
         SCRATCH["%s%d" % (_n, _t)] = ("sbuf", [128, _w], X4)
@@ -79,8 +86,8 @@ def _scheduler(g, T):
             writer[k] = token
             readers[k] = []
 
-    def run(q, reads, writes, call):
-        need(q, reads, writes)
+    def run(q, reads, writes, call, adds=False):
+        need(q, reads, [] if adds else writes)
         name = COUNTER[q]
         call(queue[q]).then_inc(T.sem[name], 1)
         count[name] += 1
@@ -115,30 +122,33 @@ def _places(T, topo, core):
     able = [c for c in topo.cores_of(core) if c != core and all(topo.may_write(c, d) for d in cores)]
     able.sort(key=lambda c: topo.die(c) != topo.die(core))
     able += [c for c in topo.cores_of(core) if c != core and c not in able and topo.die(c) == topo.die(core)]
-    return planes, mine, planes[mine].index(core), able[:len(HELPERS)]
+    able += [c for c in topo.cores_of(core) if c != core and c not in able]
+    return planes, mine, planes[mine].index(core), able
 
 
-def _write(T, topo, core, t, kind, src, to, planes, mine, me):
+def _view(T, name, t, piece, o):
+    kind, a, z = piece
+    if kind == "c":
+        return T["%s%d" % (name, t)][:, o + a:o + z].bitcast(dt.uint8)
+    return T["%ss%d" % (name, t)][:, o + a:o + z]
+
+
+def _write(T, topo, core, t, piece, src, to, planes, mine, me):
     ids, dsts = [], []
     for a, k in to:
         far = planes[(mine + a) % 2][(me + k) % 4]
         rid, pid = topo.addr(far, core)
         ids.append(DstId(rid=rid, pnc=pid))
-        o = L * (2 * k + mine)
-        dsts.append(T["la%d" % t][:, o:o + L].bitcast(dt.uint8) if kind == "c" else T["las%d" % t][:, o:o + L])
+        dsts.append(_view(T, "la", t, piece, L * (2 * k + mine)))
     sem = T.sem[("near%d" if to[0][1] < 2 else "late%d") % t]
     return RemoteDMATransfer(dst_ids=ids, dma_engine_mask=topo.mask(core, far), remote_sem=sem, srcs=[src], dsts=dsts)
 
 
-def _handed(T, t, kind):
-    return T["hd%d" % t][:].bitcast(dt.uint8) if kind == "c" else T["hds%d" % t][:]
-
-
-def _hand_over(topo, core, helper, far, t, alone):
-    if alone and t > 0:
-        return topo.mask(core, helper), len(topo.engines(core, helper))
-    return (topo.mask(core, helper) & ~topo.mask(core, far),
-            len(topo.engines(core, helper)) - len(topo.engines(core, far)))
+def _hand_over(topo, core, helper, far, which):
+    out = topo.engines(core, far)
+    inner = [e for e in topo.engines(core, helper) if e not in out]
+    n = len(inner) // 2
+    return {"all": out + inner, "out": out, "in": inner, "in0": inner[:n], "in1": inner[n:]}[which]
 
 
 def _hand_on(g, core, T, topo):
@@ -146,14 +156,14 @@ def _hand_on(g, core, T, topo):
     if not ranks:
         return
     planes, mine, me, able = _places(T, topo, ranks[0])
-    if core not in able:
+    if able.index(core) not in HELPERS[0]:
         return
-    kind, to = HELPERS[able.index(core)]
     far = planes[mine][(me + 1) % 4]
-    alone = [not call[1] for call in CALLS if able.index(core) in call[2]][0]
-    for t in range(R):
-        g.wait_ge(T.sem["hand%d" % t], _hand_over(topo, ranks[0], core, far, t, alone)[1])
-        g.remote_dma_fused([_write(T, topo, core, t, kind, _handed(T, t, kind), to, planes, mine, me)],
+    for t, calls in enumerate(PLAN):
+        piece, to = HELPERS[t][able.index(core)]
+        which = [move[1] for call in calls for move in call if able.index(core) in move[2]][0]
+        g.wait_ge(T.sem["hand%d" % t], len(_hand_over(topo, ranks[0], core, far, which)))
+        g.remote_dma_fused([_write(T, topo, core, t, piece, _view(T, "hd", t, piece, 0), to, planes, mine, me)],
                            local_sem=T.sem.sent)
     g.wait_ge(T.sem.sent, R * len(topo.engines(core, far)))
 
@@ -173,39 +183,44 @@ def rank_program(g, core, T, topo):
         return (T.pv if k < 4 else T.px)[:, 512 * (k % 4) + a:512 * (k % 4) + z]
 
     def fill(key, out, n, value, after=(), a=0, z=128):
-        run("s", ["g0"] + list(after), [key], lambda q: q.activation(out, T.g0[a:z, 0:n], F.Copy, scale=8.0 * value))
+        zeros = T.wb[a:z, 128:128 + n]
+        if value:
+            run("s", ["wbz"] + list(after), [key], lambda q: q.activation(out, zeros, F.Identity, bias=value))
+        else:
+            run("s", ["wbz"] + list(after), [key], lambda q: q.activation(out, zeros, F.Copy))
 
     dma("y", "dx0", 16, [], ["h00"], T.h0[:, 0:512], T.x[:, 0:512])
-    dma("s", "dw", 16, [], ["wb"], T.wb[:, 0:128], T.w[:, 0:128])
+    dma("s", "dw", 16, [], ["wb"], T.wb[:, 32:128], T.w[:, 0:96])
     dma("y", "dx1", 16, [], ["h01"], T.h0[:, 512:4 * NC], T.x[:, 512:4 * NC])
-    for i in range(PL - 1):
+    for i in (2, 3):
         run("g", [], ["jb%d" % i], lambda q: q.iota(T.jb[0:32, 4 * i:4 * i + 4], [[0, 4]], 0, 8 >> i))
+    run("g", [], ["hp0"], lambda q: q.iota(
+        T.h0[:, 4 * NC:4 * W], [[0, 4 * W - 4 * NC]], 0, 0, allow_small_or_imprecise_dtypes=True))
 
     def const(k):
         return T.qc[:, 128 * k:128 * k + 128], T.sc[:, 128 * k:128 * k + 128]
 
     us = ["u%d" % i for i in range(PL + 1)]
-    run("v", [], ["g0"], lambda q: q.memset(T.g0[:], 0.125))
-    run("v", [], ["u"], lambda q: q.memset(T.u[0:32, :], 0.0))
-    run("v", [], ["gka"], lambda q: q.memset(T.gk[:, 0:512], 0.0))
-    run("g", ["g0"], ["g8"], lambda q: q.affine_select(T.g8[:], T.g0[:], [[-1, 520]], A.is_equal, 0.0, 4, 4))
-    fill("wbz", T.wb[:, 128:576], 448, 0.0)
-    fill("hp0", T.h0[:, 4 * NC:4 * W], 4 * W - 4 * NC, 0.0)
+    run("v", [], ["wbz"], lambda q: q.memset(T.wb[:, 128:648], 0.0))
+    run("v", [], ["u"], lambda q: q.memset(T.u[0:32, 0:128], 0.0))
+    run("g", ["wbz"], ["g8"], lambda q: q.affine_select(
+        T.g8[:], T.wb[:, 128:648], [[-1, 520]], A.not_equal, 0.125, 4, 4))
+    fill("gka", T.gk[:, 0:512], 512, 0.0)
     fill("bqa", T.bq[:, 0:512], 512, 0.0)
-    fill("bqc", T.bq[:, 512:1024], 512, 0.0)
-    run("v", ["jb%d" % i for i in range(PL - 1)], ["jm"], lambda q: q.tensor_scalar(
-        T.jm[0:32, :], T.jb[0:32, :], 8, None, A.bitwise_and))
+    dma("y", "dz", 16, ["wbz"], ["bqc"], T.bq[:, 512:1024], T.wb[:, 128:640])
+    run("v", [], ["wl0"], lambda q: q.memset(T.wl0[:], 6))
+    run("v", ["jb2", "jb3"], ["jb0"], lambda q: q.tensor_scalar(T.jb[0:32, 0:8], T.jb[0:32, 8:16], 4.0, None, A.mult))
     run("v", ["u"], ["u4"], lambda q: q.memset(T.u[0:32, 4:64:32], -P))
-    run("v", ["jm"], ["jp"], lambda q: q.tensor_scalar(
-        T.jp[0:32, :], T.jm[0:32, :], 2 * P / 8, P, A.mult, A.subtract))
+    run("v", ["jb0", "jb2", "jb3"], ["jm"], lambda q: q.tensor_scalar(
+        T.jm[0:32, :], T.jb[0:32, :], 8, None, A.bitwise_and))
     run("v", ["u"], ["u5"], lambda q: q.memset(T.u[0:32, 68:128:32], P))
     for i in range(PL - 1):
-        run("v", ["jp", "u"], ["u%d" % i], lambda q: q.tensor_copy(T.u[0:32, i:128:32], T.jp[0:32, 4 * i:4 * i + 4]))
+        run("v", ["jm", "u"], ["u%d" % i], lambda q: q.tensor_scalar(
+            T.u[0:32, i:128:32], T.jm[0:32, 4 * i:4 * i + 4], 2 * P / 8, P, A.mult, A.subtract))
     run("v", ["gka"], ["gk1"], lambda q: q.memset(T.gk[64:128, 0:512:4], P * PL / 64))
     run("v", ["u"] + us, ["ut"], lambda q: q.transpose(T.ut[0:32, 0:128], T.u[0:32, 0:128]))
-    run("v", [], ["wl0"], lambda q: q.memset(T.wl0[:], 6))
-    run("v", ["ut", "gka"], ["gk0"], lambda q: q.tensor_copy(T.gk[0:32, 0:512:4], T.ut[0:32, 0:128]))
-    run("v", ["wb", "wbz"], ["qwb"], lambda q: q.quantize_mx(T.qwb[:], T.swb[:], T.wb[:]))
+    run("s", ["ut", "gka"], ["gk0"], lambda q: q.activation(T.gk[0:32, 0:512:4], T.ut[0:32, 0:128], F.Copy))
+    run("v", ["wb", "wbz"], ["qwb"], lambda q: q.quantize_mx(T.qwb[:], T.swb[:], T.wb[:, 32:608]))
 
     def strength_tile(t):
         ws, wss, wl = T["ws%d" % t], T["wss%d" % t], T["wl%d" % t]
@@ -216,16 +231,14 @@ def rank_program(g, core, T, topo):
 
     def pack(t, h, keys):
         run("v", keys, ["qx%d%d" % (t, h)], lambda q: q.quantize_mx(
-            T["qx%d" % t][:, 128 * h:128 * h + 128], T["sx%d" % t][:, 128 * h:128 * h + 128],
+            T["qx%d" % t][:, O + 128 * h:O + 128 * h + 128], T["sx%d" % t][:, O + 128 * h:O + 128 * h + 128],
             T["h%d" % t][:, 512 * h:512 * h + 512]))
 
-    strength_tile(0)
-    pack(0, 0, ["h00"])
-    run("v", ["gk0", "gk1", "gka"], ["qc0"], lambda q: q.quantize_mx(T.qc[:, 0:128], T.sc[:, 0:128], T.gk[:, 0:512]))
-    pack(0, 1, ["h01", "hp0"])
-    fill("bqp", T.bq[64:128, 4 * NC:4 * NC + 8:4], 2, PAD, ["bqc"], 64, 128)
     fill("tiny", T.tiny[:], 1, -TINY)
-    dma("y", "dz", 16, ["qx01"], ["zt"], T.zt[:], T.z[:])
+    pack(0, 0, ["h00"])
+    pack(0, 1, ["h01", "hp0"])
+    run("v", ["gk0", "gk1", "gka"], ["qc0"], lambda q: q.quantize_mx(T.qc[:, 0:128], T.sc[:, 0:128], T.gk[:, 0:512]))
+    strength_tile(0)
     run("g", [], ["idg"], lambda q: q.iota(T.idg[:], [[1, NC]], 128, -1))
 
     def unit_tiles(s, name, which=(0, 1, 2, 3)):
@@ -241,25 +254,25 @@ def rank_program(g, core, T, topo):
 
     def first_constants():
         ns = ["n%d" % i for i in range(PL + 1)]
+        fill("uz", T.u[0:32, 128:256], 128, 0.0, (), 0, 32)
+        fill("gkc", T.gk[:, 512:1024], 512, 0.0)
         for i in range(PL - 1):
-            fill(ns[i], T.u[0:32, 128 + i:256:32], 4, 2.0 ** i, ["u"], 0, 32)
-        fill(ns[4], T.u[0:32, 132:192:32], 2, 16.0, ["u"], 0, 32)
-        fill(ns[5], T.u[0:32, 196:256:32], 2, -16.0, ["u"], 0, 32)
+            fill(ns[i], T.u[0:32, 128 + i:256:32], 4, 2.0 ** i, ["uz"], 0, 32)
+        fill(ns[4], T.u[0:32, 132:192:32], 2, 16.0, ["uz"], 0, 32)
+        fill(ns[5], T.u[0:32, 196:256:32], 2, -16.0, ["uz"], 0, 32)
+        fill("up", T.va[:, 4:8 * S:5], 8 * L, BIG)
+        for b in range(4):
+            fill("down%d" % b, T.va[:, 2 * S * b + S + 4:2 * S * b + 2 * S:5], L, -BIG, ["up"])
         run("s", ["g8"], ["gm"], lambda q: q.activation(T.gm[:], T.g8[:], F.Copy, scale=-0.5))
         fill("m16", T.m16[:], NC, 1.0)
         fill("m16z", T.m16[:, 0:NC:16], NC // 16, 0.0, ["m16"])
-        unit_tiles(0, "g8", (2, 3))
-        run("v", [], ["gkc"], lambda q: q.memset(T.gk[:, 512:1024], 0.0))
+        unit_tiles(0, "g8")
         run("v", ["idg"], ["idh"], lambda q: q.tensor_scalar(T.idh[:], T.idg[:], 15, None, A.bitwise_and))
-        run("v", ["u"] + ns, ["un"], lambda q: q.transpose(T.ut[0:32, 128:256], T.u[0:32, 128:256]))
+        run("v", ["uz"] + ns, ["un"], lambda q: q.transpose(T.ut[0:32, 128:256], T.u[0:32, 128:256]))
         run("v", ["idh"], ["dg"], lambda q: q.tensor_scalar(T.dg[:], T.idh[:], 0.0, None, A.is_equal))
         run("v", ["un", "gkc"], ["gk2"], lambda q: q.tensor_copy(T.gk[0:32, 512:1024:4], T.ut[0:32, 128:256]))
-        run("v", [], ["up"], lambda q: q.memset(T.va[:, 4:8 * S:5], BIG))
         run("v", ["gk2", "gkc"], ["qc1"], lambda q: q.quantize_mx(
             T.qc[:, 128:256], T.sc[:, 128:256], T.gk[:, 512:1024]))
-        for b in range(4):
-            run("v", ["up"], ["down%d" % b], lambda q: q.memset(T.va[:, 2 * S * b + S + 4:2 * S * b + 2 * S:5], -BIG))
-        unit_tiles(1, "gm")
 
     half = (2 ** PL - 1) / 2
     sent = 0
@@ -267,15 +280,25 @@ def rank_program(g, core, T, topo):
         qx, sx = T["qx%d" % t], T["sx%d" % t]
         kx = ["qx%d0" % t, "qx%d1" % t]
         la, las = T["la%d" % t], T["las%d" % t]
-        for h in range(2):
-            a, z = 128 * h, 128 * h + 128
+
+        def planes_of(h):
+            a, z = O + 128 * h, O + 128 * h + 128
             run("t", ["qwb", kx[h]], ["b%d" % (2 * h)], lambda q: q.matmul_mx(
                 bank(2 * h, 0, 128), T.qwb[:, 8 * t:8 * t + 128], T.swb[:, 8 * t:8 * t + 128],
                 qx[:, a:z], sx[:, a:z], True, True))
+
+        def strengths_of(h):
+            a, z = O + 128 * h, O + 128 * h + 128
             run("t", ["ws%d" % t, "wss%d" % t, kx[h]], ["b%d" % (1 + 2 * h)], lambda q: q.matmul_mx(
                 bank(1 + 2 * h, 0, 128), T["ws%d" % t][:], T["wss%d" % t][:], qx[:, a:z], sx[:, a:z], True, False))
-        run("v", ["b0", "bqa"], ["bq0"], lambda q: q.tensor_scalar(
-            T.bq[:, 0:512:4], bank(0, 0, 128), 0.0, 0.5, A.is_lt, A.subtract))
+
+        for call, h in (((planes_of, 0), (planes_of, 1), (strengths_of, 0), (strengths_of, 1)) if t == 0 else
+                        ((planes_of, 0), (strengths_of, 0), (planes_of, 1), (strengths_of, 1))):
+            call(h)
+        run("s", ["b0", "bqa", "tiny"], ["bq0"], lambda q: q.activation(
+            T.bq[:, 0:512:4], bank(0, 0, 128), F.Sign, bias=T.tiny[:], scale=-1.0))
+        if t == 0:
+            fill("bqp", T.bq[64:128, 4 * NC:4 * NC + 8:4], 2, PAD, ["bqc"], 64, 128)
         run("s", ["b2", "bqc", "tiny"], ["bq1"], lambda q: q.activation(
             T.bq[:, 512:4 * NC:4], bank(2, 0, H), F.Sign, bias=T.tiny[:], scale=-1.0))
         for h in range(2):
@@ -286,57 +309,66 @@ def rank_program(g, core, T, topo):
             a, z = 128 * h, 128 * h + 128
             e, es = const(0)
             run("t", ["qc0", "qb%d" % h], ["b%d" % (1 + 2 * h)], lambda q: q.matmul_mx(
-                bank(1 + 2 * h, 0, 128), e, es, T.qb[:, a:z], T.sb[:, a:z], False, True))
+                bank(1 + 2 * h, 0, 128), e, es, T.qb[:, a:z], T.sb[:, a:z], False, True), True)
         run("v", ["b1", "wbz"], ["rm0"], lambda q: q.tensor_tensor_scan(
             T.rm[:, 0:128], bank(1, 0, 128), T.wb[:, 128:256], FLOOR, A.max, A.add))
-        run("v", ["b3", "wbz", "rm0"], ["rm1"], lambda q: q.tensor_tensor_scan(
-            T.rm[:, 128:NC + 2], bank(3, 0, H + 2), T.wb[:, 128:128 + H + 2], T.rm[:, 127:128], A.max, A.add))
-        run("s", ["rm0", "rm1"], ["sg", "ix"], lambda q: q.activation(
-            T.sg[:], T.rm[:, 0:NC], F.Sign, bias=T.rm[:, NC:NC + 1], scale=-1.0, accum_out=T.ix[:, 0:1]))
-        if t == 0:
-            unit_tiles(0, "g8", (0, 1))
+        run("v", ["b3", "wbz"], ["rm1"], lambda q: q.tensor_tensor_scan(
+            T.rm[:, 128:NC + 2], bank(3, 0, H + 2), T.wb[:, 128:128 + H + 2], FLOOR, A.max, A.add))
+        run("s", ["rm0"], ["sg0", "ix0"], lambda q: q.activation(
+            T.sg[:, 0:128], T.rm[:, 0:128], F.Sign, bias=T.rm[:, 127:128], scale=-1.0, accum_out=T.ix[:, 0:1]))
+        run("s", ["rm1"], ["sg1", "ix1"], lambda q: q.activation(
+            T.sg[:, 128:NC], T.rm[:, 128:NC], F.Sign, bias=T.rm[:, NC:NC + 1], scale=-1.0, accum_out=T.ix[:, 1:2]))
+        run("v", ["rm0", "rm1"], ["ix2"], lambda q: q.tensor_scalar(
+            T.ix[:, 2:3], T.rm[:, 127:128], T.rm[:, NC:NC + 1], O + 128.0, A.is_lt, A.mult))
+        run("v", ["ix0"], ["ix3"], lambda q: q.tensor_scalar(T.ix[:, 3:4], T.ix[:, 0:1], float(O), None, A.add))
         of = T["of%d" % t]
         ko = ["of%d%d" % (t, i) for i in range(3)]
-        run("v", ["ix"], ko[0:1], lambda q: q.tensor_copy(of[:, 0:1], T.ix[:, 0:1]))
-        run("v", ["ix"], ko[1:2], lambda q: q.tensor_copy(of[0:64, 1:2], T.ix[64:128, 0:1]))
-        run("v", ["ix"], ko[2:3], lambda q: q.tensor_copy(of[64:128, 1:2], T.ix[0:64, 0:1]))
+        for key, out, a, z in ((ko[0], of[:, 0:1], 0, 128), (ko[1], of[0:64, 1:2], 64, 128),
+                               (ko[2], of[64:128, 1:2], 0, 64)):
+            run("v", ["ix1", "ix2", "ix3"], [key], lambda q: q.tensor_scalar(
+                out, T.ix[a:z, 1:2], T.ix[a:z, 2:3], T.ix[a:z, 3:4], A.add, A.max))
         rep, reps = la[:, L * mine:L * mine + L], las[:, L * mine:L * mine + L]
         run("s", kx + ko, ["reps%d" % t], lambda q: q.activation(reps, sx[:].indirect(of[:]), F.Copy))
         run("v", kx + ko, ["rep%d" % t], lambda q: q.tensor_copy(
             rep.bitcast(u32), qx[:].bitcast(u32).indirect(of[:])))
-        for kind, to, helpers in CALLS:
-            need("g", [("rep%d" if kind == "c" else "reps%d") % t], [])
-            src = rep.bitcast(u8) if kind == "c" else reps
+        lands = [k for piece, to in HELPERS[t].values() for a, k in to]
+        for call in PLAN[t]:
+            need("g", [("rep%d" if call[0][0][0] == "c" else "reps%d") % t], [])
             transfers = []
-            if helpers:
+            for piece, which, to in call:
+                src = _view(T, "la", t, piece, L * mine)
+                if to[0] not in HELPERS[t]:
+                    transfers.append(_write(T, topo, core, t, piece, src, to, planes, mine, me))
+                    sent += n_off
+                    lands += [k for a, k in to]
+                    continue
                 ids = []
-                for h in helpers:
+                for h in to:
                     rid, pid = topo.addr(able[h], core)
                     ids.append(DstId(rid=rid, pnc=pid))
-                mask, n = _hand_over(topo, core, able[helpers[0]], mate, t, not to)
+                engines = _hand_over(topo, core, able[to[0]], mate, which)
                 transfers.append(RemoteDMATransfer(
-                    dst_ids=ids, dma_engine_mask=mask, remote_sem=T.sem["hand%d" % t], srcs=[src],
-                    dsts=[_handed(T, t, kind)] * len(ids)))
-                sent += n
-            if to:
-                transfers.append(_write(T, topo, core, t, kind, src, to, planes, mine, me))
-                sent += n_off
+                    dst_ids=ids, dma_engine_mask=sum(1 << e for e in engines), remote_sem=T.sem["hand%d" % t],
+                    srcs=[src], dsts=[_view(T, "hd", t, piece, 0)] * len(ids)))
+                sent += len(engines)
             g.remote_dma_fused(transfers, local_sem=T.sem.sent)
-        arrive(("near%d" % t, 2 * 3 * n_off), ["near%d" % t])
-        arrive(("late%d" % t, 2 * 4 * n_off), ["late%d" % t])
+        arrive(("near%d" % t, sum(k < 2 for k in lands) * n_off), ["near%d" % t])
+        arrive(("late%d" % t, sum(k >= 2 for k in lands) * n_off), ["late%d" % t])
         if t == 0:
             first_constants()
         e, es = const(1)
         run("t", ["qc1", "qb0", "qb1"], ["b7"], lambda q: q.matmul_mx(
             bank(7, 0, NC), e, es, T.qb[:, 0:NC], T.sb[:, 0:NC], True, True))
-        run("s", ["b7"], ["lt0"], lambda q: q.activation(T.lt[:, 0:128], bank(7, 0, 128), F.Copy))
-        run("s", ["b7"], ["lt1"], lambda q: q.activation(T.lt[:, 128:NC], bank(7, 128, NC), F.Copy, scale=0.5))
-        run("s", ["lt0", "lt1"], ["lvs%d" % t], lambda q: q.activation(
-            T.lvs[0:1, NC * t:NC * t + NC], T.lt[0:1, :], F.Identity, bias=half))
-        dma("y", "dlv", 16 * (t + 1), ["lvs%d" % t, "late%d" % t], [], T.lv[t:t + 1, :], T.lvs[0:1, NC * t:NC * t + NC])
         ov, hn = T["ov%d" % t], T["h%d" % (t + 1)]
-        run("v", [], ["hp%d" % (t + 1)], lambda q: q.memset(hn[:, 4 * NC:4 * W], 0.0))
-        run("v", ["lt0", "lt1", "dg"], ["ld"], lambda q: q.tensor_tensor(T.ld[:], T.lt[:], T.dg[:], A.mult))
+        run("v", ["dg"], ["b7", "ld"], lambda q: q.tensor_tensor(T.ld[:], bank(7, 0, NC), T.dg[:], A.mult))
+        if t == 0:
+            unit_tiles(1, "gm")
+        run("s", [], ["b7", "lvs%d" % t], lambda q: q.activation(
+            T.lvs[0:1, NC * t:NC * t + NC], T.px[0:1, 1536:1536 + NC], F.Identity, bias=half, scale=0.5))
+        dma("y", "dlv", 16 * (t + 1), ["lvs%d" % t, "late%d" % t], [], T.lv[t:t + 1, :], T.lvs[0:1, NC * t:NC * t + NC])
+        if t == 0:
+            dma("y", "dz", 32, ["late0"], ["zt"], T.zt[:], T.z[:])
+        fill("hp%d" % (t + 1), hn[:, 4 * NC:4 * W], 4 * W - 4 * NC, 0.0)
         if t + 1 < R:
             run("v", [], ["wl%d" % (t + 1)], lambda q: q.memset(T["wl%d" % (t + 1)][:], 8 * (t + 1) + 6))
         run("v", ["ld", "m16", "m16z"], ["ls"], lambda q: q.tensor_tensor_scan(
@@ -344,13 +376,13 @@ def rank_program(g, core, T, topo):
         if t + 1 < R:
             strength_tile(t + 1)
         run("v", ["ls"], ["ov%d" % t], lambda q: q.tensor_scalar(
-            ov[:], T.ls[:, 15:NC:16], 5.0, 5.0 * half + 3.0, A.mult, A.add))
-        if t == 1:
+            ov[:], T.ls[:, 15:NC:16], 2.5, 5.0 * half + 3.0, A.mult, A.add))
+        if t == R - 1:
             run("v", ["zt"], ["qz"], lambda q: q.quantize_mx(T.qz[:], T.sz[:], T.zt[:]))
 
-        order = ((1, "v"), (0, "s"), (3, "v"), (2, "s"))
         for h, keys in enumerate((["rep%d" % t, "reps%d" % t, "near%d" % t], ["late%d" % t])):
             o = 4 * L * h
+            order = ((1, "v"), (0, "s"), (3, "v"), (2, "s"))
             for b, engine in order:
                 e, es = unit(0, b)
                 run("t", ["e0%d" % b] + keys, ["b%d" % (b + 4 * h)], lambda q: q.matmul_mx(
@@ -363,7 +395,7 @@ def rank_program(g, core, T, topo):
                         run("s", ["b%d" % k], ["va%d%d" % (b, i)], lambda q: q.activation(out, in_, F.Copy))
                     else:
                         run("v", ["b%d" % k], ["va%d%d" % (b, i)], lambda q: q.tensor_copy(out, in_))
-        for h, a in enumerate((0, H)):
+        for h, a in enumerate((O, O + H)):
             for b, engine in order:
                 e, es = unit(0, b)
                 run("t", ["e0%d" % b] + kx, ["b%d" % (b + 4 * h)], lambda q: q.matmul_mx(
@@ -386,7 +418,7 @@ def rank_program(g, core, T, topo):
             for b in range(4):
                 e, es = unit(1, b)
                 run("t", ["e1%d" % b] + keys, ["b%d" % (b + 4 * h)], lambda q: q.matmul_mx(
-                    bank(b + 4 * h, 0, 128), e, es, vv[:, a:a + 128], vvs[:, a:a + 128], False, True))
+                    bank(b + 4 * h, 0, 128), e, es, vv[:, a:a + 128], vvs[:, a:a + 128], False, True), True)
 
         def cast(h, b, engine):
             k, key = b + 4 * h, "h%d%d%d" % (t + 1, h, b)
@@ -398,25 +430,25 @@ def rank_program(g, core, T, topo):
 
         for b in range(4):
             cast(0, b, "sv"[b % 2])
-        for b in range(3):
-            cast(1, b, "s")
+        for b in range(4):
+            cast(1, b, "svss"[b])
         pack(t + 1, 0, ["h%d0%d" % (t + 1, b) for b in range(4)])
-        cast(1, 3, "v")
         pack(t + 1, 1, ["h%d1%d" % (t + 1, b) for b in range(4)] + ["hp%d" % (t + 1)])
 
     qx, sx = T["qx%d" % R], T["sx%d" % R]
     kx = ["qx%d0" % R, "qx%d1" % R]
     for h in range(2):
+        a, z = O + 128 * h, O + 128 * h + 128
         run("t", ["qz", kx[h]], ["b%d" % h], lambda q: q.matmul_mx(
-            bank(h, 0, 128), T.qz[:], T.sz[:], qx[:, 128 * h:128 * h + 128], sx[:, 128 * h:128 * h + 128], True, True))
+            bank(h, 0, 128), T.qz[:], T.sz[:], qx[:, a:z], sx[:, a:z], True, True))
     total = 16 * 7
-    dma("y", "dout", total, kx[0:1], [], T.oc[:, 0:512], qx[:, 0:128].bitcast(u8))
-    dma("y", "dout", total, kx[1:2], [], T.oc[:, 512:4 * NC], qx[:, 128:NC].bitcast(u8))
-    run("s", ["b0"], ["ysb0"], lambda q: q.activation(T.ysb[:, 0:128], bank(0, 0, 128), F.Copy))
+    dma("y", "dout", total, kx, [], T.oc[:], qx[:, O:O + NC].bitcast(u8))
+    run("v", ["b0"], ["ysb0"], lambda q: q.tensor_copy(T.ysb[:, 0:128], bank(0, 0, 128)))
     run("v", ["b1"], ["ysb1"], lambda q: q.tensor_copy(T.ysb[:, 128:NC], bank(1, 0, H)))
+    dma("y", "dout", total, ["ysb0"], [], T.y[:, 0:128], T.ysb[:, 0:128])
+    dma("y", "dout", total, ["ysb1"], [], T.y[:, 128:NC], T.ysb[:, 128:NC])
     for k in range(4):
-        dma("s", "dout", total, kx, [], T.osc[4 * k:4 * k + 4, :], sx[32 * k:32 * k + 4, 0:NC])
-    dma("y", "dout", total, ["ysb0", "ysb1"], [], T.y[:], T.ysb[:])
+        dma("s", "dout", total, kx, [], T.osc[4 * k:4 * k + 4, :], sx[32 * k:32 * k + 4, O:O + NC])
     wait("g", ("sent", sent))
     finish("g")
     wait("g", ("dlv", 16 * R))

from concourse.bass import DstId, RemoteDMATransfer
from concourse.mybir import dt, AluOpType, ActivationFunctionType

NC, L, R, PL = 192, 32, 3, 5
W = 256
H = NC - 128
O = 128
S = 5 * L
P, FLOOR, PAD, BIG, TINY = 2.0 ** 76, -2.0 ** 74, -2.0 ** -5, 2.0 ** 61, 2.0 ** -120
X4, BF, F32, U8, I32, U16 = "float8_e4m3fn_x4", "bfloat16", "float32", "uint8", "int32", "uint16"

NEAR, SAME, OTHER = ((0, 1), (1, 1), (1, 0)), ((0, 2), (0, 3)), ((1, 2), (1, 3))
CODES, SCALES = ("c", 0, L), ("s", 0, L)
PLAN = [(((CODES, "in", (1, 3)),), ((SCALES, "out", NEAR), (SCALES, "in", (2, 0, 4))), ((CODES, "out", NEAR),),
         ((CODES, "out", SAME[1:]),))]
PLAN += [(((CODES, "all", (1, 4, 3)),), ((SCALES, "out", NEAR), (SCALES, "in", (2, 0))), ((CODES, "out", NEAR),),
          ((SCALES, "out", SAME[1:]),))] * (R - 1)
HELPERS = [{0: (SCALES, SAME[:1]), 1: (CODES, OTHER), 2: (SCALES, OTHER), 3: (CODES, SAME[:1]), 4: (SCALES, SAME[1:])}]
HELPERS += [{0: (SCALES, SAME[:1]), 1: (CODES, OTHER), 2: (SCALES, OTHER), 3: (CODES, SAME[1:]),
             4: (CODES, SAME[:1])}] * (R - 1)

SCRATCH = {"pv": ("psum", [128, 2048], F32), "px": ("psum", [128, 2048], F32)}
for _n, _w, _d in (
        ("wb", 648, BF), ("zt", 512, BF), ("qwb", 144, X4), ("swb", 144, U8), ("qz", 128, X4), ("sz", 128, U8),
        ("g8", 520, BF), ("gm", 520, BF),
        ("qe", 8 * 128, X4), ("se", 8 * 128, U8), ("u", 256, BF), ("ut", 256, BF), ("gk", 1024, BF),
        ("qc", 256, X4), ("sc", 256, U8), ("bq", 4 * W, BF), ("qb", W, X4), ("sb", W, U8),
        ("m16", NC, BF), ("idg", NC, I32), ("idh", NC, I32), ("dg", NC, BF),
        ("jb", 16, I32), ("jm", 16, I32), ("tiny", 1, F32),
        ("rm", NC + 2, F32), ("sg", NC, BF), ("ix", 4, F32),
        ("ld", NC, BF), ("ls", NC, BF), ("lvs", R * NC, F32),
        ("va", 8 * S, BF), ("vs", 4 * S, BF), ("ysb", NC, F32)):
    SCRATCH[_n] = ("sbuf", [128, _w], _d)
for _t in range(R + 1):
    SCRATCH["h%d" % _t] = ("sbuf", [128, 4 * W], BF)
    SCRATCH["qx%d" % _t] = ("sbuf", [128, O + W], X4)
    SCRATCH["sx%d" % _t] = ("sbuf", [128, O + W], U8)
for _t in range(R):
    for _n, _w in (("ws", 128), ("la", 8 * L), ("hd", L), ("qv", S), ("vv", NC)):
        SCRATCH["%s%d" % (_n, _t)] = ("sbuf", [128, _w], X4)
        SCRATCH["%ss%d" % (_n, _t)] = ("sbuf", [128, _w], U8)
    SCRATCH["wl%d" % _t] = ("sbuf", [128, 8], U16)
    SCRATCH["of%d" % _t] = ("sbuf", [128, 2], U16)
    SCRATCH["ov%d" % _t] = ("sbuf", [128, 12], U16)

SEMAPHORES = ["cv", "cs", "ct", "cg", "dx0", "dx1", "dw", "dz", "dlv", "dout", "sent"]
SEMAPHORES += ["%s%d" % (_n, _t) for _n in ("near", "late", "hand") for _t in range(R)]

COUNTER = {"v": "cv", "s": "cs", "t": "ct", "g": "cg"}


def _scheduler(g, T):
    queue = {"v": g.vector, "s": g.scalar, "t": g.tensor, "g": g, "y": g.sync}
    count = {"cv": 0, "cs": 0, "ct": 0, "cg": 0}
    clock = {q: {} for q in queue}
    known = {}
    writer, readers = {}, {}

    def wait(q, token):
        name, value = token
        if clock[q].get(name, 0) >= value:
            return
        queue[q].wait_ge(T.sem[name], value)
        for n, v in list(known.get(token, {}).items()) + [token]:
            clock[q][n] = max(clock[q].get(n, 0), v)

    def need(q, reads, writes):
        tokens = {}
        own = COUNTER.get(q)
        for k in list(reads) + list(writes):
            if k in writer:
                n, v = writer[k]
                tokens[n] = max(tokens.get(n, 0), v)
        for k in writes:
            for n, v in readers.get(k, []):
                if n != own:
                    tokens[n] = max(tokens.get(n, 0), v)
        for n in sorted(tokens):
            wait(q, (n, tokens[n]))

    def note(q, token, reads, writes):
        known[token] = dict(clock[q])
        for k in reads:
            readers.setdefault(k, []).append(token)
        for k in writes:
            writer[k] = token
            readers[k] = []

    def run(q, reads, writes, call, adds=False):
        need(q, reads, [] if adds else writes)
        name = COUNTER[q]
        call(queue[q]).then_inc(T.sem[name], 1)
        count[name] += 1
        note(q, (name, count[name]), reads, writes)

    def dma(q, sem, value, reads, writes, out, in_):
        need(q, reads, writes)
        queue[q].dma_start(out, in_).then_inc(T.sem[sem], 16)
        note(q, (sem, value), reads, writes)

    def arrive(token, writes):
        for k in writes:
            writer[k] = token
            readers[k] = []

    def finish(q):
        for name in sorted(count):
            if count[name]:
                wait(q, (name, count[name]))

    return run, dma, need, wait, arrive, finish


def _places(T, topo, core):
    cores = list(T.cores)
    first = [c for c in cores if c == cores[0] or topo.same_plane(c, cores[0])]
    planes = [first, [c for c in cores if c not in first]]
    for a in range(2):
        for i in range(4):
            assert planes[a][i] == cores[2 * i + a]
    mine = 0 if core in first else 1
    able = [c for c in topo.cores_of(core) if c != core and all(topo.may_write(c, d) for d in cores)]
    able.sort(key=lambda c: topo.die(c) != topo.die(core))
    able += [c for c in topo.cores_of(core) if c != core and c not in able and topo.die(c) == topo.die(core)]
    able += [c for c in topo.cores_of(core) if c != core and c not in able]
    return planes, mine, planes[mine].index(core), able


def _view(T, name, t, piece, o):
    kind, a, z = piece
    if kind == "c":
        return T["%s%d" % (name, t)][:, o + a:o + z].bitcast(dt.uint8)
    return T["%ss%d" % (name, t)][:, o + a:o + z]


def _write(T, topo, core, t, piece, src, to, planes, mine, me):
    ids, dsts = [], []
    for a, k in to:
        far = planes[(mine + a) % 2][(me + k) % 4]
        rid, pid = topo.addr(far, core)
        ids.append(DstId(rid=rid, pnc=pid))
        dsts.append(_view(T, "la", t, piece, L * (2 * k + mine)))
    sem = T.sem[("near%d" if to[0][1] < 2 else "late%d") % t]
    return RemoteDMATransfer(dst_ids=ids, dma_engine_mask=topo.mask(core, far), remote_sem=sem, srcs=[src], dsts=dsts)


def _hand_over(topo, core, helper, far, which):
    out = topo.engines(core, far)
    inner = [e for e in topo.engines(core, helper) if e not in out]
    n = len(inner) // 2
    return {"all": out + inner, "out": out, "in": inner, "in0": inner[:n], "in1": inner[n:]}[which]


def _hand_on(g, core, T, topo):
    ranks = [c for c in topo.cores_of(core) if T.rank_of(c) is not None]
    if not ranks:
        return
    planes, mine, me, able = _places(T, topo, ranks[0])
    if able.index(core) not in HELPERS[0]:
        return
    far = planes[mine][(me + 1) % 4]
    for t, calls in enumerate(PLAN):
        piece, to = HELPERS[t][able.index(core)]
        which = [move[1] for call in calls for move in call if able.index(core) in move[2]][0]
        g.wait_ge(T.sem["hand%d" % t], len(_hand_over(topo, ranks[0], core, far, which)))
        g.remote_dma_fused([_write(T, topo, core, t, piece, _view(T, "hd", t, piece, 0), to, planes, mine, me)],
                           local_sem=T.sem.sent)
    g.wait_ge(T.sem.sent, R * len(topo.engines(core, far)))


def rank_program(g, core, T, topo):
    if T.rank_of(core) is None:
        _hand_on(g, core, T, topo)
        return
    A, F = AluOpType, ActivationFunctionType
    run, dma, need, wait, arrive, finish = _scheduler(g, T)
    u8, u32 = dt.uint8, dt.uint32
    planes, mine, me, able = _places(T, topo, core)
    mate = planes[1 - mine][me]
    n_off = len(topo.engines(core, mate))

    def bank(k, a, z):
        return (T.pv if k < 4 else T.px)[:, 512 * (k % 4) + a:512 * (k % 4) + z]

    def fill(key, out, n, value, after=(), a=0, z=128):
        zeros = T.wb[a:z, 128:128 + n]
        if value:
            run("s", ["wbz"] + list(after), [key], lambda q: q.activation(out, zeros, F.Identity, bias=value))
        else:
            run("s", ["wbz"] + list(after), [key], lambda q: q.activation(out, zeros, F.Copy))

    dma("y", "dx0", 16, [], ["h00"], T.h0[:, 0:512], T.x[:, 0:512])
    dma("s", "dw", 16, [], ["wb"], T.wb[:, 32:128], T.w[:, 0:96])
    dma("y", "dx1", 16, [], ["h01"], T.h0[:, 512:4 * NC], T.x[:, 512:4 * NC])
    for i in (2, 3):
        run("g", [], ["jb%d" % i], lambda q: q.iota(T.jb[0:32, 4 * i:4 * i + 4], [[0, 4]], 0, 8 >> i))
    run("g", [], ["hp0"], lambda q: q.iota(
        T.h0[:, 4 * NC:4 * W], [[0, 4 * W - 4 * NC]], 0, 0, allow_small_or_imprecise_dtypes=True))

    def const(k):
        return T.qc[:, 128 * k:128 * k + 128], T.sc[:, 128 * k:128 * k + 128]

    us = ["u%d" % i for i in range(PL + 1)]
    run("v", [], ["wbz"], lambda q: q.memset(T.wb[:, 128:648], 0.0))
    run("v", [], ["u"], lambda q: q.memset(T.u[0:32, 0:128], 0.0))
    run("g", ["wbz"], ["g8"], lambda q: q.affine_select(
        T.g8[:], T.wb[:, 128:648], [[-1, 520]], A.not_equal, 0.125, 4, 4))
    fill("gka", T.gk[:, 0:512], 512, 0.0)
    fill("bqa", T.bq[:, 0:512], 512, 0.0)
    dma("y", "dz", 16, ["wbz"], ["bqc"], T.bq[:, 512:1024], T.wb[:, 128:640])
    run("v", [], ["wl0"], lambda q: q.memset(T.wl0[:], 6))
    run("v", ["jb2", "jb3"], ["jb0"], lambda q: q.tensor_scalar(T.jb[0:32, 0:8], T.jb[0:32, 8:16], 4.0, None, A.mult))
    run("v", ["u"], ["u4"], lambda q: q.memset(T.u[0:32, 4:64:32], -P))
    run("v", ["jb0", "jb2", "jb3"], ["jm"], lambda q: q.tensor_scalar(
        T.jm[0:32, :], T.jb[0:32, :], 8, None, A.bitwise_and))
    run("v", ["u"], ["u5"], lambda q: q.memset(T.u[0:32, 68:128:32], P))
    for i in range(PL - 1):
        run("v", ["jm", "u"], ["u%d" % i], lambda q: q.tensor_scalar(
            T.u[0:32, i:128:32], T.jm[0:32, 4 * i:4 * i + 4], 2 * P / 8, P, A.mult, A.subtract))
    run("v", ["gka"], ["gk1"], lambda q: q.memset(T.gk[64:128, 0:512:4], P * PL / 64))
    run("v", ["u"] + us, ["ut"], lambda q: q.transpose(T.ut[0:32, 0:128], T.u[0:32, 0:128]))
    run("s", ["ut", "gka"], ["gk0"], lambda q: q.activation(T.gk[0:32, 0:512:4], T.ut[0:32, 0:128], F.Copy))
    run("v", ["wb", "wbz"], ["qwb"], lambda q: q.quantize_mx(T.qwb[:], T.swb[:], T.wb[:, 32:608]))

    def strength_tile(t):
        ws, wss, wl = T["ws%d" % t], T["wss%d" % t], T["wl%d" % t]
        run("s", ["qwb", "wl%d" % t], ["wss%d" % t], lambda q: q.activation(
            wss[:], T.swb[:].indirect(wl[:]), F.Copy))
        run("v", ["qwb", "wl%d" % t], ["ws%d" % t], lambda q: q.tensor_copy(
            ws[:].bitcast(u32), T.qwb[:].bitcast(u32).indirect(wl[:])))

    def pack(t, h, keys):
        run("v", keys, ["qx%d%d" % (t, h)], lambda q: q.quantize_mx(
            T["qx%d" % t][:, O + 128 * h:O + 128 * h + 128], T["sx%d" % t][:, O + 128 * h:O + 128 * h + 128],
            T["h%d" % t][:, 512 * h:512 * h + 512]))

    fill("tiny", T.tiny[:], 1, -TINY)
    pack(0, 0, ["h00"])
    pack(0, 1, ["h01", "hp0"])
    run("v", ["gk0", "gk1", "gka"], ["qc0"], lambda q: q.quantize_mx(T.qc[:, 0:128], T.sc[:, 0:128], T.gk[:, 0:512]))
    strength_tile(0)
    run("g", [], ["idg"], lambda q: q.iota(T.idg[:], [[1, NC]], 128, -1))

    def unit_tiles(s, name, which=(0, 1, 2, 3)):
        src = T[name]
        for b in which:
            o = 128 * (4 * s + b)
            run("v", [name], ["e%d%d" % (s, b)], lambda q: q.quantize_mx(
                T.qe[:, o:o + 128], T.se[:, o:o + 128], src[:, 4 - b:516 - b]))

    def unit(s, b):
        o = 128 * (4 * s + b)
        return T.qe[:, o:o + 128], T.se[:, o:o + 128]

    def first_constants():
        ns = ["n%d" % i for i in range(PL + 1)]
        fill("uz", T.u[0:32, 128:256], 128, 0.0, (), 0, 32)
        fill("gkc", T.gk[:, 512:1024], 512, 0.0)
        for i in range(PL - 1):
            fill(ns[i], T.u[0:32, 128 + i:256:32], 4, 2.0 ** i, ["uz"], 0, 32)
        fill(ns[4], T.u[0:32, 132:192:32], 2, 16.0, ["uz"], 0, 32)
        fill(ns[5], T.u[0:32, 196:256:32], 2, -16.0, ["uz"], 0, 32)
        fill("up", T.va[:, 4:8 * S:5], 8 * L, BIG)
        for b in range(4):
            fill("down%d" % b, T.va[:, 2 * S * b + S + 4:2 * S * b + 2 * S:5], L, -BIG, ["up"])
        run("s", ["g8"], ["gm"], lambda q: q.activation(T.gm[:], T.g8[:], F.Copy, scale=-0.5))
        fill("m16", T.m16[:], NC, 1.0)
        fill("m16z", T.m16[:, 0:NC:16], NC // 16, 0.0, ["m16"])
        unit_tiles(0, "g8")
        run("v", ["idg"], ["idh"], lambda q: q.tensor_scalar(T.idh[:], T.idg[:], 15, None, A.bitwise_and))
        run("v", ["uz"] + ns, ["un"], lambda q: q.transpose(T.ut[0:32, 128:256], T.u[0:32, 128:256]))
        run("v", ["idh"], ["dg"], lambda q: q.tensor_scalar(T.dg[:], T.idh[:], 0.0, None, A.is_equal))
        run("v", ["un", "gkc"], ["gk2"], lambda q: q.tensor_copy(T.gk[0:32, 512:1024:4], T.ut[0:32, 128:256]))
        run("v", ["gk2", "gkc"], ["qc1"], lambda q: q.quantize_mx(
            T.qc[:, 128:256], T.sc[:, 128:256], T.gk[:, 512:1024]))

    half = (2 ** PL - 1) / 2
    sent = 0
    for t in range(R):
        qx, sx = T["qx%d" % t], T["sx%d" % t]
        kx = ["qx%d0" % t, "qx%d1" % t]
        la, las = T["la%d" % t], T["las%d" % t]

        def planes_of(h):
            a, z = O + 128 * h, O + 128 * h + 128
            run("t", ["qwb", kx[h]], ["b%d" % (2 * h)], lambda q: q.matmul_mx(
                bank(2 * h, 0, 128), T.qwb[:, 8 * t:8 * t + 128], T.swb[:, 8 * t:8 * t + 128],
                qx[:, a:z], sx[:, a:z], True, True))

        def strengths_of(h):
            a, z = O + 128 * h, O + 128 * h + 128
            run("t", ["ws%d" % t, "wss%d" % t, kx[h]], ["b%d" % (1 + 2 * h)], lambda q: q.matmul_mx(
                bank(1 + 2 * h, 0, 128), T["ws%d" % t][:], T["wss%d" % t][:], qx[:, a:z], sx[:, a:z], True, False))

        for call, h in (((planes_of, 0), (planes_of, 1), (strengths_of, 0), (strengths_of, 1)) if t == 0 else
                        ((planes_of, 0), (strengths_of, 0), (planes_of, 1), (strengths_of, 1))):
            call(h)
        run("s", ["b0", "bqa", "tiny"], ["bq0"], lambda q: q.activation(
            T.bq[:, 0:512:4], bank(0, 0, 128), F.Sign, bias=T.tiny[:], scale=-1.0))
        if t == 0:
            fill("bqp", T.bq[64:128, 4 * NC:4 * NC + 8:4], 2, PAD, ["bqc"], 64, 128)
        run("s", ["b2", "bqc", "tiny"], ["bq1"], lambda q: q.activation(
            T.bq[:, 512:4 * NC:4], bank(2, 0, H), F.Sign, bias=T.tiny[:], scale=-1.0))
        for h in range(2):
            a, z = 128 * h, 128 * h + 128
            run("v", ["bq%d" % h] + ["bqp"] * h, ["qb%d" % h], lambda q: q.quantize_mx(
                T.qb[:, a:z], T.sb[:, a:z], T.bq[:, 4 * a:4 * z]))
        for h in range(2):
            a, z = 128 * h, 128 * h + 128
            e, es = const(0)
            run("t", ["qc0", "qb%d" % h], ["b%d" % (1 + 2 * h)], lambda q: q.matmul_mx(
                bank(1 + 2 * h, 0, 128), e, es, T.qb[:, a:z], T.sb[:, a:z], False, True), True)
        run("v", ["b1", "wbz"], ["rm0"], lambda q: q.tensor_tensor_scan(
            T.rm[:, 0:128], bank(1, 0, 128), T.wb[:, 128:256], FLOOR, A.max, A.add))
        run("v", ["b3", "wbz"], ["rm1"], lambda q: q.tensor_tensor_scan(
            T.rm[:, 128:NC + 2], bank(3, 0, H + 2), T.wb[:, 128:128 + H + 2], FLOOR, A.max, A.add))
        run("s", ["rm0"], ["sg0", "ix0"], lambda q: q.activation(
            T.sg[:, 0:128], T.rm[:, 0:128], F.Sign, bias=T.rm[:, 127:128], scale=-1.0, accum_out=T.ix[:, 0:1]))
        run("s", ["rm1"], ["sg1", "ix1"], lambda q: q.activation(
            T.sg[:, 128:NC], T.rm[:, 128:NC], F.Sign, bias=T.rm[:, NC:NC + 1], scale=-1.0, accum_out=T.ix[:, 1:2]))
        run("v", ["rm0", "rm1"], ["ix2"], lambda q: q.tensor_scalar(
            T.ix[:, 2:3], T.rm[:, 127:128], T.rm[:, NC:NC + 1], O + 128.0, A.is_lt, A.mult))
        run("v", ["ix0"], ["ix3"], lambda q: q.tensor_scalar(T.ix[:, 3:4], T.ix[:, 0:1], float(O), None, A.add))
        of = T["of%d" % t]
        ko = ["of%d%d" % (t, i) for i in range(3)]
        for key, out, a, z in ((ko[0], of[:, 0:1], 0, 128), (ko[1], of[0:64, 1:2], 64, 128),
                               (ko[2], of[64:128, 1:2], 0, 64)):
            run("v", ["ix1", "ix2", "ix3"], [key], lambda q: q.tensor_scalar(
                out, T.ix[a:z, 1:2], T.ix[a:z, 2:3], T.ix[a:z, 3:4], A.add, A.max))
        rep, reps = la[:, L * mine:L * mine + L], las[:, L * mine:L * mine + L]
        run("s", kx + ko, ["reps%d" % t], lambda q: q.activation(reps, sx[:].indirect(of[:]), F.Copy))
        run("v", kx + ko, ["rep%d" % t], lambda q: q.tensor_copy(
            rep.bitcast(u32), qx[:].bitcast(u32).indirect(of[:])))
        lands = [k for piece, to in HELPERS[t].values() for a, k in to]
        for call in PLAN[t]:
            need("g", [("rep%d" if call[0][0][0] == "c" else "reps%d") % t], [])
            transfers = []
            for piece, which, to in call:
                src = _view(T, "la", t, piece, L * mine)
                if to[0] not in HELPERS[t]:
                    transfers.append(_write(T, topo, core, t, piece, src, to, planes, mine, me))
                    sent += n_off
                    lands += [k for a, k in to]
                    continue
                ids = []
                for h in to:
                    rid, pid = topo.addr(able[h], core)
                    ids.append(DstId(rid=rid, pnc=pid))
                engines = _hand_over(topo, core, able[to[0]], mate, which)
                transfers.append(RemoteDMATransfer(
                    dst_ids=ids, dma_engine_mask=sum(1 << e for e in engines), remote_sem=T.sem["hand%d" % t],
                    srcs=[src], dsts=[_view(T, "hd", t, piece, 0)] * len(ids)))
                sent += len(engines)
            g.remote_dma_fused(transfers, local_sem=T.sem.sent)
        arrive(("near%d" % t, sum(k < 2 for k in lands) * n_off), ["near%d" % t])
        arrive(("late%d" % t, sum(k >= 2 for k in lands) * n_off), ["late%d" % t])
        if t == 0:
            first_constants()
        e, es = const(1)
        run("t", ["qc1", "qb0", "qb1"], ["b7"], lambda q: q.matmul_mx(
            bank(7, 0, NC), e, es, T.qb[:, 0:NC], T.sb[:, 0:NC], True, True))
        ov, hn = T["ov%d" % t], T["h%d" % (t + 1)]
        run("v", ["dg"], ["b7", "ld"], lambda q: q.tensor_tensor(T.ld[:], bank(7, 0, NC), T.dg[:], A.mult))
        if t == 0:
            unit_tiles(1, "gm")
        run("s", [], ["b7", "lvs%d" % t], lambda q: q.activation(
            T.lvs[0:1, NC * t:NC * t + NC], T.px[0:1, 1536:1536 + NC], F.Identity, bias=half, scale=0.5))
        dma("y", "dlv", 16 * (t + 1), ["lvs%d" % t, "late%d" % t], [], T.lv[t:t + 1, :], T.lvs[0:1, NC * t:NC * t + NC])
        if t == 0:
            dma("y", "dz", 32, ["late0"], ["zt"], T.zt[:], T.z[:])
        fill("hp%d" % (t + 1), hn[:, 4 * NC:4 * W], 4 * W - 4 * NC, 0.0)
        if t + 1 < R:
            run("v", [], ["wl%d" % (t + 1)], lambda q: q.memset(T["wl%d" % (t + 1)][:], 8 * (t + 1) + 6))
        run("v", ["ld", "m16", "m16z"], ["ls"], lambda q: q.tensor_tensor_scan(
            T.ls[:], T.m16[:], T.ld[:], 0.0, A.mult, A.add))
        if t + 1 < R:
            strength_tile(t + 1)
        run("v", ["ls"], ["ov%d" % t], lambda q: q.tensor_scalar(
            ov[:], T.ls[:, 15:NC:16], 2.5, 5.0 * half + 3.0, A.mult, A.add))
        if t == R - 1:
            run("v", ["zt"], ["qz"], lambda q: q.quantize_mx(T.qz[:], T.sz[:], T.zt[:]))

        for h, keys in enumerate((["rep%d" % t, "reps%d" % t, "near%d" % t], ["late%d" % t])):
            o = 4 * L * h
            order = ((1, "v"), (0, "s"), (3, "v"), (2, "s"))
            for b, engine in order:
                e, es = unit(0, b)
                run("t", ["e0%d" % b] + keys, ["b%d" % (b + 4 * h)], lambda q: q.matmul_mx(
                    bank(b + 4 * h, 0, 4 * L), e, es, la[:, o:o + 4 * L], las[:, o:o + 4 * L], True, True))
            for b, engine in order:
                for j in range(2):
                    i, k = (me - 2 * h - j) % 4, b + 4 * h
                    out, in_ = T.va[:, 2 * S * b + i:2 * S * b + 2 * S:5], bank(k, 2 * L * j, 2 * L * j + 2 * L)
                    if engine == "s":
                        run("s", ["b%d" % k], ["va%d%d" % (b, i)], lambda q: q.activation(out, in_, F.Copy))
                    else:
                        run("v", ["b%d" % k], ["va%d%d" % (b, i)], lambda q: q.tensor_copy(out, in_))
        for h, a in enumerate((O, O + H)):
            for b, engine in order:
                e, es = unit(0, b)
                run("t", ["e0%d" % b] + kx, ["b%d" % (b + 4 * h)], lambda q: q.matmul_mx(
                    bank(b + 4 * h, 0, 128), e, es, qx[:, a:a + 128], sx[:, a:a + 128], True, False))
        for b, engine in order:
            o = 2 * S * b
            run("v", ["up", "down%d" % b] + ["va%d%d" % (b, i) for i in range(4)], ["vs%d" % b],
                lambda q: q.tensor_tensor_scan(
                    T.vs[:, b:4 * S:4], T.va[:, o:o + S], T.va[:, o + S:o + 2 * S], 0.0, A.add, A.add))
        qv, qvs = T["qv%d" % t], T["qvs%d" % t]
        run("v", ["vs0", "vs1", "vs2", "vs3"], ["qv%d" % t], lambda q: q.quantize_mx(qv[:], qvs[:], T.vs[:]))
        vv, vvs = T["vv%d" % t], T["vvs%d" % t]
        for h, (a, z) in enumerate(((0, 8), (8, 12))):
            run("s", ["qv%d" % t, "ov%d" % t], ["vvs%d%d" % (t, h)], lambda q: q.activation(
                vvs[:, 16 * a:16 * z], qvs[:].indirect(ov[:, a:z]), F.Copy))
            run("v", ["qv%d" % t, "ov%d" % t], ["vv%d%d" % (t, h)], lambda q: q.tensor_copy(
                vv[:, 16 * a:16 * z].bitcast(u32), qv[:].bitcast(u32).indirect(ov[:, a:z])))
        for h, a in enumerate((0, H)):
            keys = ["%s%d%d" % (k, t, j) for k in ("vv", "vvs") for j in range(h + 1)]
            for b in range(4):
                e, es = unit(1, b)
                run("t", ["e1%d" % b] + keys, ["b%d" % (b + 4 * h)], lambda q: q.matmul_mx(
                    bank(b + 4 * h, 0, 128), e, es, vv[:, a:a + 128], vvs[:, a:a + 128], False, True), True)

        def cast(h, b, engine):
            k, key = b + 4 * h, "h%d%d%d" % (t + 1, h, b)
            out, in_ = (hn[:, b:512:4], bank(k, 0, 128)) if h == 0 else (hn[:, 512 + b:4 * NC:4], bank(k, 128 - H, 128))
            if engine == "s":
                run("s", ["b%d" % k], [key], lambda q: q.activation(out, in_, F.Copy, scale=8.0))
            else:
                run("v", ["b%d" % k], [key], lambda q: q.tensor_scalar(out, in_, 8.0, None, A.mult))

        for b in range(4):
            cast(0, b, "sv"[b % 2])
        for b in range(4):
            cast(1, b, "svss"[b])
        pack(t + 1, 0, ["h%d0%d" % (t + 1, b) for b in range(4)])
        pack(t + 1, 1, ["h%d1%d" % (t + 1, b) for b in range(4)] + ["hp%d" % (t + 1)])

    qx, sx = T["qx%d" % R], T["sx%d" % R]
    kx = ["qx%d0" % R, "qx%d1" % R]
    for h in range(2):
        a, z = O + 128 * h, O + 128 * h + 128
        run("t", ["qz", kx[h]], ["b%d" % h], lambda q: q.matmul_mx(
            bank(h, 0, 128), T.qz[:], T.sz[:], qx[:, a:z], sx[:, a:z], True, True))
    total = 16 * 7
    dma("y", "dout", total, kx, [], T.oc[:], qx[:, O:O + NC].bitcast(u8))
    run("v", ["b0"], ["ysb0"], lambda q: q.tensor_copy(T.ysb[:, 0:128], bank(0, 0, 128)))
    run("v", ["b1"], ["ysb1"], lambda q: q.tensor_copy(T.ysb[:, 128:NC], bank(1, 0, H)))
    dma("y", "dout", total, ["ysb0"], [], T.y[:, 0:128], T.ysb[:, 0:128])
    dma("y", "dout", total, ["ysb1"], [], T.y[:, 128:NC], T.ysb[:, 128:NC])
    for k in range(4):
        dma("s", "dout", total, kx, [], T.osc[4 * k:4 * k + 4, :], sx[32 * k:32 * k + 4, O:O + NC])
    wait("g", ("sent", sent))
    finish("g")
    wait("g", ("dlv", 16 * R))
    wait("g", ("dout", total))
